import numpy as np, ml_dtypes
CORES = [35,38,43,46]
N = 4
BF = ml_dtypes.bfloat16
W, NB, L, E, T, LIM, HOP, STR = 4096, 1024, 256, 512, 6, 3, 1, 16
def among(rng, m, *s):
    i = rng.integers(0, m.shape[1], (N, 8) + s)
    return m[np.arange(8).reshape((1, 8) + (1,) * len(s)), i]
def parts(rng):
    rate = np.array([0.3, 0.6, 0.8, 0.93])[(np.arange(W) >> 4) & 3]
    rec = np.where(rng.random((N, 8, 16, W)) < rate, 9, rng.integers(0, 4, (N, 8, 16, W)))
    ver = rng.integers(0, W // 64, (N, 8, 16, NB)) * 64 + rng.integers(0, 3, (N, 8, 1, NB)) * 16 + rng.integers(0, 16, (N, 8, 16, NB))
    hot = rng.integers(0, W // 64, (8, 24)) * 64 + 48 + rng.integers(0, 16, (8, 24)); hb = rng.integers(0, NB, (8, 48)); s = (N, 8, 16, NB)
    known = np.where(rng.random(s) < 0.5, among(rng, hot, 16, NB), rng.integers(0, W // 64, s) * 64 + 48 + rng.integers(0, 16, s))
    stub = W + np.where(rng.random(s) < 0.5, among(rng, hb, 16, NB), rng.integers(0, NB, s))
    edge = np.where(rng.random(s) < 0.4, known, stub)
    eff = rng.integers(0, 4, (N, 8, 16, E)) * rng.integers(0, 2, (N, 8, 16, E)); x = rng.integers(0, 4, (N, 8, 16, L))
    v = np.where(rng.random((N, 8, L)) < 0.5, among(rng, hot, L), rng.integers(0, W, (N, 8, L)))
    return rec, ver, edge, eff, x, v
def own(rng, a, g, dd, lo=0):
    rec, ver, edge, eff, x, v = a; i = np.arange(L)
    v[:, g] = i; edge[:, g, :, :L] = W + i
    ver[:, g, :, :L] = STR * i + (np.arange(16)[:, None] + rng.integers(0, STR)) % STR
    far = np.argsort(rng.random((N, 16 - lo, L, STR)), axis=1) < dd.reshape(N, 1, L, -1); xx = x[:, g][:, :, :, None]
    far = np.concatenate([np.zeros((N, lo, L, STR), bool), far], axis=1)
    rec[:, g] = np.where(far, (xx + rng.integers(1, 4, far.shape)) & 3, xx).reshape(N, 16, W)
def two(a, g):
    rec, ver, edge, eff, x, v = a
    x[:, g] = 0; x[1::2, g, :LIM + 1] = 1; eff[:, g] = 0
def pack(a):
    rec, ver, edge, eff, x, v = [np.ascontiguousarray(z) for z in a]
    return {"rec0": rec.reshape(N, 128, W).astype(BF), "ver0": ver.reshape(N, 128, NB).astype(np.int32), "edge0": edge.reshape(N, 128, NB).astype(np.int32),
            "eff": eff.reshape(N, 128, E).astype(BF), "x0": x.reshape(N, 128, L).astype(BF), "v0": v.astype(np.int32)}
def setup_inputs(rng):
    return pack(parts(rng))
def skew(rng, hi, *s):
    e = rng.choice(np.array([1.0, 3.0, 8.0]), (N, 8) + (1,) * len(s))
    return np.minimum(((hi + 1) * rng.random((N, 8) + s) ** e).astype(np.int64), hi)
def setup_inputs_spread(rng):
    ex = rng.choice(np.array([0.5, 1.0, 2.0, 4.0]), (1, 8, 16, 1))
    val = np.minimum((4 * rng.random((N, 8, 16, W)) ** ex).astype(np.int64), 3)
    rec = np.where(rng.random((N, 8, 16, W)) < 0.75 * rng.random((N, 8, 1, W)), 9, val)
    x = np.minimum((4 * rng.random((N, 8, 16, L)) ** ex).astype(np.int64), 3)
    edge = np.where(rng.random((N, 8, 16, NB)) < rng.choice(np.array([0.1, 0.4, 0.7]), (N, 8, 1, 1)), skew(rng, W - 1, 16, NB), W + skew(rng, NB - 1, 16, NB))
    return pack((rec, skew(rng, W - 1, 16, NB), edge, skew(rng, 3, 16, E), x, skew(rng, W - 1, L)))
def end(rng, lo, hi, *s):
    return np.where(rng.random((N, 8) + s) < 0.5, lo, hi)
def setup_inputs_ends(rng):
    rec = end(rng, 0, 9, 16, W); ver = end(rng, 0, W - 1, 16, NB); edge = end(rng, 0, W + NB - 1, 16, NB); eff = end(rng, 0, 3, 16, E); x = end(rng, 0, 3, 16, L); v = end(rng, 0, W - 1, L)
    for g in (1, 3, 5):
        ver[:, g] = np.where(rng.random((N, 16, NB)) < 0.3, rng.integers(0, W, (N, 16, NB)), ver[:, g])
        edge[:, g] = np.where(rng.random((N, 16, NB)) < 0.3, rng.integers(0, W + NB, (N, 16, NB)), edge[:, g])
        v[:, g] = np.where(rng.random((N, L)) < 0.3, rng.integers(0, W, (N, L)), v[:, g])
    for g in (0, 7):
        rec[:, g, :, 0] = 0; rec[:, g, :, W - 1] = 0
        m = rng.random((N, 1, L)); x[:, g] = np.where(m < 0.25, 3, np.where(m < 0.5, 0, x[:, g]))
        x[:, g, :, L - 1] = 3; v[:, g, L - 1] = W - 1
    edge[:, 7, :, NB - 1] = W + NB - 1; edge[:, 7, :, 0] = 0
    x[N - 1, 7] = 0; x[N - 1, 7, :, L - 1] = 3
    return pack((rec, ver, edge, eff, x, v))
def setup_inputs_corners(rng):
    a = parts(rng); rec, ver, edge, eff, x, v = a
    ver[:, 0] = 0; ver[:, 1] = W - 1; rec[:, 1, :, W - 1] = rng.integers(0, 4, (N, 16))
    v[:, 2] = rng.integers(0, NB, (N, L)); edge[:, 2] = np.arange(NB); rec[:, 2, :, ::2] = 9
    edge[:, 3] = W + rng.integers(0, NB, (N, 16, NB)); ver[:, 3] = ver[:, 3] // STR * STR + rng.integers(0, T, (N, 16, NB)) * rng.integers(0, 2, (N, 16, NB))
    v[:, 3] = STR * np.argsort(rng.random((N, L)), axis=1) + rng.integers(0, 2, (N, L)) * rng.integers(0, T, (N, L))
    dd = np.repeat(rng.choice(np.array([0, 1, LIM, LIM + 1, LIM + 2, 16]), (N, L, 1)), STR, axis=2)
    dd[:, 3::4] = 16; dd[:, 3::4, STR - 1] = 15
    own(rng, a, 4, dd)
    i = np.arange(3, L, 4); kk = np.arange(16)[:, None]; p = np.where(rng.random((N, 1, len(i))) < 0.5, 15, rng.integers(0, 16, (N, 1, len(i))))
    ver[:, 4, :, 3:L:4] = np.where(kk == p, STR * i + STR - 1, STR * i + kk % (STR - 1))
    edge[:, 5] = W + rng.choice(np.array([0, NB - 1]), (N, 16, NB)); rec[:, 5, :, 0] = 9
    two(a, 6); own(rng, a, 6, rng.integers(0, LIM + 1, (N, L)), LIM + 1)
    fit = np.where((rng.random((N, 16, L + 1)) < 0.3) & (kk > LIM), 9, x[:, 6, :, :1])
    rec[:, 6, :, ::STR] = fit[:, :, :L]; rec[:, 6, :, W - 1] = fit[:, :, L]
    edge[:, 6] = np.where(rng.random((N, 16, NB)) < 0.5, rng.choice(np.array([0, W - 1]), (N, 16, NB)), STR * rng.integers(0, L, (N, 16, NB)))
    edge[1::2, 6, :, L - 1] = W + L - 1
    rec[:, 7] = rng.integers(0, 4, (N, 16, W))
    return pack(a)
def setup_inputs_crowd(rng):
    a = parts(rng); rec, ver, edge, eff, x, v = a; full = np.full((N, L), 16); less = full.copy(); less[:, L - 1] = 0
    soft = rng.integers(1, LIM + 1, (N, L)); soft[1::2, L - 1] = 0
    rec[:, 2:7] = np.where(rng.random((N, 5, 16, W)) < 0.5, 9, rng.integers(0, 4, (N, 5, 16, W)))
    two(a, 0); two(a, 1); two(a, 7)
    own(rng, a, 0, soft, LIM + 1); own(rng, a, 1, less); own(rng, a, 7, full)
    edge[:, 2:4] = W + rng.integers(0, NB, (N, 2, 16, NB))
    x[:, 2] = x[:, 2, :, :1].copy(); v[:, 2] = v[:, 2, :1].copy()
    x[:, 3, :, :L - 1] = x[:, 3, :, :1].copy(); v[:, 3, :L - 1] = v[:, 3, :1].copy()
    v[:, 4] = v[:, 4, :1].copy(); edge[:, 4] = W + rng.integers(0, NB, (N, 1, 1))
    edge[:, 5] = W + NB - 1; v[:, 5] = np.argsort(rng.random((N, W)), axis=1)[:, :L]
    v[:, 6] = np.arange(L); edge[:, 6, :, :L] = W + np.arange(L); ver[:, 6] = W - 1; ver[:, 6, :, L - 1] = 5
    return pack(a)
def check_inputs(d):
    bad = []
    for k, lo, hi in (("rec0", 0, 9), ("ver0", 0, W - 1), ("edge0", 0, W + NB - 1), ("eff", 0, 3), ("x0", 0, 3), ("v0", 0, W - 1)):
        a = np.asarray(d[k]).astype(np.float64)
        if not (np.min(a) >= lo and np.max(a) <= hi and np.all(a == np.floor(a))): bad.append("range of " + k)
    a = np.asarray(d["rec0"]).astype(np.float64)
    if np.any((a > 3) & (a < 9)): bad.append("rec0 holds a number between 3 and 9")
    return bad
def reference(rec0, ver0, edge0, eff, x0, v0):
    R = np.asarray(rec0).astype(np.int32).reshape(N, 8, 16, W); V = np.asarray(ver0).astype(np.int32).reshape(N, 8, 16, NB)
    S = np.tile(np.asarray(edge0).astype(np.int32).reshape(N, 8, 16, NB), (1, 1, 1, W // NB)); ef = np.asarray(eff).astype(np.int32).reshape(N, 8, 16, E)
    x = np.asarray(x0).astype(np.int32).reshape(N, 8, 16, L); v = np.asarray(v0).astype(np.int32); A = np.zeros((N, 8), np.int32)
    lane = np.arange(L); low = lane[None, :] < lane[:, None]; wt = (2 * np.arange(16) + 1)[:, None]
    for t in range(T):
        for q in range(N):
            r = (q - HOP * t) % N
            for g in range(8):
                Rg, Vg, Sg, xx, vv = R[q, g], V[q, g], S[q, g], x[r, g], v[r, g].copy()
                j = np.sum(wt * xx, axis=0) & 15; w = Sg[j, vv]; rw = Rg[:, w & (W - 1)]
                known = (w < W) & ~np.any((rw != xx) & (rw != 9), axis=0)
                b = w & (NB - 1); ver = Vg[:, b]; old = Rg[:, ver]
                mis = np.sum((old != xx[:, None, :]) & (old != 9), axis=0); k = np.argmin(mis, axis=0)
                d = mis[k, lane]; c = ver[k, lane]
                want = ~known & (d > 0)
                clash = low & want[None, :] & ((b[:, None] == b[None, :]) | (c[:, None] == c[None, :]))
                may = want & ~np.any(clash, axis=1)
                gen = may & (d <= LIM + (A[q, g] & 1)); cl = may & ~gen
                rc = Rg[:, c]; new = np.where(rc == xx, rc, 9); n = STR * lane + t
                eat = np.all((new[:, None, :] == 9) | (old == new[:, None, :]), axis=0)
                vn = np.where(known, w, np.where(cl, n, c)); sc = W + (Sg[:, c] & (NB - 1))
                Rg[:, c[gen]] = new[:, gen]; Rg[:, n[cl]] = xx[:, cl]
                Vg[:, b[gen]] = np.where(eat, c[None, :], ver)[:, gen]; Vg[(lane[cl] + t) & 15, b[cl]] = n[cl]
                Sg[:, n[cl]] = sc[:, cl]
                first = ~np.any(low & (vv[:, None] == vv[None, :]), axis=1)
                Sg[j[first], vv[first]] = vn[first]
                x[r, g] = (xx + ef[q, g][:, vn & (E - 1)]) & 3; v[r, g] = vn; A[q, g] = np.count_nonzero(cl)
    return {"yr": R.reshape(N, 128, W).astype(np.float32).astype(BF), "yl": V.reshape(N, 128, NB).astype(np.float32), "ys": np.sum(S, axis=2).astype(np.float32),
            "yx": x.reshape(N, 128, L).astype(np.float32).astype(BF), "yv": v.astype(np.float32)}

@@ -1,0 +1,799 @@
+import math
+from concourse.bass import DstId, RemoteDMATransfer
+from concourse.mybir import dt, AluOpType, AxisListType, ActivationFunctionType
+
+A = AluOpType
+F = ActivationFunctionType
+NS = 6
+BF, F32, I32, U16 = "bfloat16", "float32", "int32", "uint16"
+
+SCRATCH = {
+    "R": ("sbuf", [128, 5376], BF), "VL": ("sbuf", [128, 1280], F32), "SU": ("sbuf", [128, 4352], F32),
+    "EF": ("sbuf", [128, 4096], BF), "veri": ("sbuf", [128, 1024], I32), "edgi": ("sbuf", [128, 1024], I32),
+    "v8i": ("sbuf", [128, 256], I32), "v8f": ("sbuf", [128, 256], F32),
+    "old": ("sbuf", [128, 4352], BF), "eq": ("sbuf", [128, 4352], BF),
+    "Zb": ("sbuf", [128, 4096], BF), "Zc": ("sbuf", [128, 4096], BF), "Zv": ("sbuf", [128, 4096], BF),
+    "wx0": ("sbuf", [128, 512], BF), "wx1": ("sbuf", [128, 512], BF),
+    "jm0": ("sbuf", [128, 256], BF), "jm1": ("sbuf", [128, 256], BF),
+    "nj0": ("sbuf", [128, 256], BF), "nj1": ("sbuf", [128, 256], BF),
+    "Q": ("sbuf", [128, 256], BF), "Qb": ("sbuf", [128, 256], BF), "Qc": ("sbuf", [128, 256], BF),
+    "G": ("sbuf", [128, 256], F32), "sc1": ("sbuf", [128, 256], F32), "sc2": ("sbuf", [128, 256], F32),
+    "VD": ("sbuf", [128, 512], F32), "VX": ("sbuf", [128, 512], F32), "VT": ("sbuf", [128, 256], U16),
+    "verK": ("sbuf", [128, 256], F32), "xc": ("sbuf", [128, 256], BF),
+    "bR": ("sbuf", [128, 256], U16), "cR": ("sbuf", [128, 256], U16),
+    "sf": ("sbuf", [128, 512], F32), "si": ("sbuf", [128, 128], I32), "su": ("sbuf", [128, 256], U16),
+    "sb": ("sbuf", [128, 64], BF), "TTs": ("sbuf", [128, 128], BF),
+    "xu": ("sbuf", [128, 256], F32), "xw": ("sbuf", [128, 128], BF), "xl": ("sbuf", [128, 128], BF),
+    "xm": ("sbuf", [128, 128], BF), "xf": ("sbuf", [128, 128], BF), "wsel": ("sbuf", [128, 128], BF),
+    "efu": ("sbuf", [128, 256], BF), "sgA": ("sbuf", [128, 256], BF), "sgB": ("sbuf", [128, 256], BF),
+    "xAB": ("sbuf", [128, 512], F32), "wv": ("sbuf", [128, 512], F32), "vnR": ("sbuf", [128, 256], F32),
+    "wc": ("sbuf", [128, 256], F32), "ws": ("sbuf", [128, 512], F32), "u2": ("sbuf", [128, 256], F32),
+    "tp": ("sbuf", [128, 256], F32), "rc": ("sbuf", [128, 256], BF), "eqc": ("sbuf", [128, 256], BF),
+    "ga": ("sbuf", [128, 256], BF), "gn": ("sbuf", [128, 256], BF),
+    "Xi": ("sbuf", [128, 512], I32), "Xa": ("sbuf", [128, 512], I32), "ok": ("sbuf", [128, 512], BF),
+    "wm": ("sbuf", [128, 512], BF), "mm": ("sbuf", [128, 256], BF), "tv": ("sbuf", [128, 256], F32),
+    "xh": ("sbuf", [128, 256], BF), "lx": ("sbuf", [128, 256], BF), "lv": ("sbuf", [128, 256], F32),
+    "y1": ("sbuf", [128, 256], F32), "y2": ("sbuf", [128, 256], F32),
+    "vR0": ("sbuf", [128, 256], U16),
+    "io_f": ("sbuf", [128, 1024], F32), "io_b": ("sbuf", [128, 1024], BF), "io_i": ("sbuf", [128, 8], I32),
+    "cf": ("sbuf", [128, 256], F32), "cI": ("sbuf", [128, 640], BF), "cI32": ("sbuf", [128, 512], F32),
+    "cW": ("sbuf", [128, 512], BF), "L8": ("sbuf", [128, 2048], BF), "DG": ("sbuf", [128, 272], BF),
+    "M2": ("sbuf", [128, 768], BF), "CK": ("sbuf", [128, 528], BF), "ONE": ("sbuf", [128, 256], BF),
+    "CS": ("sbuf", [128, 256], F32), "CT": ("sbuf", [128, 256], F32), "MS": ("sbuf", [128, 128], F32),
+    "cu": ("sbuf", [128, 64], U16), "n16": ("sbuf", [128, 256], F32), "SR": ("sbuf", [128, 256], BF),
+    "cb": ("sbuf", [128, 64], BF),
+}
+for _t in range(1, NS):
+    SCRATCH["wx%d" % _t] = ("sbuf", [128, 512], BF)
+    SCRATCH["l2_%d" % _t] = ("sbuf", [128, 272], U16)
+    SCRATCH["s1_%d" % _t] = ("sbuf", [128, 256], BF)
+    SCRATCH["s2_%d" % _t] = ("sbuf", [128, 272], U16)
+for _b in range(8):
+    SCRATCH["ps%d" % _b] = ("psum", [128, 512], F32)
+SCRATCH.update({"fb": ("sbuf", [128, 256], BF), "ja": ("sbuf", [128, 256], BF), "ea": ("sbuf", [128, 256], BF),
+                "tw": ("sbuf", [128, 256], F32), "xg": ("sbuf", [128, 256], BF), "xq": ("sbuf", [128, 256], BF)})
+SCRATCH["Ec"] = ("sbuf", [128, 512], F32)
+CFG = dict(EQC="V", TV="S", XU="U", XW="S", XL="S", XM="S", XF="S", VD="VS", VR="S", ZO=1, IT=1, TP="V", JS=0,
+           SEEDS=[i * 7919 + 3 for i in range(500)], NOISE=600, FRAC=0.1)
+SCRATCH["xJ"] = ("sbuf", [128, 1024], BF)
+SCRATCH["QJ"] = ("sbuf", [128, 512], BF)
+SCRATCH["sv"] = ("sbuf", [128, 256], F32)
+for _t in range(NS):
+    SCRATCH["wx%d" % _t] = ("sbuf", [128, 768], BF)
+for _t in range(1, NS):
+    SCRATCH["s1_%d" % _t] = ("sbuf", [128, 512], BF)
+ORDER = {}
+
+NDMA = 24
+SEMAPHORES = (["sV", "sS", "sP", "sG", "sent"] + ["d%d" % i for i in range(NDMA)]
+              + ["a1_%d" % t for t in range(1, NS + 1)] + ["a2_%d" % t for t in range(1, NS + 1)])
+
+CV, CP, GA, SC = 1.0, 0.55, 1.55, 3.8
+LN256 = math.log(256.0)
+
+
+def build(g, core, T, topo, rank):
+    N = len(T.cores)
+    nxt, prv = T.cores[(rank + 1) % N], T.cores[(rank - 1) % N]
+    ops = []
+    nd = [0]
+    ps = [T["ps%d" % b] for b in range(8)]
+
+    def add(e, f, r, w, c, banks=(), **kw):
+        o = dict(e=e, f=f, r=list(r) + ([] if e == "P" else ["B%d" % b for b in banks]), w=list(w), c=c, b=tuple(banks),
+                 i=len(ops))
+        o.update(kw)
+        ops.append(o)
+
+    def V(f, r, w, n, banks=()):
+        add("V", f, r, w, max(64, n) * CV, banks)
+
+    def S(f, r, w, n, banks=()):
+        add("S", f, r, w, max(64, n) * CV + 30, banks)
+
+    def P(mms, r, w, banks, grp=False, given=False):
+        def f():
+            for n, m in enumerate(mms):
+                stop = m[4] if grp or given else (n + 1 == len(mms) or mms[n + 1][3])
+                ins = g.tensor.matmul(m[0], m[1], m[2], m[3], stop)
+            return ins
+        bn = ["B%d" % b for b in banks]
+        add("P", f, list(r) + ([] if grp else bn), list(w) + (bn if grp else []),
+            sum(max(m[5], 32) for m in mms) * CP + 40, banks)
+
+    def spread(e, out, win, lst, scale, r, w, n):
+        if e == "S":
+            act(out, win.indirect(lst), F.Identity, r, w, n * GA, scale=scale)
+        else:
+            ts(out, win.indirect(lst), scale, A.mult, r, w, n * GA)
+
+    def ts(out, in0, s1, op0, r, w, n, s2=None, op1=None, banks=()):
+        if op1 is None:
+            V(lambda: g.vector.tensor_scalar(out, in0, s1, None, op0), r, w, n, banks)
+        else:
+            V(lambda: g.vector.tensor_scalar(out, in0, s1, s2, op0, op1), r, w, n, banks)
+
+    def tt(out, a, b, op, r, w, n, banks=()):
+        V(lambda: g.vector.tensor_tensor(out, a, b, op), r, w, n, banks)
+
+    def cp(out, a, r, w, n, banks=()):
+        V(lambda: g.vector.tensor_copy(out, a), r, w, n, banks)
+
+    def act(out, a, func, r, w, n, bias=0.0, scale=1.0, banks=()):
+        S(lambda: g.scalar.activation(out, a, func, bias=bias, scale=scale), r, w, n, banks)
+
+    def iota(out, pat, w, n, cm=0, flt=True, base=0):
+        if flt:
+            add("G", lambda: g.iota(out, pat, base, cm, allow_small_or_imprecise_dtypes=True), [], w, 130 + 2 * n * CV)
+        else:
+            add("G", lambda: g.iota(out, pat, 0, cm), [], w, 130 + 2 * n * CV)
+
+    def dma(q, out, in_, r, w, nbytes):
+        sem = "d%d" % nd[0]
+        nd[0] += 1
+        eng = g.sync if q == "Y" else g.scalar
+        add(q, lambda: eng.dma_start(out, in_), r, w, 60 + nbytes / 200.0, lat=1800, sem=sem)
+
+    def send(dst, out, in_, sem, r, w):
+        rid, pid, _ = topo.addr(dst)
+        m = topo.mask(core, dst)
+        add("G", lambda: g.remote_dma(out, in_, T.sem[sem], T.sem.sent, pid, rid, m), r, w, 300,
+            send=len(topo.engines(core, dst)))
+
+    def recv(src, sem, r, w):
+        add("X", None, r, w, 2500, sem=sem, val=len(topo.engines(src, core)))
+
+    dma("Y", T.v8i[0:8, :], T.v0[:], [], ["v8i"], 8192)
+    dma("Y", T.wx0[:, 256:512], T.x0[:], [], ["xb0"], 65536)
+    dma("Y", T.edgi[:], T.edge0[:], [], ["edgi"], 524288)
+    dma("Y", T.veri[:], T.ver0[:], [], ["veri"], 524288)
+    dma("Y", T.R[:, 0:4096], T.rec0[:], [], ["R"], 1048576)
+    dma("Y", T.EF[:, 0:512], T.eff[:], [], ["EF0"], 131072)
+
+    io, ib, cf = T.io_f, T.io_b, T.cf
+    col = lambda j: cf[:, j:j + 1]
+    partf, pf, gf, wt, wl, wh, offp, bW_, bT_, bV_, x2s, pms, nwl, nwh, p4, tmpc = [col(j) for j in range(16)]
+    iota(T.io_i[:, 0:1], [[0, 1]], ["ii0"], 1, cm=1, flt=False)
+    F128, CG, DI, CH, HI, C16, H16 = (io[:, 0:128], io[:, 128:256], io[:, 256:528], io[:, 528:656], io[:, 656:784],
+                                      io[:, 784:912], io[:, 912:928])
+    iota(F128, [[1, 128]], ["F128"], 128)
+    iota(CG, [[1, 8], [0, 16]], ["CG"], 128)
+    iota(DI, [[0, 17], [1, 16]], ["DI"], 272)
+    iota(CH, [[0, 16], [1, 8]], ["CH"], 128)
+    iota(io[:, 656:672], [[1, 8], [16, 2]], ["HI"], 16)
+    iota(C16, [[1, 16], [0, 8]], ["C16"], 128)
+    iota(H16, [[1, 2], [0, 8]], ["H16"], 16)
+    iota(ib[:], [[-16, 8], [16, 8], [1, 16]], ["ib"], 1024)
+    ii = T.io_i
+    ts(ii[:, 1:2], ii[:, 0:1], 15, A.bitwise_and, ["ii0"], ["ii1"], 1)
+    ts(ii[:, 2:3], ii[:, 0:1], 4, A.arith_shift_right, ["ii0"], ["ii2"], 1)
+    ts(ii[:, 3:4], ii[:, 0:1], 17, A.bitwise_and, ["ii0"], ["ii3"], 1)
+    ts(ii[:, 4:5], ii[:, 0:1], 7, A.bitwise_and, ["ii0"], ["ii4"], 1)
+    cp(cf[:, 0:3], ii[:, 0:3], ["ii0", "ii1", "ii2"], ["pg"], 3)
+    c17, p7, ca, cb_, cm_, cn, co = [col(j) for j in range(128, 135)]
+    cp(cf[:, 128:130], ii[:, 3:5], ["ii3", "ii4"], ["c17"], 2)
+    ts(ca, c17, 0.0, A.is_gt, ["c17"], ["ca"], 1)
+    ts(tmpc, c17, 17.0, A.is_lt, ["c17", "ca"], ["tmpc"], 1, ca, A.mult)
+    ts(cb_, pf, 0.0, A.is_equal, ["pg"], ["cb_"], 1, 256.0, A.mult)
+    ts(cb_, cb_, 240.0, A.add, ["cb_", "tmpc"], ["cb_"], 1, tmpc, A.mult)
+    ts(cm_, p7, gf, A.is_equal, ["c17", "pg"], ["cm_"], 1)
+    ts(wt, pf, 2.0, A.mult, ["pg"], ["wt"], 1, 1.0, A.add)
+    ts(offp, pf, 0.0, A.is_equal, ["pg"], ["offp0"], 1, -16384.0, A.mult)
+    ts(offp, offp, 8192.0, A.add, ["offp0"], ["offp"], 1)
+    ts(bW_, partf, -0.55, A.mult, ["pg"], ["bW_"], 1, 70.0, A.add)
+    ts(bT_, partf, -0.55, A.mult, ["pg"], ["bT_"], 1, 70.0 + math.log(2.55), A.add)
+    ts(bV_, pf, -0.55, A.mult, ["pg"], ["bV_"], 1, 70.0, A.add)
+    ts(x2s, pf, 8.0, A.is_ge, ["pg"], ["x2s"], 1, 8.0, A.mult)
+    ts(pms, pf, 16.0, A.mult, ["pg", "cb_"], ["pms"], 1, cb_, A.add)
+    cb = T.cb
+    act(cb[:, 0:1], pf, F.Exp, ["pg"], ["p4b"], 1, scale=math.log(4.0))
+    cp(p4, cb[:, 0:1], ["p4b"], ["p4"], 1)
+    ts(wl, pf, 8.0, A.is_lt, ["pg", "p4"], ["wl"], 1, p4, A.mult)
+    ts(wh, x2s, p4, A.mult, ["x2s", "p4"], ["wh"], 1, 2.0 ** -19, A.mult)
+    ts(cf[:, 12:14], cf[:, 4:6], -1.0, A.mult, ["wl", "wh"], ["nw"], 2)
+    cI = T.cI
+    Ib, In, I16, Im2, I8k = [cI[:, 128 * j:128 * j + 128] for j in range(5)]
+    for ap, nm, val in ((Ib, "Ib", 1.0), (In, "In", -1.0), (I16, "I16", 16.0), (Im2, "Im2", -2.0), (I8k, "I8k", 8192.0)):
+        ts(ap, F128, partf, A.is_equal, ["F128", "pg"], [nm], 128, val, A.mult)
+    If, Ifn, BO, SB = [T.cI32[:, 128 * j:128 * j + 128] for j in range(4)]
+    ts(If, F128, partf, A.is_equal, ["F128", "pg"], ["If"], 128)
+    ts(Ifn, F128, partf, A.is_equal, ["F128", "pg"], ["Ifn"], 128, -1.0, A.mult)
+    ts(BO, CG, gf, A.is_equal, ["CG", "pg"], ["BO"], 128)
+    ts(SB, CG, partf, A.is_equal, ["CG", "pg"], ["SB"], 128)
+    cW = T.cW
+    WT, WEC, WKE, WK17, S16 = cW[:, 0:128], cW[:, 128:384], cW[:, 384:408], cW[:, 408:416], cW[:, 416:432]
+    ts(WT, CG, gf, A.is_equal, ["CG", "pg", "wt"], ["WT"], 128, wt, A.mult)
+    ts(cW[:, 128:256], CG, gf, A.is_equal, ["CG", "pg", "wl"], ["WEC0"], 128, wl, A.mult)
+    ts(cW[:, 256:384], CG, gf, A.is_equal, ["CG", "pg", "wh"], ["WEC1"], 128, wh, A.mult)
+    F8 = io[:, 0:8]
+    ts(cW[:, 384:392], F8, gf, A.is_equal, ["F128", "pg"], ["WKE0"], 8, -65536.0, A.mult)
+    ts(cW[:, 392:400], F8, gf, A.is_equal, ["F128", "pg", "nw"], ["WKE1"], 8, nwl, A.mult)
+    ts(cW[:, 400:408], F8, gf, A.is_equal, ["F128", "pg", "nw"], ["WKE2"], 8, nwh, A.mult)
+    ts(WK17, F8, gf, A.is_equal, ["F128", "pg"], ["WK17"], 8, -2.0 ** 21, A.mult)
+    SEL8, thT, iWf, DW, thrA = cf[:, 16:24], cf[:, 32:48], cf[:, 48:64], cf[:, 64:112], cf[:, 112:128]
+    ts(SEL8, F8, gf, A.is_equal, ["F128", "pg"], ["SEL8"], 8)
+    act(thT, H16, F.Exp, ["H16", "bT_"], ["thT"], 16, bias=bT_, scale=-0.55 * 128)
+    ts(iWf, io[:, 0:16], 16.0, A.mult, ["F128", "pg"], ["iWf"], 16, pf, A.add)
+    iWb = cb[:, 16:32]
+    cp(iWb, iWf, ["iWf"], ["iWb"], 16)
+    for j, base in enumerate((5120.0, 1024.0, 4096.0)):
+        ts(cf[:, 64 + 16 * j:80 + 16 * j], iWf, base, A.add, ["iWf"], ["DW%d" % j], 16)
+    V(lambda: g.vector.memset(thrA, 4.0 * 65536), [], ["thrA"], 16)
+    L8 = T.L8[:, 0:1024]
+    ts(L8, ib[:], pf, A.is_equal, ["ib", "pg"], ["L8"], 512)
+    In8 = T.L8[:, 1024:1152]
+    ts(In8, F128, partf, A.is_equal, ["F128", "pg"], ["In8"], 128, -8192.0, A.mult)
+    DG = T.DG
+    ts(DG[:], DI, pf, A.is_equal, ["DI", "pg"], ["DG"], 272)
+    M2 = T.M2
+    M2o, M2w, M2c, M2n, WSV, M2t = [M2[:, 128 * j:128 * j + 128] for j in range(6)]
+    ts(M2o, CH, gf, A.is_equal, ["CH", "pg"], ["M2o"], 128)
+    act(M2t, C16, F.Exp, ["C16", "bV_"], ["M2t"], 128, bias=bV_, scale=-0.55 * 16)
+    tt(WSV, M2t, M2o, A.mult, ["M2t", "M2o"], ["WSV"], 256)
+    CK, ONE = T.CK, T.ONE
+    V(lambda: g.vector.memset(ONE[:], 1.0), [], ["ONE"], 128)
+    V(lambda: g.vector.memset(CK[0:64, :], 0.0), [], ["CK"], 264)
+    for (lo, hi, v0, v1) in ((0, 128, 2.0 ** 20, None), (128, 384, 21760.0, 85.0), (384, 400, 2.0 ** 25, -4096.0),
+                             (400, 528, 3072.0, None)):
+        V(lambda lo=lo, hi=hi, v0=v0: g.vector.memset(CK[0:1, lo:hi], v0), ["CK"], ["CK"], 64)
+        if v1 is not None:
+            V(lambda lo=lo, hi=hi, v1=v1: g.vector.memset(CK[32:33, lo:hi], v1), ["CK"], ["CK"], 64)
+    ts(CK[32:33, 0:128], io[32:33, 256:384], 4096.0, A.mult, ["DI", "CK"], ["CK"], 128)
+    ts(CK[32:33, 400:528], io[32:33, 256:384], -1.0, A.mult, ["DI", "CK"], ["CK"], 128)
+    ts(T.CS[:], DG[:, 0:256], -8192.0, A.mult, ["DG"], ["CS0"], 256)
+    act(T.CT[:], DG[:, 1:257], F.Identity, ["DG"], ["CT"], 256, scale=16384.0)
+    tt(T.CS[:], T.CS[:], T.CT[:], A.add, ["CS0", "CT"], ["CS"], 512)
+    ts(T.MS[:], io[:, 256:384], 0.0, A.is_equal, ["DI"], ["MS"], 128, 2.0 ** 23, A.mult)
+    cu = T.cu
+    X1, X2, PM, X3 = cu[:, 0:16], cu[:, 16:24], cu[:, 32:48], cu[:, 48:64]
+    cp(X1, io[:, 0:16], ["F128"], ["X1"], 16)
+    for lst, nm, src, srcn, zc, tc in ((X2, "X2", F8, "F128", 16.0, cn), (X3, "X3", io[:, 656:672], "HI", 32.0, co)):
+        ts(tc, x2s, -zc, A.add, ["x2s", "cm_"], [nm + "c"], 1, cm_, A.mult)
+        ts(tc, tc, zc, A.add, [nm + "c"], [nm + "c"], 1)
+        ts(lst, src, cm_, A.mult, [srcn, "cm_", nm + "c"], [nm], 16, tc, A.add)
+    V(lambda: g.vector.memset(T.fb[:], 0.0), [], ["clT", "nmT", "ngT", "nfT", "thrW0", "thrW1", "hl"], 128)
+    ts(PM, io[:, 0:16], pms, A.add, ["F128", "pms"], ["PM"], 16)
+    for h in range(2):
+        ts(T.SR[0:32, 128 * h:128 * h + 128], io[0:32, 128:256], float(8 * h), A.add, ["CG", "pg"], ["SR%d" % h], 128,
+           cf[0:32, 1:2], A.is_equal)
+    V(lambda: g.vector.memset(T.R[:, 4096:5120], 5.0), [], ["R5"], 512)
+    cp(T.SU[:, 0:1024], T.edgi[:], ["edgi"], ["SU0"], 1024)
+    act(T.SU[:, 1024:2048], T.SU[:, 0:1024], F.Identity, ["SU0"], ["SU1"], 1024)
+    act(T.SU[:, 2048:3072], T.SU[:, 0:1024], F.Identity, ["SU0"], ["SU2"], 1024)
+    act(T.SU[:, 3072:4096], T.SU[:, 0:1024], F.Identity, ["SU0", "SU1", "SU2"], ["SU"], 1024)
+    cp(T.VL[:, 0:1024], T.veri[:], ["veri"], ["VL"], 1024)
+    act(T.EF[:, 512:1024], T.EF[:, 0:512], F.Identity, ["EF0"], ["EF1"], 512)
+    cp(T.EF[:, 1024:2048], T.EF[:, 0:1024], ["EF0", "EF1"], ["EF2"], 512)
+    act(T.EF[:, 2048:3072], T.EF[:, 0:1024], F.Identity, ["EF0", "EF1"], ["EF3"], 1024)
+    cp(T.EF[:, 3072:4096], T.EF[:, 0:1024], ["EF0", "EF1", "EF2", "EF3"], ["EF"], 512)
+
+    sf, si, su, sb = T.sf, T.si, T.su, T.sb
+    f16 = lambda j: sf[:, 16 * j:16 * j + 16]
+    (bWf, vWf, uT, wantT, hardT, uWf, nb, thrW, thrM, thrC, clT, nmT, nfT, clW, dnW, t1, vnW, nWf, lf, _a, lfF) = \
+        [f16(j) for j in range(21)]
+    lfGM = sf[:, 288:320]
+    A256, parc = sf[:, 352:353], sf[:, 353:354]
+    wWi, bWi, keyT, hiT, loT, vWi = [si[:, 16 * j:16 * j + 16] for j in range(6)]
+    bl, wl_, bl1, ul, sel, lG, lM, lF, vl0, vm0 = (su[:, 0:32], su[:, 32:48], su[:, 48:64], su[:, 64:80], su[:, 80:96],
+                                                   su[:, 96:112], su[:, 112:128], su[:, 128:144], su[:, 144:160],
+                                                   su[:, 160:176])
+    fb = T.fb
+    clT, ngT, nmT, nfT, thrW, hl = fb[:, 0:16], fb[:, 32:48], fb[:, 48:64], fb[:, 80:96], fb[:, 112:128], fb[:, 144:176]
+    Q2, par2 = sb[:, 0:16], f16(19)
+
+    cp(T.v8f[0:8, :], T.v8i[0:8, :], ["v8i"], ["v8f"], 256)
+    P([(ps[1][:, 0:256], T.cI32[0:8, 384:512], T.v8f[0:8, :], True, True, 1024)], ["SB", "v8f"], ["wR"], [1])
+    V(lambda: g.vector.tensor_tensor_scan(T.sc1[:], ps[1][:, 0:256], T.CS[:], 8192.0, A.min, A.add),
+      ["wR", "CS"], ["sc1"], 256, [1])
+    cp(T.vR0[:], ps[1][:, 0:256], ["wR"], ["vR_0"], 256, [1])
+    ts(vWi, T.sc1[:, 15:256:16], offp, A.add, ["sc1", "offp"], ["vWi"], 16)
+    cp(vl0, vWi, ["vWi"], ["vW_0"], 16)
+    ts(vWi, vWi, 1023, A.bitwise_and, ["vWi"], ["vWi"], 16)
+    cp(vm0, vWi, ["vWi"], ["vm0"], 16)
+
+    def zstart(c):
+        q = c % 8
+        return 128 * (c // 8) + (0 if q < 4 else 64 if q < 6 else 96)
+
+    def zcalls(Z, nm, keyR, keyRn, keyW, keyWn, more=()):
+        for c in range(16):
+            s = zstart(c)
+            ts(Z[:, 256 * c + s:256 * c + 256], keyR[:, s:256], keyW[:, c:c + 1], A.is_equal, [keyRn, keyWn] + list(more),
+               ["%s%d" % (nm, c)], (256 - s) // 2)
+
+    def zsum(Z, nm, wsel, wn, bk, o, on, cs, first, grp=False):
+        mms = []
+        if first:
+            mms.append((ps[bk][:, o:o + 16], T.ONE[32:64, 0:128], T.cb[32:64, 32:48], True, False, 64))
+        for c in cs:
+            s = zstart(c)
+            for h in range(c // 8, 2):
+                lo = max(s, 128 * h)
+                mms.append((ps[bk][lo - 128 * h:128, o + 8 * h:o + 8 * h + 8],
+                            Z[:, 256 * c + lo:256 * c + 128 * h + 128], wsel[:, 8 * c:8 * c + 8], False, c == 0 and h == 1, 64))
+        P(mms, ["%s%d" % (nm, c) for c in cs] + [wn, "ONE", "zer"], [on], [bk], grp, True)
+
+    V(lambda: g.vector.memset(T.cb[:, 32:48], 0.0), [], ["zer"], 16)
+
+    def toW(xp, bk, o, n=16, st=16, at=0, first=False):
+        return [(ps[bk][:, o:o + n], T.L8[:, 128 * k:128 * k + 128], xp[:, st * k + at:st * k + at + n], first and k == 0,
+                 False, 64) for k in range(8)]
+
+    for t in range(NS):
+        par = t % 2
+        wx = T["wx%d" % t]
+        xb, xn = wx[:, 256:512], "xb%d" % t
+        jm, nj, jn, njn = T["jm%d" % par], T["nj%d" % par], "jm%d" % par, "nj%d" % par
+        if t == 0:
+            vW, vR, vWn, vRn = vl0, T.vR0, "vW_0", "vR_0"
+        else:
+            vW, vR, vWn, vRn = T["l2_%d" % t][:, 256:272], T["l2_%d" % t], "vR_%d" % t, "vR_%d" % t
+        def jmask(out, on, x, xname, Q, Qn):
+            P([(ps[0][:, 0:256], CK[0:64, 400:528], ONE[0:64, :], True, False, 256),
+               (ps[0][:, 0:256], WT, x, False, True, 256)], ["CK", "ONE", "WT", xname], ["pY"], [0])
+            act(Q, ps[0][:, 0:256], F.Identity, ["pY"], [Qn], 256, banks=[0])
+            tt(out, ps[0][:, 0:256], Q, A.is_equal, ["pY", Qn], [on], 256, [0])
+        if CFG["JS"] and t:
+            jm, jn = wx[:, 512:768], xn
+        else:
+            jm = jm[:]
+            jmask(jm, jn, xb, xn, T.Q[:], "Q")
+        if CFG["TP"] == "V":
+            act(nj[:], jm, F.Identity, [jn], [njn], 256, bias=1.0, scale=-1.0)
+        if t == 0:
+            tt(T.G[:], T.edgi[:].indirect(vm0), jm, A.mult, ["edgi", "vm0", jn], ["G"], 256 * GA)
+        else:
+            tt(T.G[:], T.SU[:, 0:4096].indirect(vW), jm, A.mult, ["SU", vWn, jn], ["G"], 256 * GA)
+        P([(ps[1][:, 0:256], BO, T.G[:], True, True, 1024)], ["BO", "G"], ["wR"], [1])
+        V(lambda: g.vector.tensor_tensor_scan(T.sc1[:], ps[1][:, 0:256], T.CS[:], 8192.0, A.min, A.add),
+          ["wR", "CS"], ["sc1"], 256, [1])
+        ts(wWi, T.sc1[:, 15:256:16], offp, A.add, ["sc1", "offp"], ["wWi"], 16)
+        ts(wl_, T.sc1[:, 15:256:16], offp, A.add, ["sc1", "offp"], ["wl_"], 16)
+        ts(bWi, wWi, 1023, A.bitwise_and, ["wWi"], ["bWi"], 16)
+        cp(su[:, 0:16], bWi, ["bWi"], ["bla"], 16)
+        cp(su[:, 16:18], si[:, 16:18], ["bWi"], ["blb"], 16)
+        cp(bWf, bWi, ["bWi"], ["bWf"], 16)
+        VLw = T.VL[:, 0:1024]
+        verK, vk = T.VD[:, 0:256], ["VD0", "VD1"]
+        if t == 0:
+            cp(T.VD[:, 0:272], T.veri[:].indirect(su[:, 0:17]), ["veri", "bla", "blb"], vk, 272 * GA)
+        elif CFG["VD"] == "VS":
+            cp(T.VD[:, 0:128], VLw.indirect(su[:, 0:8]), ["VL", "bla"], ["VD0"], 128 * GA)
+            act(T.VD[:, 128:272], VLw.indirect(su[:, 8:17]), F.Identity, ["VL", "bla", "blb"], ["VD1"], 144 * GA)
+        elif CFG["VD"] == "S":
+            act(T.VD[:, 0:272], VLw.indirect(su[:, 0:17]), F.Identity, ["VL", "bla", "blb"], vk, 272 * GA)
+        else:
+            cp(T.VD[:, 0:272], VLw.indirect(su[:, 0:17]), ["VL", "bla", "blb"], vk, 272 * GA)
+        for h in range(2):
+            V(lambda h=h: g.vector.transpose(T.VX[:, 256 * h:256 * h + 256], T.VD[:, 16 * h:16 * h + 256]),
+              vk, ["VX%d" % h], 256)
+        for q in range(4):
+            cp(T.VT[:, 64 * q:64 * q + 64], T.VX[:].indirect(cu[:, 32 + 4 * q:36 + 4 * q]), ["VX0", "VX1", "PM"],
+               ["VT%d" % q], 64 * GA)
+        act(T.xc[:], xb, F.Exp, [xn], ["xc"], 256, bias=-9 * LN256, scale=LN256)
+        P([(ps[2][:, 0:256], Ib, T.xc[:], True, True, 256), (ps[2][:, 256:512], Ib, T.xc[:], True, True, 256)],
+          ["Ib", "xc"], ["pX"], [2])
+        act(T.Qb[:], ps[1][:, 0:256], F.Identity, ["wR"], ["Qb"], 256, bias=196096.5, banks=[1])
+        P([(ps[1][:, 256:512], BO, T.G[:], True, True, 1024), (ps[1][:, 256:512], In, T.Qb[:], False, True, 256)],
+          ["In", "Qb", "BO", "G"], ["pb"], [1])
+        ts(T.bR[:], ps[1][:, 256:512], 196608.0, A.add, ["pb"], ["bR"], 256, banks=[1])
+        cp(vWf, vW, [vWn], ["vWf"], 16)
+        zcalls(T.Zv, "Zv", vR, vRn, vWf, "vWf")
+        zcalls(T.Zb, "Zb", T.bR, "bR", bWf, "bWf", ["Zv15"] if CFG["ZO"] else [])
+        zsum(T.Zv, "Zv", WSV, "WSV", 7, 64, "Sv", range(15, -1, -1), True)
+        tt(nfT, ps[7][:, 64:80], thT, A.is_ge, ["Sv", "thT"], ["nfT"], 16, [7])
+        spread(CFG["XF"], T.xf[:], fb[:, 80:112], X2, 8192.0, ["nfT", "X2"], ["xf"], 128)
+        P([(ps[7][:, 80:96], If, vWf, True, False, 256)] + toW(T.xf, 7, 80), ["If", "vWf", "xf", "L8"], ["pF"], [7])
+        tt(lfF, ps[7][:, 80:96], cf[:, 96:112], A.min, ["pF", "DW2"], ["lfF"], 16, [7])
+        cp(lF, lfF, ["lfF"], ["lF"], 16)
+        P([(ps[0][:, 256:512], Ib, T.EF[:, t:4096:16], True, False, 256), (ps[0][:, 256:512], Ib, xb, False, True, 256)],
+          ["Ib", "EF", xn], ["pB"], [0])
+        act(T.sgB[:], ps[0][:, 256:512], F.Sign, ["pB"], ["sgB"], 256, bias=-3.5, banks=[0])
+        P([(ps[0][:, 256:512], Ib, T.EF[:, t:4096:16], True, False, 256), (ps[0][:, 256:512], Ib, xb, False, True, 256),
+           (ps[0][:, 256:512], Im2, T.sgB[:], False, True, 256)], ["Im2", "sgB", "Ib", "EF", xn], ["pB"], [0])
+        act(T.xJ[:, 256:512], ps[0][:, 256:512], F.Identity, ["pB"], ["xB"], 256, bias=-2.0, banks=[0])
+        if CFG["JS"] and t + 1 < NS:
+            jmask(T.xJ[:, 768:1024], "jB", T.xJ[:, 256:512], "xB", T.QJ[:, 256:512], "QB")
+        act(T.ws[:, 0:256], T.SU[:, t:4096:16], F.Identity, ["SU"], ["ws0"], 256)
+        iota(T.wv[:, 256:512], [[16, 256]], ["wv1"], 256, base=t)
+        dma("Y", T.wm[:, 256:512], DG[:, t:t + 256], ["DG"], ["wm1"], 65536)
+        act(nWf, iWf, F.Identity, ["iWf"], ["nWf"], 16, bias=float(t), scale=16.0)
+        P([(ps[3][:, 0:384], ONE[0:64, 0:128], CK[0:64, 0:384], True, False, 384),
+           (ps[4][:, 0:400], ONE[0:64, 0:128], CK[0:64, 0:400], True, False, 400)], ["ONE", "CK"], ["K0", "K1"], [3, 4], True)
+        Rw = T.R[:, 0:5120]
+        act(T.old[:, 4096:4352], Rw.indirect(wl_), F.Exp, ["R", "R5", "wl_"], ["oldw"], 256 * GA, bias=-9 * LN256,
+            scale=LN256)
+        tt(T.eq[:, 4096:4352], ps[2][:, 0:256], T.old[:, 4096:4352], A.is_equal, ["pX", "oldw"], ["eqw"], 256, [2])
+        mms = []
+        for h in range(2):
+            o = ps[4][:, 384 + 8 * h:392 + 8 * h]
+            cs = slice(4096 + 128 * h, 4224 + 128 * h)
+            mms += [(o, T.old[:, cs], WK17, False, False, 64), (o, T.eq[:, cs], WK17, False, False, 64),
+                    (o, T.G[:, 128 * h:128 * h + 128], SEL8, False, False, 256)]
+        P(mms, ["oldw", "eqw", "WK17", "G", "SEL8"], ["K1"], [4], True)
+        P([(ps[3 + h][:, 0:128], T.VD[:, 128 * h:128 * h + 128], If, False, False, 512) for h in range(2)],
+          vk + ["If"], ["K0", "K1"], [3, 4], True)
+        for q in range(8):
+            cs = slice(512 * q, 512 * q + 512)
+            act(T.old[:, cs], T.R[:, 0:4096].indirect(T.VT[:, 32 * q:32 * q + 32]), F.Exp, ["R", "VT%d" % (q // 2)],
+                ["old%d" % q], 512 * GA, bias=-9 * LN256, scale=LN256)
+            tt(T.eq[:, cs], ps[2][:], T.old[:, cs], A.is_equal, ["pX", "old%d" % q], ["eq%d" % q], 512, [2])
+            m1, m2 = [], []
+            for k in (2 * q, 2 * q + 1):
+                for h in range(2):
+                    c2 = slice(256 * k + 128 * h, 256 * k + 128 * h + 128)
+                    m1.append((ps[3 + h][:, k:128:16], T.old[:, c2], cW[:, 384:392], False, False, 64))
+                    m2.append((ps[3 + h][:, k:384:16], T.eq[:, c2], WKE, False, k == 15, 64))
+            P(m1, ["old%d" % q, "WKE0"], ["K0", "K1"], [3, 4], True)
+            P(m2, ["eq%d" % q, "WKE0", "WKE1", "WKE2"], ["K0", "K1"], [3, 4], True)
+        for h in range(2):
+            V(lambda h=h: g.vector.tensor_tensor_scan(T.sc2[:, 128 * h:128 * h + 128], T.MS[:], ps[3 + h][:, 0:128], 0.0,
+                                                      A.add, A.min), ["MS", "K%d" % h], ["sc2%d" % h], 128, [3 + h])
+        tt(keyT, T.sc2[:, 15:256:16], ps[4][:, 384:400], A.min, ["sc20", "sc21", "K1"], ["keyT"], 16, [4])
+        ts(hiT, keyT, 4032, A.bitwise_and, ["keyT"], ["hiT"], 16)
+        ts(loT, keyT, 63, A.bitwise_and, ["keyT"], ["loT"], 16)
+        cp(hl, si[:, 48:80], ["hiT", "loT"], ["hl"], 32)
+        P([(ps[5][0:32, 0:128], hl, Ib, True, True, 128)], ["hl", "Ib"], ["TT"], [5])
+        act(T.TTs[0:32, :], ps[5][0:32, 0:128], F.Identity, ["TT"], ["TTs"], 128, banks=[5])
+        P([(ps[6][:, 128 * h:128 * h + 128], T.SR[0:32, 128 * h:128 * h + 128], T.TTs[0:32, :], True, True, 128)
+           for h in range(2)], ["SR0", "SR1", "TTs"], ["uR"], [6])
+        cp(T.cR[:], ps[6][:, 0:256], ["uR"], ["cR"], 256, [6])
+        act(T.wv[:, 0:256], ps[6][:, 0:256], F.Identity, ["uR"], ["wv0"], 256, banks=[6])
+        if CFG["XU"] == "U":
+            tt(uT, hiT, loT, A.add, ["hiT", "loT"], ["uT"], 32)
+            tt(T.xu[:], uT.indirect(X1), DG[:, 0:256], A.mult, ["uT", "X1", "DG"], ["xu"], 256 * GA)
+            P([(ps[7][:, 8 * h:8 * h + 8], T.xu[:, 128 * h:128 * h + 128], SEL8, True, True, 256) for h in range(2)],
+              ["xu", "SEL8"], ["pU"], [7])
+        else:
+            spread(CFG["XU"], T.xq[:], fb[:, 144:192], X3, 1.0, ["hl", "X3"], ["xq"], 256)
+            P(toW(T.xq, 7, 0, 16, 32, 0, True) + toW(T.xq, 7, 0, 16, 32, 16), ["xq", "L8"], ["pU"], [7])
+        cp(ul, ps[7][:, 0:16], ["pU"], ["ul"], 16, [7])
+        cp(uWf, ps[7][:, 0:16], ["pU"], ["uWf"], 16, [7])
+        for h in range(2):
+            ts(fb[:, 112 + 8 * h:120 + 8 * h], si[:, 32 + 8 * h:40 + 8 * h], 65536.0, A.is_ge, ["keyT", "thT"], ["thrW%d" % h],
+               16, cf[:, 32 + 8 * h:33 + 8 * h], A.mult)
+        tt(hardT, keyT, thrA, A.is_ge, ["keyT", "thrA"], ["hardT"], 32)
+        spread(CFG["XW"], T.xw[:], fb[:, 112:144], X2, 1 / 2.55, ["thrW0", "thrW1", "X2"], ["xw"], 128)
+        P([(ps[0][:, k:128:8], T.L8[:, 128 * k:128 * k + 128], T.xw[:, 16 * k:16 * k + 16], True, True, 64)
+           for k in range(8)], ["L8", "xw"], ["pY"], [0])
+        act(T.wsel[:], ps[0][:, 0:128], F.Identity, ["pY"], ["wsel"], 128, banks=[0])
+        zsum(T.Zb, "Zb", T.wsel, "wsel", 0, 256, "pB", range(15, -1, -1), True)
+        zcalls(T.Zc, "Zc", T.cR, "cR", uWf, "uWf")
+        tt(nb, ps[0][:, 256:272], thT, A.is_lt, ["pB", "thT"], ["nb"], 16, [0])
+        tt(thrM, nb, thrW, A.mult, ["nb", "thrW0", "thrW1"], ["thrM"], 32)
+        tt(thrC, thrM, hardT, A.mult, ["thrM", "hardT"], ["thrC"], 32)
+        zsum(T.Zc, "Zc", T.wsel, "wsel", 5, 288, "Sc", range(15, 5, -1), True, True)
+        zsum(T.Zc, "Zc", T.wsel, "wsel", 5, 288, "Sc", range(5, 1, -1), False, True)
+        zsum(T.Zc, "Zc", T.wsel, "wsel", 5, 288, "Sc", (1,), False, True)
+        zsum(T.Zc, "Zc", T.wsel, "wsel", 5, 288, "Sc", (0,), False, True)
+        tt(clT, ps[5][:, 288:304], thrC, A.is_lt, ["Sc", "thrC"], ["clT"], 16, [5])
+        tt(nmT, ps[5][:, 288:304], thrM, A.is_ge, ["Sc", "thrM"], ["nmT"], 16, [5])
+        tt(ngT, nmT, clT, A.add, ["nmT", "clT"], ["ngT"], 32)
+        spread(CFG["XL"], T.xl[:], fb[:, 0:32], X2, 256.0, ["clT", "X2"], ["xl"], 128)
+        P([(ps[5][:, 320:336], Ib, iWb, True, False, 64)] + toW(T.xl, 5, 320), ["Ib", "iWb", "xl", "L8"], ["pS"], [5])
+        cp(sel, ps[5][:, 320:336], ["pS"], ["sel"], 16, [5])
+        act(T.efu[:], T.EF[:].indirect(ul), F.Identity, ["EF", "ul"], ["efu"], 256 * GA)
+        P([(ps[1][:, 0:256], Ib, T.efu[:], True, False, 256), (ps[1][:, 0:256], Ib, xb, False, True, 256)],
+          ["Ib", "efu", xn], ["wR"], [1])
+        act(T.sgA[:], ps[1][:, 0:256], F.Sign, ["wR"], ["sgA"], 256, bias=-3.5, banks=[1])
+        P([(ps[1][:, 0:256], Ib, T.efu[:], True, False, 256), (ps[1][:, 0:256], Ib, xb, False, True, 256),
+           (ps[1][:, 0:256], Im2, T.sgA[:], False, True, 256)], ["Im2", "sgA", "Ib", "efu", xn], ["wR"], [1])
+        act(T.xJ[:, 0:256], ps[1][:, 0:256], F.Identity, ["wR"], ["xA"], 256, bias=-2.0, banks=[1])
+        u = t + 1
+        if u < NS:
+            s1, s2 = T["s1_%d" % u], T["s2_%d" % u]
+            act(s1[:, 0:256], T.xJ[:, 0:512].indirect(sel), F.Identity, ["xA", "xB", "sel"], ["s1_%d" % u], 256 * GA)
+            if CFG["JS"]:
+                jmask(T.xJ[:, 512:768], "jA", T.xJ[:, 0:256], "xA", T.QJ[:, 0:256], "QA")
+                act(s1[:, 256:512], T.xJ[:, 512:1024].indirect(sel), F.Identity, ["jA", "jB", "sel"], ["s1j%d" % u], 256 * GA)
+                send(nxt, T["wx%d" % u][:, 256:768], s1[:], "a1_%d" % u, ["s1_%d" % u, "s1j%d" % u], ["m1_%d" % u])
+            else:
+                send(nxt, T["wx%d" % u][:, 256:512], s1[:, 0:256], "a1_%d" % u, ["s1_%d" % u], ["m1_%d" % u])
+            recv(prv, "a1_%d" % u, ["m1_%d" % u], ["xb%d" % u])
+        act(T.vnR[:], T.wv[:].indirect(sel), F.Identity, ["wv0", "wv1", "sel"], ["vnR"], 256 * GA)
+        if u < NS:
+            ts(clW, ps[5][:, 320:336], 256.0, A.is_ge, ["pS"], ["clW"], 16, banks=[5])
+            tt(dnW, nWf, uWf, A.subtract, ["nWf", "uWf"], ["dnW"], 32)
+            tt(t1, clW, dnW, A.mult, ["clW", "dnW"], ["t1"], 32)
+            tt(vnW, t1, uWf, A.add, ["t1", "uWf"], ["vnW"], 32)
+            cp(s2[:, 256:272], vnW, ["vnW"], ["s2v%d" % u], 16)
+            if CFG["VR"] == "V":
+                cp(s2[:, 0:256], T.wv[:].indirect(sel), ["wv0", "wv1", "sel"], ["s2_%d" % u], 256 * GA)
+            else:
+                cp(s2[:, 0:256], T.vnR[:], ["vnR"], ["s2_%d" % u], 256)
+            send(nxt, T["l2_%d" % u][:], s2[:], "a2_%d" % u, ["s2_%d" % u, "s2v%d" % u], ["m2_%d" % u])
+            recv(prv, "a2_%d" % u, ["m2_%d" % u], ["vR_%d" % u])
+        else:
+            home, frm = T.cores[(rank - t) % N], T.cores[(rank + t) % N]
+            act(T.xh[:], T.xJ[:, 0:512].indirect(sel), F.Identity, ["xA", "xB", "sel"], ["xh"], 256 * GA)
+            send(home, T.lx[:], T.xh[:], "a1_%d" % u, ["xh"], ["m1_%d" % u])
+            recv(frm, "a1_%d" % u, ["m1_%d" % u], ["lx"])
+            send(home, T.lv[:], T.vnR[:], "a2_%d" % u, ["vnR"], ["m2_%d" % u])
+            recv(frm, "a2_%d" % u, ["m2_%d" % u], ["lv"])
+            dma("Y", T.yx[:], T.lx[:], ["lx"], ["yx"], 65536)
+            dma("Y", T.yv[:], T.lv[0:128:16, :], ["lv"], ["yv"], 8192)
+        spread(CFG["XM"], T.xg[:], fb[:, 32:80], X3, 8192.0, ["nmT", "ngT", "X3"], ["xg"], 256)
+        P(toW(T.xg, 5, 336, 32, 32, 0, True) + [(ps[5][:, 336:352], If, uWf, False, True, 256),
+                                                (ps[5][:, 352:368], If, bWf, False, True, 256)],
+          ["If", "uWf", "bWf", "xg", "L8"], ["pG"], [5])
+        tt(lfGM, ps[5][:, 336:368], cf[:, 64:96], A.min, ["pG", "DW0", "DW1"], ["lfGM"], 32, [5])
+        cp(su[:, 96:128], lfGM, ["lfGM"], ["lGM"], 32)
+        act(T.wc[:], T.SU[:, 0:4096].indirect(ul), F.Identity, ["SU", "ul"], ["wc"], 256 * GA)
+        act(T.Qc[:], T.wc[:], F.Identity, ["wc"], ["Qc"], 256, bias=196096.5)
+        P([(ps[7][:, 256:512], If, T.wc[:], True, False, 1024), (ps[7][:, 256:512], In, T.Qc[:], False, True, 256)],
+          ["If", "In", "wc", "Qc"], ["pC"], [7])
+        act(T.ws[:, 256:512], ps[7][:, 256:512], F.Identity, ["pC"], ["ws1"], 256, bias=200704.0, banks=[7])
+        act(T.SU[:, t:4096:16], T.ws[:].indirect(sel), F.Identity, ["ws0", "ws1", "sel"], ["SU"], 256 * GA)
+        P([(ps[7][:, 256:512], If, T.vnR[:], True, False, 1024), (ps[7][:, 256:512], I8k, jm, False, True, 256)],
+          ["If", "I8k", "vnR", jn], ["pC"], [7])
+        act(T.u2[:], ps[7][:, 256:512], F.Relu, ["pC"], ["u2"], 256, bias=-8192.0, banks=[7])
+        if CFG["TP"] == "V":
+            tt(T.tp[:], T.SU[:, 0:4096].indirect(vW), nj[:], A.mult, ["SU", vWn, njn], ["tp"], 256 * GA)
+        else:
+            act(T.sv[:], T.SU[:, 0:4096].indirect(vW), F.Identity, ["SU", vWn], ["sv"], 256 * GA)
+            P([(ps[0][:, 256:512], If, T.sv[:], True, False, 1024), (ps[0][:, 256:512], In8, jm, False, True, 256)],
+              ["If", "In8", "sv", jn], ["pB"], [0])
+            act(T.tp[:], ps[0][:, 256:512], F.Relu, ["pB"], ["tp"], 256, banks=[0])
+        tt(T.SU[:].indirect(lF), T.tp[:], T.u2[:], A.add, ["tp", "u2", "lF"], ["SU"], 256 * SC)
+        if CFG["EQC"] == "V":
+            act(T.rc[:], T.R[:, 0:4096].indirect(ul), F.Exp, ["R", "ul"], ["rc"], 256 * GA, bias=-9 * LN256, scale=LN256)
+            tt(T.eqc[:], ps[2][:, 0:256], T.rc[:], A.is_equal, ["pX", "rc"], ["eqc"], 256, [2])
+        else:
+            act(T.rc[:], T.R[:, 0:4096].indirect(ul), F.Identity, ["R", "ul"], ["rc"], 256 * GA)
+            P([(ps[2][:, 0:256], Ib, T.rc[:], True, False, 256), (ps[2][:, 0:256], In, xb, False, True, 256)],
+              ["Ib", "In", "rc", xn], ["pX"], [2])
+            act(T.ea[:], ps[2][:, 0:256], F.Abs, ["pX"], ["ea"], 256, banks=[2])
+            act(T.eqc[:], T.ea[:], F.Relu, ["ea"], ["eqc"], 256, bias=1.0, scale=-1.0)
+        P([(ps[2][:, 256 * h:256 * h + 256], T.eqc[:, 128 * h:128 * h + 128], WEC, True, True, 256) for h in range(2)],
+          ["eqc", "WEC0", "WEC1"], ["pX"], [2])
+        act(T.Ec[:], ps[2][:], F.Identity, ["pX"], ["Ec"], 512, banks=[2])
+        for h in range(2):
+            tt(T.Xi[:, 256 * h:256 * h + 256], ps[3 + h][:, 128:384], T.Ec[:, 256 * h:256 * h + 256], A.add,
+               ["K%d" % h, "Ec"], ["Xi%d" % h], 256, [3 + h])
+        ts(T.Xa[:], T.Xi[:], 43690, A.bitwise_and, ["Xi0", "Xi1"], ["Xa"], 512)
+        ts(T.ok[:], T.Xa[:], 0.0, A.is_equal, ["Xa"], ["ok"], 512)
+        P([(ps[6][:, 256 + 128 * h:384 + 128 * h], T.ok[:, 256 * h + 128 * q:256 * h + 128 * q + 128], Ib, q == 0, q == 1, 128)
+           for h in range(2) for q in range(2)], ["ok", "Ib"], ["pE"], [6])
+        act(T.wm[:, 0:256], ps[6][:, 256:512], F.Relu, ["pE"], ["wm0"], 256, bias=-1.0, banks=[6])
+        act(T.mm[:], T.wm[:].indirect(sel), F.Identity, ["wm0", "wm1", "sel"], ["mm"], 256 * GA)
+        if CFG["TV"] == "V":
+            P([(ps[6][:, 0:256], If, T.vnR[:], True, False, 1024), (ps[6][:, 0:256], Ifn, verK, False, True, 1024)],
+              ["If", "Ifn", "vnR"] + vk, ["uR"], [6])
+            tt(T.tv[:], ps[6][:, 0:256], T.mm[:], A.mult, ["uR", "mm"], ["tv"], 256, [6])
+            tt(T.VL[:].indirect(lM), verK, T.tv[:], A.add, vk + ["tv", "lGM"], ["VL"], 256 * SC)
+        else:
+            P([(ps[6][:, 0:256], If, T.vnR[:], True, False, 1024), (ps[6][:, 0:256], I8k, T.mm[:], False, True, 256),
+               (ps[6][:, 256:512], If, verK, True, False, 1024), (ps[6][:, 256:512], In8, T.mm[:], False, True, 256)],
+              ["If", "I8k", "In8", "vnR", "mm"] + vk, ["uR", "pE"], [6])
+            act(T.tv[:], ps[6][:, 0:256], F.Relu, ["uR"], ["tv"], 256, bias=-8192.0, banks=[6])
+            act(T.tw[:], ps[6][:, 256:512], F.Relu, ["pE"], ["tw"], 256, banks=[6])
+            tt(T.VL[:].indirect(lM), T.tw[:], T.tv[:], A.add, ["tw", "tv", "lGM"], ["VL"], 256 * SC)
+        P([(ps[1][:, 256:512], In, xb, True, False, 256), (ps[1][:, 256:512], I16, T.eqc[:], False, True, 256)],
+          ["In", "I16", xn, "eqc"], ["pb"], [1])
+        act(T.ga[:], ps[1][:, 256:512], F.Relu, ["pb"], ["ga"], 256, bias=-7.0, banks=[1])
+        act(T.gn[:], T.ga[:], F.Identity, ["ga"], ["gn"], 256, bias=9.0, scale=-1.0)
+        cp(T.R[:].indirect(lG), T.gn[:], ["gn", "lGM", "R5"], ["R"], 256 * SC)
+        act(wx[:, 0:256], T.R[:, t:4096:16], F.Identity, ["R"], ["wx0_%d" % t], 256)
+        act(T.R[:, t:4096:16], wx[:, 0:512].indirect(sel), F.Identity, ["wx0_%d" % t, xn, "sel"], ["R"], 256 * GA)
+        if u < NS:
+            cnt = lambda o: [(ps[7][:, o + 8 * k:o + 8 * k + 8], ONE[:, 0:128], fb[:, 8 * h:8 * h + 8], h == 0, h == 1, 64)
+                             for k in range(2) for h in range(2)]
+            P(cnt(16), ["ONE", "clT"], ["pA"], [7])
+            act(Q2, ps[7][:, 16:32], F.Identity, ["pA"], ["Q2"], 16, bias=256.0, banks=[7])
+            P([(ps[7][:, 32:48], In, Q2, True, False, 64)] + [m[:3] + (False,) + m[4:] for m in cnt(32)],
+              ["ONE", "clT", "In", "Q2"], ["pT"], [7])
+            act(par2, ps[7][:, 32:48], F.Abs, ["pT"], ["par2"], 16, bias=2.0 ** 24, scale=65536.0, banks=[7])
+            act(thrA, par2, F.Identity, ["par2"], ["thrA"], 16, bias=4.0 * 65536)
+
+    dma("Y", T.yr[:], T.R[:, 0:4096], ["R"], ["yr"], 1048576)
+    dma("Y", T.yl[:], T.VL[:, 0:1024], ["VL"], ["yl"], 524288)
+    for q in range(8):
+        P([(ps[1][:, k:256:32], T.SU[:, 128 * k:128 * k + 128], SEL8, True, True, 256) for k in range(4 * q, 4 * q + 4)],
+          ["SU", "SEL8"], ["wR"], [1])
+    act(T.y1[:], ps[1][:, 0:256], F.Identity, ["wR"], ["y1"], 256, banks=[1])
+    P([(ps[0][:, 128 * h:128 * h + 128], T.y1[:, 128 * h:128 * h + 128], If, True, True, 512) for h in range(2)],
+      ["y1", "If"], ["pY"], [0])
+    act(T.y2[:], ps[0][:, 0:256], F.Identity, ["pY"], ["y2"], 256, banks=[0])
+    for h in range(2):
+        dma("Y", T.ys[4 * h:4 * h + 4, :], T.y2[:, 128 * h:128 * h + 128], ["y2"], ["ys%d" % h], 65536)
+    return ops
+
+
+HOP, SELF = 110.0, 60.0
+
+
+def plan(ops):
+    lastw, readers = {}, {}
+    for o in ops:
+        d = set()
+        for r in o["r"]:
+            if r in lastw:
+                d.add(lastw[r])
+        for w in o["w"]:
+            if w in lastw:
+                d.add(lastw[w])
+            d.update(readers.get(w, ()))
+        d.discard(o["i"])
+        o["d"] = d
+        for r in o["r"]:
+            readers.setdefault(r, []).append(o["i"])
+        for w in o["w"]:
+            lastw[w] = o["i"]
+            readers[w] = []
+    succ = [[] for _ in ops]
+    for o in ops:
+        for d in o["d"]:
+            succ[d].append(o["i"])
+    for o in reversed(ops):
+        o["p"] = o["c"] + o.get("lat", 0) + max([HOP + ops[s]["p"] for s in succ[o["i"]]], default=0)
+    left = [len(o["d"]) for o in ops]
+    ready = [o["i"] for o in ops if not o["d"]]
+    free, bank, order = {}, {}, []
+
+    def est(o):
+        s = 0.0 if o["e"] == "X" else free.get(o["e"], 0.0)
+        for d in o["d"]:
+            p = ops[d]
+            s = max(s, p["end"] + (0 if p["e"] == o["e"] == "P" else SELF if p["e"] == o["e"] else HOP))
+        for b in o["b"]:
+            for e, tm in bank.get(b, {}).items():
+                if e != o["e"]:
+                    s = max(s, tm + HOP)
+        return s
+
+    while ready:
+        c = [(est(ops[i]), i) for i in ready]
+        m = min(c)
+        e = ops[m[1]]["e"]
+        s, i = max([x for x in c if ops[x[1]]["e"] == e and x[0] <= m[0] + 70], key=lambda x: (ops[x[1]]["p"], -x[1]))
+        o = ops[i]
+        o["s"] = s
+        o["end"] = s + o["c"] + o.get("lat", 0)
+        free[e] = s + o["c"]
+        for b in o["b"]:
+            bank.setdefault(b, {})[e] = o["end"]
+        order.append(o)
+        ready.remove(i)
+        for j in succ[i]:
+            left[j] -= 1
+            if left[j] == 0:
+                ready.append(j)
+
+    def hop(a, b):
+        return 1.0 if a["e"] == b["e"] == "P" else SELF if a["e"] == b["e"] else HOP
+
+    def fit(lst, s, c, own):
+        lo, hi = 0, len(lst)
+        while lo < hi:
+            mid = (lo + hi) // 2
+            if lst[mid][0] < s - 6000:
+                lo = mid + 1
+            else:
+                hi = mid
+        pad = 0.0 if own is None else HOP
+        for a, b, e in lst[lo:]:
+            if a - pad >= s + c:
+                break
+            if e != own and b + pad > s:
+                s = b + pad
+        return s
+
+    def put(lst, it):
+        k = len(lst)
+        while k and lst[k - 1][0] > it[0]:
+            k -= 1
+        lst.insert(k, it)
+
+    def sweep(seq, back):
+        at, eng, bk = {}, {}, {}
+        for i in seq:
+            o = ops[i]
+            if back:
+                s = max([at[j] + ops[j]["c"] + hop(o, ops[j]) for j in succ[i]], default=0.0) + o.get("lat", 0)
+            else:
+                s = max([at[j] + ops[j]["c"] + ops[j].get("lat", 0) + hop(ops[j], o) for j in o["d"]], default=0.0)
+            if o["e"] != "X":
+                while True:
+                    s2 = fit(eng.setdefault(o["e"], []), s, o["c"], None)
+                    for b in o["b"]:
+                        s2 = fit(bk.setdefault(b, []), s2, o["c"], o["e"])
+                    if s2 == s:
+                        break
+                    s = s2
+                put(eng[o["e"]], (s, s + o["c"], o["e"]))
+                for b in o["b"]:
+                    put(bk[b], (s, s + o["c"], o["e"]))
+            at[i] = s
+        return at
+
+    at = {o["i"]: o["s"] for o in ops}
+    best = (max(o["end"] for o in ops), at)
+    for seed in CFG["SEEDS"]:
+        key, sh = {}, {}
+        for o in ops:
+            nm = o["e"] + o["w"][0].split("_")[0]
+            if nm not in sh:
+                seed = (seed * 1103515245 + 12345) % 2147483648
+                z = (seed >> 8) % 1000 / 1000.0
+                sh[nm] = (z / CFG["FRAC"] - 0.5) * 2 * CFG["NOISE"] if z < CFG["FRAC"] else 0.0
+            key[o["i"]] = max([best[1][o["i"]] + sh[nm]] + [key[d] + 0.01 for d in o["d"]])
+        at = sweep(sorted(key, key=lambda i: (key[i], i)), False)
+        for _ in range(CFG["IT"]):
+            bk_ = sweep(sorted(at, key=lambda i: (-(at[i] + ops[i]["c"] + ops[i].get("lat", 0)), -i)), True)
+            at = sweep(sorted(bk_, key=lambda i: (-(bk_[i] + ops[i]["c"]), i)), False)
+            end = max(at[i] + ops[i]["c"] + ops[i].get("lat", 0) for i in at)
+            if end < best[0]:
+                best = (end, at)
+    for o in ops:
+        o["s"] = best[1][o["i"]]
+        o["end"] = o["s"] + o["c"] + o.get("lat", 0)
+    return sorted(ops, key=lambda o: (o["s"], o["i"]))
+
+
+def emit(g, T, ops, order):
+    q = {"V": g.vector, "S": g.scalar, "P": g.tensor, "G": g, "Y": g.sync}
+    pos, bank, seen, need = {}, {}, {}, set()
+    for n, o in enumerate(order):
+        pos[o["i"]] = n
+    for o in order:
+        if o["e"] == "X":
+            continue
+        d = set(o["d"])
+        for b in o["b"]:
+            for e, i in bank.get(b, {}).items():
+                if e != o["e"]:
+                    d.add(i)
+            bank.setdefault(b, {})[o["e"]] = o["i"]
+        best, ws = {}, []
+        for i in d:
+            p = ops[i]
+            if "sem" in p:
+                if (o["e"], p["sem"]) not in seen:
+                    seen[(o["e"], p["sem"])] = 1
+                    ws.append(i)
+            elif "send" in p or (p["e"] == o["e"] == "P"):
+                continue
+            elif pos[i] > best.get(p["e"], -1):
+                best[p["e"]] = pos[i]
+        for e, n in best.items():
+            if n > seen.get((o["e"], e), -1):
+                seen[(o["e"], e)] = n
+                ws.append(order[n]["i"])
+                need.add(order[n]["i"])
+        o["ws"] = ws
+    cnt, sent = {}, 0
+    for o in order:
+        e = o["e"]
+        if e == "X":
+            continue
+        for i in o["ws"]:
+            p = ops[i]
+            if "sem" in p:
+                q[e].wait_ge(T.sem[p["sem"]], p.get("val", 16))
+            else:
+                q[e].wait_ge(T.sem["s" + p["e"]], p["n"])
+        ins = o["f"]()
+        if "sem" in o:
+            ins.then_inc(T.sem[o["sem"]], 16)
+        elif "send" in o:
+            sent += o["send"]
+        elif o["i"] in need:
+            cnt[e] = cnt.get(e, 0) + 1
+            o["n"] = cnt[e]
+            ins.then_inc(T.sem["s" + e], 1)
+    g.wait_ge(T.sem.sent, sent)
+    for o in ops:
+        if "sem" in o and o["e"] != "X" and o["w"][0].startswith("y"):
+            g.wait_ge(T.sem[o["sem"]], 16)
+
+
+def rank_program(g, core, T, topo):
+    rank = T.rank_of(core)
+    if rank is None:
+        return
+    ops = build(g, core, T, topo, rank)
+    if "o" not in ORDER:
+        ORDER["o"] = [(o["i"], o["d"]) for o in plan(ops)]
+    for i, d in ORDER["o"]:
+        ops[i]["d"] = d
+    emit(g, T, ops, [ops[i] for i, d in ORDER["o"]])

@@ -53,8 +53,9 @@ for _b in range(8):
 SCRATCH.update({"fb": ("sbuf", [128, 256], BF), "ja": ("sbuf", [128, 256], BF), "ea": ("sbuf", [128, 256], BF),
                 "tw": ("sbuf", [128, 256], F32), "xg": ("sbuf", [128, 256], BF), "xq": ("sbuf", [128, 256], BF)})
 SCRATCH["Ec"] = ("sbuf", [128, 512], F32)
-CFG = dict(EQC="V", TV="S", XU="U", XW="S", XL="S", XM="S", XF="S", VD="VS", VR="S", ZO=1, IT=1, TP="V", JS=0,
-           SEEDS=[i * 7919 + 3 for i in range(500)], NOISE=600, FRAC=0.1)
+CFG = dict(EQC="V", TV="S", XU="U", XW="S", XL="S", XM="S", XF="S", VD="W", VR="S", ZO=1, IT=1, TP="V", JS=0,
+           VT=((0, 1), (1, 4)), UW="S", VN="R",
+           SEEDS=[i * 7919 + 3 for i in range(1200)], NOISE=600, FRAC=0.1)
 SCRATCH["xJ"] = ("sbuf", [128, 1024], BF)
 SCRATCH["QJ"] = ("sbuf", [128, 512], BF)
 SCRATCH["sv"] = ("sbuf", [128, 256], F32)
@@ -62,13 +63,14 @@ for _t in range(NS):
     SCRATCH["wx%d" % _t] = ("sbuf", [128, 768], BF)
 for _t in range(1, NS):
     SCRATCH["s1_%d" % _t] = ("sbuf", [128, 512], BF)
+SCRATCH["kb"] = ("sbuf", [128, 96], BF)
 ORDER = {}
 
-NDMA = 24
+NDMA = 32
 SEMAPHORES = (["sV", "sS", "sP", "sG", "sent"] + ["d%d" % i for i in range(NDMA)]
               + ["a1_%d" % t for t in range(1, NS + 1)] + ["a2_%d" % t for t in range(1, NS + 1)])
 
-CV, CP, GA, SC = 1.0, 0.55, 1.55, 3.8
+CV, CP, GA, SC, OV = 0.92, 0.5, 1.55, 3.8, 25.0
 LN256 = math.log(256.0)
 
 
@@ -76,20 +78,20 @@ def build(g, core, T, topo, rank):
     N = len(T.cores)
     nxt, prv = T.cores[(rank + 1) % N], T.cores[(rank - 1) % N]
     ops = []
-    nd = [0]
+    nd, phase = [0], ["a"]
     ps = [T["ps%d" % b] for b in range(8)]
 
     def add(e, f, r, w, c, banks=(), **kw):
         o = dict(e=e, f=f, r=list(r) + ([] if e == "P" else ["B%d" % b for b in banks]), w=list(w), c=c, b=tuple(banks),
-                 i=len(ops))
+                 i=len(ops), t=phase[0])
         o.update(kw)
         ops.append(o)
 
     def V(f, r, w, n, banks=()):
-        add("V", f, r, w, max(64, n) * CV, banks)
+        add("V", f, r, w, max(64, n) * CV + OV, banks)
 
     def S(f, r, w, n, banks=()):
-        add("S", f, r, w, max(64, n) * CV + 30, banks)
+        add("S", f, r, w, max(64, n) * CV + 30 + OV, banks)
 
     def P(mms, r, w, banks, grp=False, given=False):
         def f():
@@ -193,36 +195,37 @@ def build(g, core, T, topo, rank):
     ts(cf[:, 12:14], cf[:, 4:6], -1.0, A.mult, ["wl", "wh"], ["nw"], 2)
     cI = T.cI
     Ib, In, I16, Im2, I8k = [cI[:, 128 * j:128 * j + 128] for j in range(5)]
-    for ap, nm, val in ((Ib, "Ib", 1.0), (In, "In", -1.0), (I16, "I16", 16.0), (Im2, "Im2", -2.0), (I8k, "I8k", 8192.0)):
-        ts(ap, F128, partf, A.is_equal, ["F128", "pg"], [nm], 128, val, A.mult)
     If, Ifn, BO, SB = [T.cI32[:, 128 * j:128 * j + 128] for j in range(4)]
+    In8 = T.L8[:, 1024:1152]
     ts(If, F128, partf, A.is_equal, ["F128", "pg"], ["If"], 128)
-    ts(Ifn, F128, partf, A.is_equal, ["F128", "pg"], ["Ifn"], 128, -1.0, A.mult)
+    for ap, nm, val in ((Ib, "Ib", 1.0), (In, "In", -1.0), (I16, "I16", 16.0), (Im2, "Im2", -2.0), (I8k, "I8k", 8192.0),
+                        (In8, "In8", -8192.0)):
+        act(ap, If, F.Identity, ["If"], [nm], 128, scale=val)
+    if CFG["TV"] == "V":
+        act(Ifn, If, F.Identity, ["If"], ["Ifn"], 128, scale=-1.0)
     ts(BO, CG, gf, A.is_equal, ["CG", "pg"], ["BO"], 128)
     ts(SB, CG, partf, A.is_equal, ["CG", "pg"], ["SB"], 128)
     cW = T.cW
-    WT, WEC, WKE, WK17, S16 = cW[:, 0:128], cW[:, 128:384], cW[:, 384:408], cW[:, 408:416], cW[:, 416:432]
-    ts(WT, CG, gf, A.is_equal, ["CG", "pg", "wt"], ["WT"], 128, wt, A.mult)
-    ts(cW[:, 128:256], CG, gf, A.is_equal, ["CG", "pg", "wl"], ["WEC0"], 128, wl, A.mult)
-    ts(cW[:, 256:384], CG, gf, A.is_equal, ["CG", "pg", "wh"], ["WEC1"], 128, wh, A.mult)
+    WT, WEC, WKE, WK17 = cW[:, 0:128], cW[:, 128:384], cW[:, 384:408], cW[:, 408:416]
+    act(WT, BO, F.Identity, ["BO", "wt"], ["WT"], 128, scale=wt)
+    act(cW[:, 128:256], BO, F.Identity, ["BO", "wl"], ["WEC0"], 128, scale=wl)
+    act(cW[:, 256:384], BO, F.Identity, ["BO", "wh"], ["WEC1"], 128, scale=wh)
     F8 = io[:, 0:8]
-    ts(cW[:, 384:392], F8, gf, A.is_equal, ["F128", "pg"], ["WKE0"], 8, -65536.0, A.mult)
-    ts(cW[:, 392:400], F8, gf, A.is_equal, ["F128", "pg", "nw"], ["WKE1"], 8, nwl, A.mult)
-    ts(cW[:, 400:408], F8, gf, A.is_equal, ["F128", "pg", "nw"], ["WKE2"], 8, nwh, A.mult)
-    ts(WK17, F8, gf, A.is_equal, ["F128", "pg"], ["WK17"], 8, -2.0 ** 21, A.mult)
     SEL8, thT, iWf, DW, thrA = cf[:, 16:24], cf[:, 32:48], cf[:, 48:64], cf[:, 64:112], cf[:, 112:128]
     ts(SEL8, F8, gf, A.is_equal, ["F128", "pg"], ["SEL8"], 8)
+    act(cW[:, 384:392], SEL8, F.Identity, ["SEL8"], ["WKE0"], 8, scale=-65536.0)
+    act(cW[:, 392:400], SEL8, F.Identity, ["SEL8", "nw"], ["WKE1"], 8, scale=nwl)
+    act(cW[:, 400:408], SEL8, F.Identity, ["SEL8", "nw"], ["WKE2"], 8, scale=nwh)
+    act(WK17, SEL8, F.Identity, ["SEL8"], ["WK17"], 8, scale=-2.0 ** 21)
     act(thT, H16, F.Exp, ["H16", "bT_"], ["thT"], 16, bias=bT_, scale=-0.55 * 128)
-    ts(iWf, io[:, 0:16], 16.0, A.mult, ["F128", "pg"], ["iWf"], 16, pf, A.add)
+    act(iWf, io[:, 0:16], F.Identity, ["F128", "pg"], ["iWf"], 16, bias=pf, scale=16.0)
     iWb = cb[:, 16:32]
-    cp(iWb, iWf, ["iWf"], ["iWb"], 16)
+    act(iWb, iWf, F.Identity, ["iWf"], ["iWb"], 16)
     for j, base in enumerate((5120.0, 1024.0, 4096.0)):
-        ts(cf[:, 64 + 16 * j:80 + 16 * j], iWf, base, A.add, ["iWf"], ["DW%d" % j], 16)
-    V(lambda: g.vector.memset(thrA, 4.0 * 65536), [], ["thrA"], 16)
+        act(cf[:, 64 + 16 * j:80 + 16 * j], iWf, F.Identity, ["iWf"], ["DW%d" % j], 16, bias=base)
+    iota(thrA, [[0, 16]], ["thrA"], 16, base=4 * 65536)
     L8 = T.L8[:, 0:1024]
     ts(L8, ib[:], pf, A.is_equal, ["ib", "pg"], ["L8"], 512)
-    In8 = T.L8[:, 1024:1152]
-    ts(In8, F128, partf, A.is_equal, ["F128", "pg"], ["In8"], 128, -8192.0, A.mult)
     DG = T.DG
     ts(DG[:], DI, pf, A.is_equal, ["DI", "pg"], ["DG"], 272)
     M2 = T.M2
@@ -240,9 +243,9 @@ def build(g, core, T, topo, rank):
             V(lambda lo=lo, hi=hi, v1=v1: g.vector.memset(CK[32:33, lo:hi], v1), ["CK"], ["CK"], 64)
     ts(CK[32:33, 0:128], io[32:33, 256:384], 4096.0, A.mult, ["DI", "CK"], ["CK"], 128)
     ts(CK[32:33, 400:528], io[32:33, 256:384], -1.0, A.mult, ["DI", "CK"], ["CK"], 128)
-    ts(T.CS[:], DG[:, 0:256], -8192.0, A.mult, ["DG"], ["CS0"], 256)
-    act(T.CT[:], DG[:, 1:257], F.Identity, ["DG"], ["CT"], 256, scale=16384.0)
-    tt(T.CS[:], T.CS[:], T.CT[:], A.add, ["CS0", "CT"], ["CS"], 512)
+    P([(ps[0][:, 256:512], In8, DG[:, 0:256], True, False, 256), (ps[0][:, 256:512], I8k, DG[:, 1:257], False, False, 256),
+       (ps[0][:, 256:512], I8k, DG[:, 1:257], False, True, 256)], ["In8", "I8k", "DG"], ["pB"], [0])
+    act(T.CS[:], ps[0][:, 256:512], F.Identity, ["pB"], ["CS"], 256, banks=[0])
     ts(T.MS[:], io[:, 256:384], 0.0, A.is_equal, ["DI"], ["MS"], 128, 2.0 ** 23, A.mult)
     cu = T.cu
     X1, X2, PM, X3 = cu[:, 0:16], cu[:, 16:24], cu[:, 32:48], cu[:, 48:64]
@@ -256,16 +259,17 @@ def build(g, core, T, topo, rank):
     for h in range(2):
         ts(T.SR[0:32, 128 * h:128 * h + 128], io[0:32, 128:256], float(8 * h), A.add, ["CG", "pg"], ["SR%d" % h], 128,
            cf[0:32, 1:2], A.is_equal)
-    V(lambda: g.vector.memset(T.R[:, 4096:5120], 5.0), [], ["R5"], 512)
+    iota(T.R[:, 4096:5120], [[0, 1024]], ["R5"], 1024, base=5)
     cp(T.SU[:, 0:1024], T.edgi[:], ["edgi"], ["SU0"], 1024)
-    act(T.SU[:, 1024:2048], T.SU[:, 0:1024], F.Identity, ["SU0"], ["SU1"], 1024)
-    act(T.SU[:, 2048:3072], T.SU[:, 0:1024], F.Identity, ["SU0"], ["SU2"], 1024)
-    act(T.SU[:, 3072:4096], T.SU[:, 0:1024], F.Identity, ["SU0", "SU1", "SU2"], ["SU"], 1024)
+    dma("Y", T.SU[:, 1024:2048], T.SU[:, 0:1024], ["SU0"], ["SU1"], 524288)
+    dma("Y", T.SU[:, 2048:3072], T.SU[:, 0:1024], ["SU0"], ["SU2"], 524288)
+    act(T.SU[:, 3072:4096], T.SU[:, 0:1024], F.Identity, ["SU0"], ["SU3"], 1024)
+    add("X", None, ["SU0", "SU1", "SU2", "SU3"], ["SU"], 1, join=True)
     cp(T.VL[:, 0:1024], T.veri[:], ["veri"], ["VL"], 1024)
     act(T.EF[:, 512:1024], T.EF[:, 0:512], F.Identity, ["EF0"], ["EF1"], 512)
-    cp(T.EF[:, 1024:2048], T.EF[:, 0:1024], ["EF0", "EF1"], ["EF2"], 512)
-    act(T.EF[:, 2048:3072], T.EF[:, 0:1024], F.Identity, ["EF0", "EF1"], ["EF3"], 1024)
-    cp(T.EF[:, 3072:4096], T.EF[:, 0:1024], ["EF0", "EF1", "EF2", "EF3"], ["EF"], 512)
+    for k in range(1, 4):
+        dma("Y", T.EF[:, 1024 * k:1024 * k + 1024], T.EF[:, 0:1024], ["EF0", "EF1"], ["EF%d" % (k + 1)], 262144)
+    add("X", None, ["EF0", "EF1", "EF2", "EF3", "EF4"], ["EF"], 1, join=True)
 
     sf, si, su, sb = T.sf, T.si, T.su, T.sb
     f16 = lambda j: sf[:, 16 * j:16 * j + 16]
@@ -279,7 +283,7 @@ def build(g, core, T, topo, rank):
                                                    su[:, 160:176])
     fb = T.fb
     clT, ngT, nmT, nfT, thrW, hl = fb[:, 0:16], fb[:, 32:48], fb[:, 48:64], fb[:, 80:96], fb[:, 112:128], fb[:, 144:176]
-    Q2, par2 = sb[:, 0:16], f16(19)
+    Q2, par2 = sb[:, 0:16], f16(23)
 
     cp(T.v8f[0:8, :], T.v8i[0:8, :], ["v8i"], ["v8f"], 256)
     P([(ps[1][:, 0:256], T.cI32[0:8, 384:512], T.v8f[0:8, :], True, True, 1024)], ["SB", "v8f"], ["wR"], [1])
@@ -295,11 +299,15 @@ def build(g, core, T, topo, rank):
         q = c % 8
         return 128 * (c // 8) + (0 if q < 4 else 64 if q < 6 else 96)
 
-    def zcalls(Z, nm, keyR, keyRn, keyW, keyWn, more=()):
+    def zcalls(Z, nm, keyR, keyRn, keyW, keyWn, more=(), bk=()):
+        o = {"Zb": 0, "Zc": 32, "Zv": 64}[nm]
+        act(T.kb[:, o:o + 16], keyW, F.Identity, [keyWn], [nm + "h"], 16, banks=bk)
+        tt(T.kb[:, o + 16:o + 32], keyW, T.kb[:, o:o + 16], A.subtract, [keyWn, nm + "h"], [nm + "l"], 32, bk)
         for c in range(16):
             s = zstart(c)
-            ts(Z[:, 256 * c + s:256 * c + 256], keyR[:, s:256], keyW[:, c:c + 1], A.is_equal, [keyRn, keyWn] + list(more),
-               ["%s%d" % (nm, c)], (256 - s) // 2)
+            ts(Z[:, 256 * c + s:256 * c + 256], keyR[:, s:256], T.kb[:, o + c:o + c + 1], A.subtract,
+               [keyRn, nm + "h", nm + "l"] + list(more), ["%s%d" % (nm, c)], (256 - s) // 2,
+               T.kb[:, o + 16 + c:o + 17 + c], A.is_equal)
 
     def zsum(Z, nm, wsel, wn, bk, o, on, cs, first, grp=False):
         mms = []
@@ -321,6 +329,7 @@ def build(g, core, T, topo, rank):
 
     for t in range(NS):
         par = t % 2
+        phase[0] = "a" if t == 0 else "z" if t == NS - 1 else "m"
         wx = T["wx%d" % t]
         xb, xn = wx[:, 256:512], "xb%d" % t
         jm, nj, jn, njn = T["jm%d" % par], T["nj%d" % par], "jm%d" % par, "nj%d" % par
@@ -351,11 +360,16 @@ def build(g, core, T, topo, rank):
         ts(wl_, T.sc1[:, 15:256:16], offp, A.add, ["sc1", "offp"], ["wl_"], 16)
         ts(bWi, wWi, 1023, A.bitwise_and, ["wWi"], ["bWi"], 16)
         cp(su[:, 0:16], bWi, ["bWi"], ["bla"], 16)
-        cp(su[:, 16:18], si[:, 16:18], ["bWi"], ["blb"], 16)
+        if t == 0 or CFG["VD"] != "W":
+            cp(su[:, 16:18], si[:, 16:18], ["bWi"], ["blb"], 16)
         cp(bWf, bWi, ["bWi"], ["bWf"], 16)
         VLw = T.VL[:, 0:1024]
         verK, vk = T.VD[:, 0:256], ["VD0", "VD1"]
-        if t == 0:
+        if t and CFG["VD"] == "W":
+            cp(T.VD[:, 0:128], VLw.indirect(su[:, 0:8]), ["VL", "bla"], ["VD0"], 128 * GA)
+            act(T.VD[:, 128:256], VLw.indirect(su[:, 8:16]), F.Identity, ["VL", "bla"], ["VD1"], 128 * GA)
+            act(T.VD[:, 256:272], VLw.indirect(su[:, 0:1]), F.Identity, ["VL", "bla"], ["VD2"], 16 * GA)
+        elif t == 0:
             cp(T.VD[:, 0:272], T.veri[:].indirect(su[:, 0:17]), ["veri", "bla", "blb"], vk, 272 * GA)
         elif CFG["VD"] == "VS":
             cp(T.VD[:, 0:128], VLw.indirect(su[:, 0:8]), ["VL", "bla"], ["VD0"], 128 * GA)
@@ -366,10 +380,10 @@ def build(g, core, T, topo, rank):
             cp(T.VD[:, 0:272], VLw.indirect(su[:, 0:17]), ["VL", "bla", "blb"], vk, 272 * GA)
         for h in range(2):
             V(lambda h=h: g.vector.transpose(T.VX[:, 256 * h:256 * h + 256], T.VD[:, 16 * h:16 * h + 256]),
-              vk, ["VX%d" % h], 256)
-        for q in range(4):
-            cp(T.VT[:, 64 * q:64 * q + 64], T.VX[:].indirect(cu[:, 32 + 4 * q:36 + 4 * q]), ["VX0", "VX1", "PM"],
-               ["VT%d" % q], 64 * GA)
+              vk + (["VD2"] if h else []), ["VX%d" % h], 256)
+        for lo, hi in CFG["VT"]:
+            cp(T.VT[:, 64 * lo:64 * hi], T.VX[:].indirect(cu[:, 32 + 4 * lo:32 + 4 * hi]), ["VX0", "VX1", "PM"],
+               ["VT%d" % q for q in range(lo, hi)], 64 * (hi - lo) * GA)
         act(T.xc[:], xb, F.Exp, [xn], ["xc"], 256, bias=-9 * LN256, scale=LN256)
         P([(ps[2][:, 0:256], Ib, T.xc[:], True, True, 256), (ps[2][:, 256:512], Ib, T.xc[:], True, True, 256)],
           ["Ib", "xc"], ["pX"], [2])
@@ -397,7 +411,6 @@ def build(g, core, T, topo, rank):
         act(T.ws[:, 0:256], T.SU[:, t:4096:16], F.Identity, ["SU"], ["ws0"], 256)
         iota(T.wv[:, 256:512], [[16, 256]], ["wv1"], 256, base=t)
         dma("Y", T.wm[:, 256:512], DG[:, t:t + 256], ["DG"], ["wm1"], 65536)
-        act(nWf, iWf, F.Identity, ["iWf"], ["nWf"], 16, bias=float(t), scale=16.0)
         P([(ps[3][:, 0:384], ONE[0:64, 0:128], CK[0:64, 0:384], True, False, 384),
            (ps[4][:, 0:400], ONE[0:64, 0:128], CK[0:64, 0:400], True, False, 400)], ["ONE", "CK"], ["K0", "K1"], [3, 4], True)
         Rw = T.R[:, 0:5120]
@@ -440,15 +453,18 @@ def build(g, core, T, topo, rank):
         cp(T.cR[:], ps[6][:, 0:256], ["uR"], ["cR"], 256, [6])
         act(T.wv[:, 0:256], ps[6][:, 0:256], F.Identity, ["uR"], ["wv0"], 256, banks=[6])
         if CFG["XU"] == "U":
-            tt(uT, hiT, loT, A.add, ["hiT", "loT"], ["uT"], 32)
-            tt(T.xu[:], uT.indirect(X1), DG[:, 0:256], A.mult, ["uT", "X1", "DG"], ["xu"], 256 * GA)
+            ts(si[:, 96:112], keyT, 4095, A.bitwise_and, ["keyT"], ["uT"], 16)
+            tt(T.xu[:], si[:, 96:112].indirect(X1), DG[:, 0:256], A.mult, ["uT", "X1", "DG"], ["xu"], 256 * GA)
             P([(ps[7][:, 8 * h:8 * h + 8], T.xu[:, 128 * h:128 * h + 128], SEL8, True, True, 256) for h in range(2)],
               ["xu", "SEL8"], ["pU"], [7])
         else:
             spread(CFG["XU"], T.xq[:], fb[:, 144:192], X3, 1.0, ["hl", "X3"], ["xq"], 256)
             P(toW(T.xq, 7, 0, 16, 32, 0, True) + toW(T.xq, 7, 0, 16, 32, 16), ["xq", "L8"], ["pU"], [7])
         cp(ul, ps[7][:, 0:16], ["pU"], ["ul"], 16, [7])
-        cp(uWf, ps[7][:, 0:16], ["pU"], ["uWf"], 16, [7])
+        if CFG["UW"] == "V":
+            cp(uWf, ps[7][:, 0:16], ["pU"], ["uWf"], 16, [7])
+        else:
+            act(uWf, ps[7][:, 0:16], F.Identity, ["pU"], ["uWf"], 16, banks=[7])
         for h in range(2):
             ts(fb[:, 112 + 8 * h:120 + 8 * h], si[:, 32 + 8 * h:40 + 8 * h], 65536.0, A.is_ge, ["keyT", "thT"], ["thrW%d" % h],
                16, cf[:, 32 + 8 * h:33 + 8 * h], A.mult)
@@ -458,7 +474,7 @@ def build(g, core, T, topo, rank):
            for k in range(8)], ["L8", "xw"], ["pY"], [0])
         act(T.wsel[:], ps[0][:, 0:128], F.Identity, ["pY"], ["wsel"], 128, banks=[0])
         zsum(T.Zb, "Zb", T.wsel, "wsel", 0, 256, "pB", range(15, -1, -1), True)
-        zcalls(T.Zc, "Zc", T.cR, "cR", uWf, "uWf")
+        zcalls(T.Zc, "Zc", T.cR, "cR", ps[7][:, 0:16], "pU", bk=[7])
         tt(nb, ps[0][:, 256:272], thT, A.is_lt, ["pB", "thT"], ["nb"], 16, [0])
         tt(thrM, nb, thrW, A.mult, ["nb", "thrW0", "thrW1"], ["thrM"], 32)
         tt(thrC, thrM, hardT, A.mult, ["thrM", "hardT"], ["thrC"], 32)
@@ -492,11 +508,17 @@ def build(g, core, T, topo, rank):
             recv(prv, "a1_%d" % u, ["m1_%d" % u], ["xb%d" % u])
         act(T.vnR[:], T.wv[:].indirect(sel), F.Identity, ["wv0", "wv1", "sel"], ["vnR"], 256 * GA)
         if u < NS:
-            ts(clW, ps[5][:, 320:336], 256.0, A.is_ge, ["pS"], ["clW"], 16, banks=[5])
-            tt(dnW, nWf, uWf, A.subtract, ["nWf", "uWf"], ["dnW"], 32)
-            tt(t1, clW, dnW, A.mult, ["clW", "dnW"], ["t1"], 32)
-            tt(vnW, t1, uWf, A.add, ["t1", "uWf"], ["vnW"], 32)
-            cp(s2[:, 256:272], vnW, ["vnW"], ["s2v%d" % u], 16)
+            if CFG["VN"] == "W":
+                act(nWf, iWf, F.Identity, ["iWf"], ["nWf"], 16, bias=float(t), scale=16.0)
+                ts(clW, ps[5][:, 320:336], 256.0, A.is_ge, ["pS"], ["clW"], 16, banks=[5])
+                tt(dnW, nWf, uWf, A.subtract, ["nWf", "uWf"], ["dnW"], 32)
+                tt(t1, clW, dnW, A.mult, ["clW", "dnW"], ["t1"], 32)
+                tt(vnW, t1, uWf, A.add, ["t1", "uWf"], ["vnW"], 32)
+                cp(s2[:, 256:272], vnW, ["vnW"], ["s2v%d" % u], 16)
+            else:
+                V(lambda: g.vector.tensor_tensor_scan(T.CT[:], T.vnR[:], T.CS[:], 8192.0, A.min, A.add),
+                  ["vnR", "CS"], ["CT"], 256)
+                ts(s2[:, 256:272], T.CT[:, 15:256:16], offp, A.add, ["CT", "offp"], ["s2v%d" % u], 16)
             if CFG["VR"] == "V":
                 cp(s2[:, 0:256], T.wv[:].indirect(sel), ["wv0", "wv1", "sel"], ["s2_%d" % u], 256 * GA)
             else:
@@ -686,6 +708,9 @@ def plan(ops):
 
     def sweep(seq, back):
         at, eng, bk = {}, {}, {}
+        if not back:
+            first = [o["i"] for o in ops if o["e"] == "Y" and not o["d"]]
+            seq = first + [i for i in seq if i not in first]
         for i in seq:
             o = ops[i]
             if back:
@@ -707,15 +732,15 @@ def plan(ops):
         return at
 
     at = {o["i"]: o["s"] for o in ops}
-    best = (max(o["end"] for o in ops), at)
+    best = (1e18, at)
     for seed in CFG["SEEDS"]:
-        key, sh = {}, {}
+        key, sh, part, big = {}, {}, "mmaz"[seed % 4], (1, 3)[seed // 4 % 2]
         for o in ops:
-            nm = o["e"] + o["w"][0].split("_")[0]
+            nm = o["e"] + o["w"][0].split("_")[0] + o["t"]
             if nm not in sh:
                 seed = (seed * 1103515245 + 12345) % 2147483648
                 z = (seed >> 8) % 1000 / 1000.0
-                sh[nm] = (z / CFG["FRAC"] - 0.5) * 2 * CFG["NOISE"] if z < CFG["FRAC"] else 0.0
+                sh[nm] = (z / CFG["FRAC"] - 0.5) * 2 * CFG["NOISE"] * big if z < CFG["FRAC"] and o["t"] == part else 0.0
             key[o["i"]] = max([best[1][o["i"]] + sh[nm]] + [key[d] + 0.01 for d in o["d"]])
         at = sweep(sorted(key, key=lambda i: (key[i], i)), False)
         for _ in range(CFG["IT"]):
@@ -738,7 +763,9 @@ def emit(g, T, ops, order):
     for o in order:
         if o["e"] == "X":
             continue
-        d = set(o["d"])
+        d = set()
+        for i in o["d"]:
+            d.update(ops[i]["d"] if "join" in ops[i] else (i,))
         for b in o["b"]:
             for e, i in bank.get(b, {}).items():
                 if e != o["e"]:

@@ -7,107 +7,100 @@ F = ActivationFunctionType
 NS = 6
 BF, F32, I32, U16 = "bfloat16", "float32", "int32", "uint16"
 
-SCRATCH = {
-    "R": ("sbuf", [128, 5376], BF), "VL": ("sbuf", [128, 1280], F32), "SU": ("sbuf", [128, 4352], F32),
-    "EF": ("sbuf", [128, 4096], BF), "veri": ("sbuf", [128, 1024], I32), "edgi": ("sbuf", [128, 1024], I32),
-    "v8i": ("sbuf", [128, 256], I32), "v8f": ("sbuf", [128, 256], F32),
-    "old": ("sbuf", [128, 4352], BF), "eq": ("sbuf", [128, 4352], BF),
-    "Zb": ("sbuf", [128, 4096], BF), "Zc": ("sbuf", [128, 4096], BF), "Zv": ("sbuf", [128, 4096], BF),
-    "wx0": ("sbuf", [128, 512], BF), "wx1": ("sbuf", [128, 512], BF),
-    "jm0": ("sbuf", [128, 256], BF), "jm1": ("sbuf", [128, 256], BF),
-    "nj0": ("sbuf", [128, 256], BF), "nj1": ("sbuf", [128, 256], BF),
-    "Q": ("sbuf", [128, 256], BF), "Qb": ("sbuf", [128, 256], BF), "Qc": ("sbuf", [128, 256], BF),
-    "G": ("sbuf", [128, 256], F32), "sc1": ("sbuf", [128, 256], F32), "sc2": ("sbuf", [128, 256], F32),
-    "VD": ("sbuf", [128, 512], F32), "VX": ("sbuf", [128, 512], F32), "VT": ("sbuf", [128, 256], U16),
-    "verK": ("sbuf", [128, 256], F32), "xc": ("sbuf", [128, 256], BF),
-    "bR": ("sbuf", [128, 256], U16), "cR": ("sbuf", [128, 256], U16),
-    "sf": ("sbuf", [128, 512], F32), "si": ("sbuf", [128, 128], I32), "su": ("sbuf", [128, 256], U16),
-    "sb": ("sbuf", [128, 64], BF), "TTs": ("sbuf", [128, 128], BF),
-    "xu": ("sbuf", [128, 256], F32), "xw": ("sbuf", [128, 128], BF), "xl": ("sbuf", [128, 128], BF),
-    "xm": ("sbuf", [128, 128], BF), "xf": ("sbuf", [128, 128], BF), "wsel": ("sbuf", [128, 128], BF),
-    "efu": ("sbuf", [128, 256], BF), "sgA": ("sbuf", [128, 256], BF), "sgB": ("sbuf", [128, 256], BF),
-    "xAB": ("sbuf", [128, 512], F32), "wv": ("sbuf", [128, 512], F32), "vnR": ("sbuf", [128, 256], F32),
-    "wc": ("sbuf", [128, 256], F32), "ws": ("sbuf", [128, 512], F32), "u2": ("sbuf", [128, 256], F32),
-    "tp": ("sbuf", [128, 256], F32), "rc": ("sbuf", [128, 256], BF), "eqc": ("sbuf", [128, 256], BF),
-    "ga": ("sbuf", [128, 256], BF), "gn": ("sbuf", [128, 256], BF),
-    "Xi": ("sbuf", [128, 512], I32), "Xa": ("sbuf", [128, 512], I32), "ok": ("sbuf", [128, 512], BF),
-    "wm": ("sbuf", [128, 512], BF), "mm": ("sbuf", [128, 256], BF), "tv": ("sbuf", [128, 256], F32),
-    "xh": ("sbuf", [128, 256], BF), "lx": ("sbuf", [128, 256], BF), "lv": ("sbuf", [128, 256], F32),
-    "y1": ("sbuf", [128, 256], F32), "y2": ("sbuf", [128, 256], F32),
-    "vR0": ("sbuf", [128, 256], U16),
-    "io_f": ("sbuf", [128, 1024], F32), "io_b": ("sbuf", [128, 1024], BF), "io_i": ("sbuf", [128, 8], I32),
-    "cf": ("sbuf", [128, 256], F32), "cI": ("sbuf", [128, 640], BF), "cI32": ("sbuf", [128, 512], F32),
-    "cW": ("sbuf", [128, 512], BF), "L8": ("sbuf", [128, 2048], BF), "DG": ("sbuf", [128, 272], BF),
-    "M2": ("sbuf", [128, 768], BF), "CK": ("sbuf", [128, 528], BF), "ONE": ("sbuf", [128, 256], BF),
-    "CS": ("sbuf", [128, 256], F32), "CT": ("sbuf", [128, 256], F32), "MS": ("sbuf", [128, 128], F32),
-    "cu": ("sbuf", [128, 64], U16), "n16": ("sbuf", [128, 256], F32), "SR": ("sbuf", [128, 256], BF),
-    "cb": ("sbuf", [128, 64], BF),
-}
-for _t in range(1, NS):
-    SCRATCH["wx%d" % _t] = ("sbuf", [128, 512], BF)
-    SCRATCH["l2_%d" % _t] = ("sbuf", [128, 272], U16)
-    SCRATCH["s1_%d" % _t] = ("sbuf", [128, 256], BF)
-    SCRATCH["s2_%d" % _t] = ("sbuf", [128, 272], U16)
-for _b in range(8):
-    SCRATCH["ps%d" % _b] = ("psum", [128, 512], F32)
-SCRATCH.update({"fb": ("sbuf", [128, 256], BF), "ja": ("sbuf", [128, 256], BF), "ea": ("sbuf", [128, 256], BF),
-                "tw": ("sbuf", [128, 256], F32), "xg": ("sbuf", [128, 256], BF), "xq": ("sbuf", [128, 256], BF)})
-SCRATCH["Ec"] = ("sbuf", [128, 512], F32)
-CFG = dict(EQC="V", TV="S", XU="U", XW="S", XL="S", XM="S", XF="S", VD="W", VR="S", ZO=1, IT=1, TP="V", JS=0,
-           VT=((0, 1), (1, 4)), UW="S", VN="R",
-           SEEDS=[i * 7919 + 3 for i in range(1200)], NOISE=600, FRAC=0.1)
-SCRATCH["xJ"] = ("sbuf", [128, 1024], BF)
-SCRATCH["QJ"] = ("sbuf", [128, 512], BF)
-SCRATCH["sv"] = ("sbuf", [128, 256], F32)
-for _t in range(NS):
-    SCRATCH["wx%d" % _t] = ("sbuf", [128, 768], BF)
-for _t in range(1, NS):
-    SCRATCH["s1_%d" % _t] = ("sbuf", [128, 512], BF)
-SCRATCH["kb"] = ("sbuf", [128, 96], BF)
+CFG = dict(EQC="X", TV="S", XU="K", XW="S", XL="S", XM="S", XF="S", XQ="S", VD="C", ZO=1, IT=1, TP="V", JS=0,
+           PARTS=((0, 4), (4, 16)), VT=((0, 4), (4, 16)), GS="G", GR="G", GRZ="S", BR="G", KT=0, TT="P", OK="V", CVT="G", DUP=1, ZC="S", EB=0, CUT=800,
+           COSTS=((0.92, 0.48, 1.4, 3.0, 4000, 500, 400, 110, 60, 1.0, 8), (0.83, 0.45, 1.1, 1.8, 4500, 700, 700, 130, 80, 1.1, 15),
+                  (1.15, 0.6, 1.9, 5.0, 3500, 500, 250, 110, 60, 0.75, 5)),
+           ROUNDS=3800, NOISE=600, FRAC=0.05, PAIR=0.85, SLACK=1500, HEAT=1000, ALL=0.5, MEAN=0.5)
+
+
+def _buffers():
+    s = {}
+    for dtype, names in (
+        (BF, dict(R=4368, EF=4096, ef0=512, old=4352, eq=4352, Zb=4096, Zc=4096, Zv=4096, QZ=4096, Q0=512, jm0=256, jm1=256,
+                  nj0=256, nj1=256, Qb=256, xc=256, TTs=128, xw=128, xl=128, xg=384, xq=256, wsel=256, efu=256,
+                  rc=256, eqc=256, ga=256, ok=512, wm=512, mm=256, xh=256, lx=256, fb=192, kb=96, xJ=1024,
+                  cI=512, cW=640, L8=1152, DG=272, M2=384, CK=656, MK=784, ONE=256, NEG=128, REP=512, SR=256, cb=64)),
+        (F32, dict(VL=1280, SU=4352, v8f=256, G=256, sc1=256, sc2=256, VD=256, sf=512, wv=512, vnR=256, ws=512, u2=256,
+                   tp=256, tv=256, tw=256, lv=256, y1=256, y2=256, io_f=768, cf=256, cI32=512, CS=256, MS=256, NUM=1024, Ec=512)),
+        (I32, dict(veri=1024, edgi=1024, v8i=256, si=128, Xi=512, Xa=512, io_i=8)),
+        (U16, dict(VT=256, bR=256, cR=256, su=256, vR0=256, cu=96)),
+    ):
+        for n, c in names.items():
+            s[n] = ("sbuf", [128, c], dtype)
+    for t in range(NS):
+        s["wx%d" % t] = ("sbuf", [128, 800], BF)
+    for t in range(1, NS):
+        s["s1_%d" % t] = ("sbuf", [128, 544], BF)
+        s["s2_%d" % t] = ("sbuf", [128, 256], U16)
+        s["l2_%d" % t] = ("sbuf", [128, 256], U16)
+    for b in range(8):
+        s["ps%d" % b] = ("psum", [128, 512], F32)
+    return s
+
+
+SCRATCH = _buffers()
 ORDER = {}
 
-NDMA = 32
+NDMA = 40
 SEMAPHORES = (["sV", "sS", "sP", "sG", "sent"] + ["d%d" % i for i in range(NDMA)]
               + ["a1_%d" % t for t in range(1, NS + 1)] + ["a2_%d" % t for t in range(1, NS + 1)])
 
-CV, CP, GA, SC, OV = 0.92, 0.5, 1.55, 3.8, 25.0
+OV = 22.0
 LN256 = math.log(256.0)
+FALL, TOP, THR, BIG = math.log(2.5), 58.0, 3.9, 2.0 ** 88
 
 
-def build(g, core, T, topo, rank):
+def build(g, core, T, topo, rank, costs):
+    CV, CP, GA, SC, FAR, CALL, RATE = costs[:7]
     N = len(T.cores)
     nxt, prv = T.cores[(rank + 1) % N], T.cores[(rank - 1) % N]
     ops = []
-    nd, phase = [0], ["a"]
+    nd, phase = [0], ["c", {}]
     ps = [T["ps%d" % b] for b in range(8)]
 
     def add(e, f, r, w, c, banks=(), **kw):
+        nm = e + "".join(x for x in w[0] if not x.isdigit())
+        phase[1][nm] = phase[1].get(nm, 0) + 1
         o = dict(e=e, f=f, r=list(r) + ([] if e == "P" else ["B%d" % b for b in banks]), w=list(w), c=c, b=tuple(banks),
-                 i=len(ops), t=phase[0])
+                 i=len(ops), nm="%s%d%s" % (nm, phase[1][nm], phase[0]))
         o.update(kw)
         ops.append(o)
 
+    def cost(n, extra):
+        return n[0] * n[1] * CV + 58 + extra if isinstance(n, tuple) else max(64, n) * CV + OV + extra
+
     def V(f, r, w, n, banks=()):
-        add("V", f, r, w, max(64, n) * CV + OV, banks)
+        add("V", f, r, w, cost(n, 0), banks)
 
     def S(f, r, w, n, banks=()):
-        add("S", f, r, w, max(64, n) * CV + 30 + OV, banks)
+        add("S", f, r, w, cost(n, 18), banks)
 
     def P(mms, r, w, banks, grp=False, given=False):
+        if CFG["CUT"] and len(mms) > 1 and sum(m[5] for m in mms) > CFG["CUT"]:
+            if not (grp or given):
+                mms = [m[:4] + (n + 1 == len(mms) or mms[n + 1][3], m[5]) for n, m in enumerate(mms)]
+            part, tot = [], 0
+            for m in mms:
+                if part and tot + m[5] > CFG["CUT"]:
+                    P(part, r, w, banks, True)
+                    part, tot = [], 0
+                part, tot = part + [m], tot + m[5]
+            return P(part, r, w, banks, True) if len(part) < len(mms) else None
+
         def f():
             for n, m in enumerate(mms):
                 stop = m[4] if grp or given else (n + 1 == len(mms) or mms[n + 1][3])
-                ins = g.tensor.matmul(m[0], m[1], m[2], m[3], stop)
+                ins = g.tensor.matmul(m[0], m[1], m[2], bool(m[3]), bool(stop))
             return ins
         bn = ["B%d" % b for b in banks]
-        add("P", f, list(r) + ([] if grp else bn), list(w) + (bn if grp else []),
-            sum(max(m[5], 32) for m in mms) * CP + 40, banks)
+        add("P", f, list(r) + ([] if grp else bn), list(w) + (bn if grp else []), sum(m[5] * CP + costs[10] for m in mms) + 10, banks)
 
     def spread(e, out, win, lst, scale, r, w, n):
         if e == "S":
-            act(out, win.indirect(lst), F.Identity, r, w, n * GA, scale=scale)
+            act(out, win.indirect(lst), F.Identity, r, w, (n, GA), scale=scale)
         else:
-            ts(out, win.indirect(lst), scale, A.mult, r, w, n * GA)
+            ts(out, win.indirect(lst), scale, A.mult, r, w, (n, GA))
 
     def ts(out, in0, s1, op0, r, w, n, s2=None, op1=None, banks=()):
         if op1 is None:
@@ -121,510 +114,567 @@ def build(g, core, T, topo, rank):
     def cp(out, a, r, w, n, banks=()):
         V(lambda: g.vector.tensor_copy(out, a), r, w, n, banks)
 
+    def fill(out, val, w, n):
+        V(lambda: g.vector.memset(out, val), [], w, n)
+
+    def scan(out, a, b, init, op0, op1, r, w, n, banks=()):
+        V(lambda: g.vector.tensor_tensor_scan(out, a, b, init, op0, op1), r, w, n, banks)
+
     def act(out, a, func, r, w, n, bias=0.0, scale=1.0, banks=()):
         S(lambda: g.scalar.activation(out, a, func, bias=bias, scale=scale), r, w, n, banks)
 
-    def iota(out, pat, w, n, cm=0, flt=True, base=0):
-        if flt:
-            add("G", lambda: g.iota(out, pat, base, cm, allow_small_or_imprecise_dtypes=True), [], w, 130 + 2 * n * CV)
+    def iota(out, pat, w, n, cm=0, base=0, r=()):
+        add("G", lambda: g.iota(out, pat, base, cm, allow_small_or_imprecise_dtypes=True), r, w, 130 + 2 * n * CV)
+
+    def select(out, a, pat, op, other, base, cm, r, w, n):
+        add("G", lambda: g.affine_select(out, a, pat, op, other, base, cm), r, w, 170 + 2 * n * CV)
+
+    def copy(e, out, a, r, w, n):
+        if e == "G":
+            select(out, a, [[0, n]], A.is_ge, 0.0, 0, 0, r, w, n)
+        elif e == "S":
+            act(out, a, F.Identity, r, w, n)
         else:
-            add("G", lambda: g.iota(out, pat, 0, cm), [], w, 130 + 2 * n * CV)
+            cp(out, a, r, w, n)
 
     def dma(q, out, in_, r, w, nbytes):
         sem = "d%d" % nd[0]
         nd[0] += 1
         eng = g.sync if q == "Y" else g.scalar
-        add(q, lambda: eng.dma_start(out, in_), r, w, 60 + nbytes / 200.0, lat=1800, sem=sem)
+        add(q, lambda: eng.dma_start(out, in_), r, w, 60 + nbytes / RATE, lat=1800, sem=sem)
 
     def send(dst, out, in_, sem, r, w):
         rid, pid, _ = topo.addr(dst)
         m = topo.mask(core, dst)
-        add("G", lambda: g.remote_dma(out, in_, T.sem[sem], T.sem.sent, pid, rid, m), r, w, 300,
+        add("G", lambda: g.remote_dma(out, in_, T.sem[sem], T.sem.sent, pid, rid, m), r, w, CALL,
             send=len(topo.engines(core, dst)))
 
     def recv(src, sem, r, w):
-        add("X", None, r, w, 2500, sem=sem, val=len(topo.engines(src, core)))
+        add("X", None, r, w, FAR, sem=sem, val=len(topo.engines(src, core)))
 
     dma("Y", T.v8i[0:8, :], T.v0[:], [], ["v8i"], 8192)
     dma("Y", T.wx0[:, 256:512], T.x0[:], [], ["xb0"], 65536)
     dma("Y", T.edgi[:], T.edge0[:], [], ["edgi"], 524288)
     dma("Y", T.veri[:], T.ver0[:], [], ["veri"], 524288)
     dma("Y", T.R[:, 0:4096], T.rec0[:], [], ["R"], 1048576)
-    dma("Y", T.EF[:, 0:512], T.eff[:], [], ["EF0"], 131072)
+    dma("Y", T.ef0[:], T.eff[:], [], ["ef0"], 131072)
 
-    io, ib, cf = T.io_f, T.io_b, T.cf
+    io, cf, cb, ii = T.io_f, T.cf, T.cb, T.io_i
     col = lambda j: cf[:, j:j + 1]
-    partf, pf, gf, wt, wl, wh, offp, bW_, bT_, bV_, x2s, pms, nwl, nwh, p4, tmpc = [col(j) for j in range(16)]
-    iota(T.io_i[:, 0:1], [[0, 1]], ["ii0"], 1, cm=1, flt=False)
-    F128, CG, DI, CH, HI, C16, H16 = (io[:, 0:128], io[:, 128:256], io[:, 256:528], io[:, 528:656], io[:, 656:784],
-                                      io[:, 784:912], io[:, 912:928])
+    partf, pf, gf, p7, wl, wh, offp, wt, bT_, bV_, x2s, nwt, nwl, nwh, p4, pf1 = [col(j) for j in range(16)]
+    cm_, p32 = col(128), cb[:, 2:3]
+    add("G", lambda: g.iota(ii[:, 0:1], [[0, 1]], 0, 1), [], ["ii0"], 132)
+    F128, CG, DI, HI, C16, H16 = (io[:, 0:128], io[:, 128:256], io[:, 256:528], io[:, 528:544], io[:, 544:672],
+                                  io[:, 672:688])
     iota(F128, [[1, 128]], ["F128"], 128)
     iota(CG, [[1, 8], [0, 16]], ["CG"], 128)
     iota(DI, [[0, 17], [1, 16]], ["DI"], 272)
-    iota(CH, [[0, 16], [1, 8]], ["CH"], 128)
-    iota(io[:, 656:672], [[1, 8], [16, 2]], ["HI"], 16)
-    iota(C16, [[1, 16], [0, 8]], ["C16"], 128)
-    iota(H16, [[1, 2], [0, 8]], ["H16"], 16)
-    iota(ib[:], [[-16, 8], [16, 8], [1, 16]], ["ib"], 1024)
-    ii = T.io_i
+    iota(HI, [[1, 8], [16, 2]], ["HI"], 16, base=16)
+    iota(C16, [[0, 2], [1, 8], [0, 8]], ["C16"], 128)
+    H3 = io[:, 672:696]
+    iota(H3, [[1, 8], [16, 3]], ["H3"], 24, base=16)
     ts(ii[:, 1:2], ii[:, 0:1], 15, A.bitwise_and, ["ii0"], ["ii1"], 1)
     ts(ii[:, 2:3], ii[:, 0:1], 4, A.arith_shift_right, ["ii0"], ["ii2"], 1)
-    ts(ii[:, 3:4], ii[:, 0:1], 17, A.bitwise_and, ["ii0"], ["ii3"], 1)
-    ts(ii[:, 4:5], ii[:, 0:1], 7, A.bitwise_and, ["ii0"], ["ii4"], 1)
-    cp(cf[:, 0:3], ii[:, 0:3], ["ii0", "ii1", "ii2"], ["pg"], 3)
-    c17, p7, ca, cb_, cm_, cn, co = [col(j) for j in range(128, 135)]
-    cp(cf[:, 128:130], ii[:, 3:5], ["ii3", "ii4"], ["c17"], 2)
-    ts(ca, c17, 0.0, A.is_gt, ["c17"], ["ca"], 1)
-    ts(tmpc, c17, 17.0, A.is_lt, ["c17", "ca"], ["tmpc"], 1, ca, A.mult)
-    ts(cb_, pf, 0.0, A.is_equal, ["pg"], ["cb_"], 1, 256.0, A.mult)
-    ts(cb_, cb_, 240.0, A.add, ["cb_", "tmpc"], ["cb_"], 1, tmpc, A.mult)
-    ts(cm_, p7, gf, A.is_equal, ["c17", "pg"], ["cm_"], 1)
-    ts(wt, pf, 2.0, A.mult, ["pg"], ["wt"], 1, 1.0, A.add)
-    ts(offp, pf, 0.0, A.is_equal, ["pg"], ["offp0"], 1, -16384.0, A.mult)
-    ts(offp, offp, 8192.0, A.add, ["offp0"], ["offp"], 1)
-    ts(bW_, partf, -0.55, A.mult, ["pg"], ["bW_"], 1, 70.0, A.add)
-    ts(bT_, partf, -0.55, A.mult, ["pg"], ["bT_"], 1, 70.0 + math.log(2.55), A.add)
-    ts(bV_, pf, -0.55, A.mult, ["pg"], ["bV_"], 1, 70.0, A.add)
+    ts(ii[:, 3:4], ii[:, 0:1], 7, A.bitwise_and, ["ii0"], ["ii3"], 1)
+    ts(ii[:, 4:5], ii[:, 0:1], 31, A.bitwise_and, ["ii0"], ["ii4"], 1)
+    cp(cf[:, 0:4], ii[:, 0:4], ["ii0", "ii1", "ii2", "ii3"], ["pg"], 4)
+    cp(p32, ii[:, 4:5], ["ii4"], ["p32"], 1)
+    ts(cm_, p7, gf, A.is_equal, ["pg"], ["cm_"], 1)
+    for ap, nm, src, sc_, bi in ((wt, "wt", pf, 2.0, 1.0), (nwt, "nwt", pf, -2.0, -1.0), (pf1, "pf1", pf, 1.0, 1.0),
+                                 (bT_, "bT_", partf, -FALL, TOP + math.log(THR)), (bV_, "bV_", pf, -FALL, TOP + math.log(1.5))):
+        act(ap, src, F.Identity, ["pg"], [nm], 1, bias=bi, scale=sc_)
+    ts(offp, pf, 0.0, A.is_equal, ["pg"], ["offp0"], 1, -65536.0, A.mult)
+    act(offp, offp, F.Identity, ["offp0"], ["offp"], 1, bias=32768.0)
     ts(x2s, pf, 8.0, A.is_ge, ["pg"], ["x2s"], 1, 8.0, A.mult)
-    ts(pms, pf, 16.0, A.mult, ["pg", "cb_"], ["pms"], 1, cb_, A.add)
-    cb = T.cb
     act(cb[:, 0:1], pf, F.Exp, ["pg"], ["p4b"], 1, scale=math.log(4.0))
-    cp(p4, cb[:, 0:1], ["p4b"], ["p4"], 1)
+    act(p4, cb[:, 0:1], F.Identity, ["p4b"], ["p4"], 1)
     ts(wl, pf, 8.0, A.is_lt, ["pg", "p4"], ["wl"], 1, p4, A.mult)
     ts(wh, x2s, p4, A.mult, ["x2s", "p4"], ["wh"], 1, 2.0 ** -19, A.mult)
-    ts(cf[:, 12:14], cf[:, 4:6], -1.0, A.mult, ["wl", "wh"], ["nw"], 2)
-    cI = T.cI
-    Ib, In, I16, Im2, I8k = [cI[:, 128 * j:128 * j + 128] for j in range(5)]
+    act(cf[:, 12:14], cf[:, 4:6], F.Identity, ["wl", "wh"], ["nw"], 2, scale=-1.0)
+    Ib, In, I16, I8k = [T.cI[:, 128 * j:128 * j + 128] for j in range(4)]
     If, Ifn, BO, SB = [T.cI32[:, 128 * j:128 * j + 128] for j in range(4)]
     In8 = T.L8[:, 1024:1152]
     ts(If, F128, partf, A.is_equal, ["F128", "pg"], ["If"], 128)
-    for ap, nm, val in ((Ib, "Ib", 1.0), (In, "In", -1.0), (I16, "I16", 16.0), (Im2, "Im2", -2.0), (I8k, "I8k", 8192.0),
-                        (In8, "In8", -8192.0)):
+    for ap, nm, val in ((Ib, "Ib", 1.0), (In, "In", -1.0), (I16, "I16", -16.0), (I8k, "I8k", 8192.0), (In8, "In8", -8192.0)):
         act(ap, If, F.Identity, ["If"], [nm], 128, scale=val)
-    if CFG["TV"] == "V":
+    if CFG["TV"] == "V" or CFG["TP"] == "D":
         act(Ifn, If, F.Identity, ["If"], ["Ifn"], 128, scale=-1.0)
+    ONE, NEG, MK, CK = T.ONE, T.NEG, T.MK, T.CK
+    ON32, NE32 = ONE[0:32, 0:128], NEG[0:32, :]
+    MJ, M4, H64, M2p = MK[0:32, 0:256], MK[0:32, 256:512], MK[0:32, 512:768], MK[0:32, 768:784]
+    fill(ONE[:], 1.0, ["ONE"], 128)
+    fill(NEG[:], -1.0, ["NEG"], 64)
+    fill(MJ, 1.5 * 2 ** 22, ["MJ"], 128)
+    fill(H64, 1 / 64, ["H64"], 128)
+    iota(M4, [[0, 256]], ["M4"], 256, base=3 * 2 ** 19)
+    iota(M2p, [[0, 16]], ["M2p"], 16, base=3 * 2 ** 18)
+    KC, K17, EC, JC = CK[0:32, 0:256], CK[0:32, 256:272], CK[0:2, 272:528], CK[0:32, 528:656]
+    iota(KC, [[0, 16], [128, 16]], ["KC"], 256)
+    iota(K17, [[0, 16]], ["K17"], 16, base=31 * 2 ** 16)
+    iota(EC, [[0, 256]], ["EC"], 256, base=85, cm=21760 - 85)
+    iota(JC, [[0, 8], [-2, 16]], ["JC"], 128, base=-15)
+    iota(T.Q0[:], [[1, 32], [0, 16]], ["Q00", "Q01"], 512)
+    ts(T.REP[:], T.Q0[:], p32, A.is_equal, ["Q00", "Q01", "p32"], ["REP"], 256)
+    iota(T.QZ[:, 0:512], [[0, 512]], ["QZa"], 512)
+    dma("Y", T.QZ[:, 512:1024], T.QZ[:, 0:512], ["QZa"], ["QZb"], 131072)
+    for k in range(1, 4):
+        dma("Y", T.QZ[:, 1024 * k:1024 * k + 1024], T.QZ[:, 0:1024], ["QZa", "QZb"], ["QZc%d" % k], 262144)
+    add("X", None, ["QZa", "QZb", "QZc1", "QZc2", "QZc3"], ["QZ"], 1, join=True)
     ts(BO, CG, gf, A.is_equal, ["CG", "pg"], ["BO"], 128)
     ts(SB, CG, partf, A.is_equal, ["CG", "pg"], ["SB"], 128)
     cW = T.cW
-    WT, WEC, WKE, WK17 = cW[:, 0:128], cW[:, 128:384], cW[:, 384:408], cW[:, 408:416]
+    WT, WEC, WK17, NS8, WTn = cW[:, 0:128], cW[:, 128:384], cW[:, 408:416], cW[:, 416:424], cW[:, 512:640]
     act(WT, BO, F.Identity, ["BO", "wt"], ["WT"], 128, scale=wt)
+    act(WTn, BO, F.Identity, ["BO", "nwt"], ["WTn"], 128, scale=nwt)
     act(cW[:, 128:256], BO, F.Identity, ["BO", "wl"], ["WEC0"], 128, scale=wl)
     act(cW[:, 256:384], BO, F.Identity, ["BO", "wh"], ["WEC1"], 128, scale=wh)
-    F8 = io[:, 0:8]
-    SEL8, thT, iWf, DW, thrA = cf[:, 16:24], cf[:, 32:48], cf[:, 48:64], cf[:, 64:112], cf[:, 112:128]
-    ts(SEL8, F8, gf, A.is_equal, ["F128", "pg"], ["SEL8"], 8)
-    act(cW[:, 384:392], SEL8, F.Identity, ["SEL8"], ["WKE0"], 8, scale=-65536.0)
-    act(cW[:, 392:400], SEL8, F.Identity, ["SEL8", "nw"], ["WKE1"], 8, scale=nwl)
-    act(cW[:, 400:408], SEL8, F.Identity, ["SEL8", "nw"], ["WKE2"], 8, scale=nwh)
-    act(WK17, SEL8, F.Identity, ["SEL8"], ["WK17"], 8, scale=-2.0 ** 21)
-    act(thT, H16, F.Exp, ["H16", "bT_"], ["thT"], 16, bias=bT_, scale=-0.55 * 128)
+    SEL8, thT, iWf, thrA = cf[:, 16:24], cf[:, 32:48], cf[:, 48:64], cf[:, 112:128]
+    nHL = cf[:, 144:176]
+    act(SEL8, T.cI32[:, 256:384:16], F.Identity, ["BO"], ["SEL8"], 8)
+    for ap, nm, val, vn in ((cW[:, 384:392], "WKE0", -65536.0, []), (cW[:, 392:400], "WKE1", nwl, ["nw"]),
+                            (cW[:, 400:408], "WKE2", nwh, ["nw"]), (WK17, "WK17", -2.0 ** 22, []), (NS8, "NS8", -1.0, [])):
+        act(ap, SEL8, F.Identity, ["SEL8"] + vn, [nm], 8, scale=val)
+    thr = col(32)
+    act(thr, bT_, F.Exp, ["bT_"], ["thr"], 1)
     act(iWf, io[:, 0:16], F.Identity, ["F128", "pg"], ["iWf"], 16, bias=pf, scale=16.0)
-    iWb = cb[:, 16:32]
-    act(iWb, iWf, F.Identity, ["iWf"], ["iWb"], 16)
-    for j, base in enumerate((5120.0, 1024.0, 4096.0)):
-        act(cf[:, 64 + 16 * j:80 + 16 * j], iWf, F.Identity, ["iWf"], ["DW%d" % j], 16, bias=base)
-    iota(thrA, [[0, 16]], ["thrA"], 16, base=4 * 65536)
-    L8 = T.L8[:, 0:1024]
-    ts(L8, ib[:], pf, A.is_equal, ["ib", "pg"], ["L8"], 512)
+    iWb, zer = cb[:, 16:32], cb[:, 32:48]
+    act(iWb, iWf, F.Identity, ["iWf"], ["iWb"], 16, scale=32.0)
+    act(nHL[:, 0:16] if False else cf[:, 144:160], iWf, F.Identity, ["iWf"], ["nH"], 16, scale=16.0)
+    for j, base in enumerate((4112.0 - 8192, 1024.0 - 8192, 4096.0)):
+        act(cf[:, 64 + 16 * j:80 + 16 * j], iWf, F.Identity, ["iWf"], ["DW%d" % j], 16, bias=base + (8192 if j < 2 else 0))
+    KD = 65536.0 - 2.0 ** 20
+    iota(thrA, [[0, 16]], ["thrA"], 16, base=4 * 65536 - 2 ** 20)
     DG = T.DG
     ts(DG[:], DI, pf, A.is_equal, ["DI", "pg"], ["DG"], 272)
-    M2 = T.M2
-    M2o, M2w, M2c, M2n, WSV, M2t = [M2[:, 128 * j:128 * j + 128] for j in range(6)]
-    ts(M2o, CH, gf, A.is_equal, ["CH", "pg"], ["M2o"], 128)
-    act(M2t, C16, F.Exp, ["C16", "bV_"], ["M2t"], 128, bias=bV_, scale=-0.55 * 16)
-    tt(WSV, M2t, M2o, A.mult, ["M2t", "M2o"], ["WSV"], 256)
-    CK, ONE = T.CK, T.ONE
-    V(lambda: g.vector.memset(ONE[:], 1.0), [], ["ONE"], 128)
-    V(lambda: g.vector.memset(CK[0:64, :], 0.0), [], ["CK"], 264)
-    for (lo, hi, v0, v1) in ((0, 128, 2.0 ** 20, None), (128, 384, 21760.0, 85.0), (384, 400, 2.0 ** 25, -4096.0),
-                             (400, 528, 3072.0, None)):
-        V(lambda lo=lo, hi=hi, v0=v0: g.vector.memset(CK[0:1, lo:hi], v0), ["CK"], ["CK"], 64)
-        if v1 is not None:
-            V(lambda lo=lo, hi=hi, v1=v1: g.vector.memset(CK[32:33, lo:hi], v1), ["CK"], ["CK"], 64)
-    ts(CK[32:33, 0:128], io[32:33, 256:384], 4096.0, A.mult, ["DI", "CK"], ["CK"], 128)
-    ts(CK[32:33, 400:528], io[32:33, 256:384], -1.0, A.mult, ["DI", "CK"], ["CK"], 128)
+    for k in range(2):
+        dma("Y", T.L8[:, 512 * k:512 * k + 512], T.QZ[:, 0:512], ["QZa"], ["L8z%d" % k], 131072)
+    for k in range(8):
+        copy("G", T.L8[:, 144 * k:144 * k + 16], DG[:, 0:16], ["DG", "L8", "L8z0", "L8z1"], ["L8"], 16)
+    WSV, M2t = T.M2[:, 0:192], T.M2[:, 192:384]
+    act(T.M2[:, 192:320], C16, F.Exp, ["C16", "bV_"], ["M2t"], 128, bias=bV_, scale=-FALL * 16)
+    act(T.M2[:, 320:384], ONE[:, 0:64], F.Identity, ["ONE"], ["M2u"], 64, scale=BIG)
+    select(WSV, M2t, [[0, 24], [-16, 8]], A.is_ge, 0.0, 0, 1, ["M2t", "M2u"], ["WSV"], 192)
+    select(WSV, WSV, [[0, 24], [16, 8]], A.is_ge, 0.0, 15, -1, ["WSV"], ["WSV"], 192)
     P([(ps[0][:, 256:512], In8, DG[:, 0:256], True, False, 256), (ps[0][:, 256:512], I8k, DG[:, 1:257], False, False, 256),
        (ps[0][:, 256:512], I8k, DG[:, 1:257], False, True, 256)], ["In8", "I8k", "DG"], ["pB"], [0])
-    act(T.CS[:], ps[0][:, 256:512], F.Identity, ["pB"], ["CS"], 256, banks=[0])
-    ts(T.MS[:], io[:, 256:384], 0.0, A.is_equal, ["DI"], ["MS"], 128, 2.0 ** 23, A.mult)
+    act(T.CS[:], ps[0][:, 256:512], F.Identity, ["pB"], ["CS"], 256, scale=4.0, banks=[0])
+    iota(T.MS[:], [[0, 256]], ["MS"], 256)
+    iota(T.MS[:, 0:256:16], [[0, 16]], ["MS"], 16, base=2 ** 23)
+    if CFG["BR"] == "G":
+        iota(T.NUM[:], [[1, 1024]], ["NUM"], 1024)
     cu = T.cu
-    X1, X2, PM, X3 = cu[:, 0:16], cu[:, 16:24], cu[:, 32:48], cu[:, 48:64]
-    cp(X1, io[:, 0:16], ["F128"], ["X1"], 16)
-    for lst, nm, src, srcn, zc, tc in ((X2, "X2", F8, "F128", 16.0, cn), (X3, "X3", io[:, 656:672], "HI", 32.0, co)):
-        ts(tc, x2s, -zc, A.add, ["x2s", "cm_"], [nm + "c"], 1, cm_, A.mult)
-        ts(tc, tc, zc, A.add, [nm + "c"], [nm + "c"], 1)
-        ts(lst, src, cm_, A.mult, [srcn, "cm_", nm + "c"], [nm], 16, tc, A.add)
-    V(lambda: g.vector.memset(T.fb[:], 0.0), [], ["clT", "nmT", "ngT", "nfT", "thrW0", "thrW1", "hl"], 128)
-    ts(PM, io[:, 0:16], pms, A.add, ["F128", "pms"], ["PM"], 16)
+    X2, X3, ID = cu[:, 16:24], cu[:, 48:64], cu[:, 64:96]
+    ts(X2, io[:, 16:24], x2s, A.add, ["F128", "x2s", "cm_"], ["X2"], 8, cm_, A.mult)
+    ts(X3, HI, x2s, A.add, ["HI", "x2s", "cm_"], ["X3"], 16, cm_, A.mult)
+    if CFG["OK"] == "S":
+        ts(ID, io[:, 0:32], 16.0, A.mult, ["F128", "pg"], ["ID"], 32, pf, A.add)
+    X4 = cu[:, 24:48]
+    ts(X4, H3, x2s, A.add, ["H3", "x2s", "cm_"], ["X4"], 24, cm_, A.mult)
+    iota(T.fb[:], [[0, 192]], ["clT", "nmT", "ngT", "nfT", "thrW", "hl"], 192)
+    iota(zer, [[0, 16]], ["zer"], 16)
     for h in range(2):
-        ts(T.SR[0:32, 128 * h:128 * h + 128], io[0:32, 128:256], float(8 * h), A.add, ["CG", "pg"], ["SR%d" % h], 128,
-           cf[0:32, 1:2], A.is_equal)
-    iota(T.R[:, 4096:5120], [[0, 1024]], ["R5"], 1024, base=5)
-    cp(T.SU[:, 0:1024], T.edgi[:], ["edgi"], ["SU0"], 1024)
-    dma("Y", T.SU[:, 1024:2048], T.SU[:, 0:1024], ["SU0"], ["SU1"], 524288)
-    dma("Y", T.SU[:, 2048:3072], T.SU[:, 0:1024], ["SU0"], ["SU2"], 524288)
-    act(T.SU[:, 3072:4096], T.SU[:, 0:1024], F.Identity, ["SU0"], ["SU3"], 1024)
+        ts(T.SR[:, 128 * h:128 * h + 128], CG, float(8 * h), A.add, ["CG", "pg"], ["SR%d" % h], 128, pf, A.is_equal)
+    iota(T.R[:, 4096:4112], [[0, 16]], ["R5"], 16, base=5)
+    copy(CFG["CVT"], T.SU[:, 0:1024], T.edgi[:], ["edgi"], ["SU0"], 1024)
+    for k in range(1, 4):
+        dma("Y", T.SU[:, 1024 * k:1024 * k + 1024], T.SU[:, 0:1024], ["SU0"], ["SU%d" % k], 524288)
     add("X", None, ["SU0", "SU1", "SU2", "SU3"], ["SU"], 1, join=True)
-    cp(T.VL[:, 0:1024], T.veri[:], ["veri"], ["VL"], 1024)
-    act(T.EF[:, 512:1024], T.EF[:, 0:512], F.Identity, ["EF0"], ["EF1"], 512)
+    copy(CFG["CVT"], T.VL[:, 0:1024], T.veri[:], ["veri"], ["VL"], 1024)
+    act(T.EF[:, 0:512], T.ef0[:], F.Identity, ["ef0"], ["EF0"], 512, bias=-1.5)
+    dma("Y", T.EF[:, 512:1024], T.EF[:, 0:512], ["EF0"], ["EF1"], 131072)
     for k in range(1, 4):
         dma("Y", T.EF[:, 1024 * k:1024 * k + 1024], T.EF[:, 0:1024], ["EF0", "EF1"], ["EF%d" % (k + 1)], 262144)
     add("X", None, ["EF0", "EF1", "EF2", "EF3", "EF4"], ["EF"], 1, join=True)
 
-    sf, si, su, sb = T.sf, T.si, T.su, T.sb
+    sf, si, su, fb = T.sf, T.si, T.su, T.fb
     f16 = lambda j: sf[:, 16 * j:16 * j + 16]
-    (bWf, vWf, uT, wantT, hardT, uWf, nb, thrW, thrM, thrC, clT, nmT, nfT, clW, dnW, t1, vnW, nWf, lf, _a, lfF) = \
-        [f16(j) for j in range(21)]
-    lfGM = sf[:, 288:320]
-    A256, parc = sf[:, 352:353], sf[:, 353:354]
+    bWf, vWf, hardT, nb, thrM, thrC, clW, lfF = [f16(j) for j in range(8)]
+    lfGM, dn, tn = sf[:, 224:272], sf[:, 160:192], sf[:, 192:224]
     wWi, bWi, keyT, hiT, loT, vWi = [si[:, 16 * j:16 * j + 16] for j in range(6)]
-    bl, wl_, bl1, ul, sel, lG, lM, lF, vl0, vm0 = (su[:, 0:32], su[:, 32:48], su[:, 48:64], su[:, 64:80], su[:, 80:96],
-                                                   su[:, 96:112], su[:, 112:128], su[:, 128:144], su[:, 144:160],
-                                                   su[:, 160:176])
-    fb = T.fb
-    clT, ngT, nmT, nfT, thrW, hl = fb[:, 0:16], fb[:, 32:48], fb[:, 48:64], fb[:, 80:96], fb[:, 112:128], fb[:, 144:176]
-    Q2, par2 = sb[:, 0:16], f16(23)
+    wl_, ul, sel, lG, lM, lF, vm0 = [su[:, 16 * j:16 * j + 16] for j in (2, 4, 5, 6, 7, 8, 10)]
+    clT, ngT, nmT, nfT, thrW, hl = fb[:, 16:32], fb[:, 48:64], fb[:, 64:80], fb[:, 80:96], fb[:, 128:144], fb[:, 160:192]
+    alias = {5: ["TT", "Sc", "pS", "pG"], 6: ["uR"]}
 
     cp(T.v8f[0:8, :], T.v8i[0:8, :], ["v8i"], ["v8f"], 256)
     P([(ps[1][:, 0:256], T.cI32[0:8, 384:512], T.v8f[0:8, :], True, True, 1024)], ["SB", "v8f"], ["wR"], [1])
-    V(lambda: g.vector.tensor_tensor_scan(T.sc1[:], ps[1][:, 0:256], T.CS[:], 8192.0, A.min, A.add),
-      ["wR", "CS"], ["sc1"], 256, [1])
+    scan(T.sc2[:], ps[1][:, 0:256], T.CS[:], 32768.0, A.min, A.add, ["wR", "CS"], ["sc20", "sc21"], 256, [1])
     cp(T.vR0[:], ps[1][:, 0:256], ["wR"], ["vR_0"], 256, [1])
-    ts(vWi, T.sc1[:, 15:256:16], offp, A.add, ["sc1", "offp"], ["vWi"], 16)
-    cp(vl0, vWi, ["vWi"], ["vW_0"], 16)
-    ts(vWi, vWi, 1023, A.bitwise_and, ["vWi"], ["vWi"], 16)
-    cp(vm0, vWi, ["vWi"], ["vm0"], 16)
+    ts(vWi, T.sc2[:, 15:256:16], offp, A.add, ["sc20", "sc21", "offp"], ["vWi"], 16)
+    cp(su[:, 176:192], vWi, ["vWi"], ["vW0"], 16)
+    cp(vWf, vWi, ["vWi"], ["vWf"], 16)
+    ts(hiT, vWi, 1023, A.bitwise_and, ["vWi"], ["hiT"], 16)
+    cp(vm0, hiT, ["hiT"], ["vm0"], 16)
 
     def zstart(c):
         q = c % 8
         return 128 * (c // 8) + (0 if q < 4 else 64 if q < 6 else 96)
 
-    def zcalls(Z, nm, keyR, keyRn, keyW, keyWn, more=(), bk=()):
-        o = {"Zb": 0, "Zc": 32, "Zv": 64}[nm]
-        act(T.kb[:, o:o + 16], keyW, F.Identity, [keyWn], [nm + "h"], 16, banks=bk)
-        tt(T.kb[:, o + 16:o + 32], keyW, T.kb[:, o:o + 16], A.subtract, [keyWn, nm + "h"], [nm + "l"], 32, bk)
+    def split(kb, keyW, keyWn, nm):
+        act(kb[0], keyW, F.Identity, [keyWn], [nm + "h"], 16)
+        tt(kb[1], keyW, kb[0], A.subtract, [keyWn, nm + "h"], [nm + "l"], 32)
+
+    def zcalls(Z, nm, keyR, keyRn, buf, o, kn, more=()):
         for c in range(16):
             s = zstart(c)
-            ts(Z[:, 256 * c + s:256 * c + 256], keyR[:, s:256], T.kb[:, o + c:o + c + 1], A.subtract,
-               [keyRn, nm + "h", nm + "l"] + list(more), ["%s%d" % (nm, c)], (256 - s) // 2,
-               T.kb[:, o + 16 + c:o + 17 + c], A.is_equal)
+            ts(Z[:, 256 * c + s:256 * c + 256], keyR[:, s:256], buf[:, o + c:o + c + 1], A.subtract,
+               [keyRn] + kn + list(more), ["%s%d" % (nm, c)], (256 - s) // 2, buf[:, o + 16 + c:o + 17 + c], A.is_equal)
 
-    def zsum(Z, nm, wsel, wn, bk, o, on, cs, first, grp=False):
+    def zsum(Z, nm, wsel, wn, bk, o, on, cs, first, last, grp=False):
         mms = []
         if first:
-            mms.append((ps[bk][:, o:o + 16], T.ONE[32:64, 0:128], T.cb[32:64, 32:48], True, False, 64))
+            mms.append((ps[bk][:, o:o + 16], ONE[32:64, 0:128], cb[32:64, 32:48], True, False, 64))
         for c in cs:
             s = zstart(c)
             for h in range(c // 8, 2):
                 lo = max(s, 128 * h)
-                mms.append((ps[bk][lo - 128 * h:128, o + 8 * h:o + 8 * h + 8],
-                            Z[:, 256 * c + lo:256 * c + 128 * h + 128], wsel[:, 8 * c:8 * c + 8], False, c == 0 and h == 1, 64))
-        P(mms, ["%s%d" % (nm, c) for c in cs] + [wn, "ONE", "zer"], [on], [bk], grp, True)
-
-    V(lambda: g.vector.memset(T.cb[:, 32:48], 0.0), [], ["zer"], 16)
+                at = 8 * c + (128 if h > c // 8 else 0)
+                mms.append((ps[bk][lo - 128 * h:128, o + 8 * h:o + 8 * h + 8], Z[:, 256 * c + lo:256 * c + 128 * h + 128],
+                            wsel[:, at:at + 8], False, last and c == 0 and h == 1, min(64, 128 * h + 128 - lo)))
+        P(mms, ["%s%d" % (nm, c) for c in cs] + wn + ["ONE", "zer"], [on], [bk], grp, True)
 
     def toW(xp, bk, o, n=16, st=16, at=0, first=False):
         return [(ps[bk][:, o:o + n], T.L8[:, 128 * k:128 * k + 128], xp[:, st * k + at:st * k + at + n], first and k == 0,
                  False, 64) for k in range(8)]
 
+    def addkey(bk, o, buf, at, first=False):
+        return [(ps[bk][:, o:o + 16], Ib, buf[:, at + 16 * k:at + 16 * k + 16], first and k == 0, False, 64) for k in range(2)]
+
     for t in range(NS):
-        par = t % 2
+        par, u = t % 2, t + 1
         phase[0] = "a" if t == 0 else "z" if t == NS - 1 else "m"
+        phase[1] = {}
         wx = T["wx%d" % t]
         xb, xn = wx[:, 256:512], "xb%d" % t
-        jm, nj, jn, njn = T["jm%d" % par], T["nj%d" % par], "jm%d" % par, "nj%d" % par
+        jb, nj, jn, njn = T["jm%d" % par], T["nj%d" % par], "jm%d" % par, "nj%d" % par
+        vW, vWn = su[:, 176 + 16 * par:192 + 16 * par], "vW%d" % par
         if t == 0:
-            vW, vR, vWn, vRn = vl0, T.vR0, "vW_0", "vR_0"
+            vR, vRn, vkb, vo, vkn = T.vR0, "vR_0", T.kb, 64, ["Zvh", "Zvl"]
+            split((T.kb[:, 64:80], T.kb[:, 80:96]), vWf, "vWf", "Zv")
         else:
-            vW, vR, vWn, vRn = T["l2_%d" % t][:, 256:272], T["l2_%d" % t], "vR_%d" % t, "vR_%d" % t
-        def jmask(out, on, x, xname, Q, Qn):
-            P([(ps[0][:, 0:256], CK[0:64, 400:528], ONE[0:64, :], True, False, 256),
-               (ps[0][:, 0:256], WT, x, False, True, 256)], ["CK", "ONE", "WT", xname], ["pY"], [0])
-            act(Q, ps[0][:, 0:256], F.Identity, ["pY"], [Qn], 256, banks=[0])
-            tt(out, ps[0][:, 0:256], Q, A.is_equal, ["pY", Qn], [on], 256, [0])
-        if CFG["JS"] and t:
-            jm, jn = wx[:, 512:768], xn
-        else:
-            jm = jm[:]
-            jmask(jm, jn, xb, xn, T.Q[:], "Q")
+            vR, vRn, vkb, vo, vkn = T["l2_%d" % t], "vR_%d" % t, wx, 512, [xn]
+            P(addkey(7, 32, wx, 512, True), ["Ib", xn], ["pV"], [7])
+            cp(vW, ps[7][:, 32:48], ["pV"], [vWn], 16, [7])
+
+        def jmask(out, on, xbuf, xo, xname, lo=0, hi=256, bk=0, at=0, pn="pY"):
+            o, x, n = ps[bk][:, at:at + hi - lo], xbuf[:, xo + lo:xo + hi], hi - lo
+            P([(o, JC, MK[0:32, 512:512 + n], True, False, n), (o, WT, x, False, False, n),
+               (o, ON32, MK[0:32, 0:n], False, False, n), (o, NE32, MK[0:32, 0:n], False, False, n), (o, WTn, x, False, True, n)],
+              ["JC", "H64", "ONE", "NEG", "WT", "WTn", "MJ", xname], [pn], [bk])
+            act(out, o, F.Relu, [pn, "pf1"], [on], n, bias=pf1, banks=[bk])
+
+        def nextx(o, on, bk, ef, efn, out, outn):
+            P([(o, In, xb, True, False, 256), (o, In, ef, False, False, 256), (o, ON32, M4, False, False, 256),
+               (o, NE32, M4, False, False, 256), (o, Ib, xb, False, False, 256), (o, Ib, ef, False, True, 256)],
+              ["Ib", "In", "ONE", "NEG", "M4", efn, xn], [on], [bk])
+            act(out, o, F.Identity, [on], [outn], 256, bias=1.5, banks=[bk])
+
+        js = CFG["JS"] and t
+        jbuf, jo = (wx, 544) if js else (jb, 0)
+        jm = jbuf[:, jo:jo + 256]
+        parts = CFG["PARTS"]
+        pn = lambda s: [s + str(k) for k in range(len(parts))]
+        jns = [xn] if js else pn(jn)
+        VLw, VLn = (T.VL[:, 0:1024], "VL") if t else (T.veri[:], "veri")
+        for k, (a, b) in enumerate(parts):
+            lo, hi, n = 16 * a, 16 * b, 16 * (b - a)
+            head = k + 1 < len(parts)
+            if not js:
+                jmask(jb[:, lo:hi], jns[k], wx, 256, xn, lo, hi, *((3, 400, "pJ") if head else (0, lo, "pY")))
+            src, lst, rn = ((T.SU[:, 0:4096], su[:, 176 + 16 * par + a:176 + 16 * par + b], ["SU", vWn]) if t
+                            else (T.edgi[:], su[:, 160 + a:160 + b], ["edgi", "vm0"]))
+            tt(T.G[:, lo:hi], src.indirect(lst), jbuf[:, jo + lo:jo + hi], A.mult, rn + [jns[k % len(jns)]], ["G%d" % k], (n, GA))
+            bk, wn = (4, "K1") if head else (1, "wR")
+            P([(ps[bk][:, lo:hi], BO, T.G[:, lo:hi], True, True, 4 * n)], ["BO", "G%d" % k], [wn], [bk])
+            scan(T.sc1[:, lo:hi], ps[bk][:, lo:hi], T.CS[:, lo:hi], 32768.0, A.min, A.add, [wn, "CS"], ["sc1%d" % k], n, [bk])
+            ts(si[:, a:b], T.sc1[:, lo + 15:hi:16], offp, A.add, ["sc1%d" % k, "offp"], ["wWi%d" % k], 16)
+            ts(si[:, 16 + a:16 + b], si[:, a:b], 1023, A.bitwise_and, ["wWi%d" % k], ["bWi%d" % k], 16)
+            cp(su[:, a:b], si[:, 16 + a:16 + b], ["bWi%d" % k], ["bla%d" % k], 16)
+            if CFG["BR"] != "G":
+                act(T.Qb[:, lo:hi], ps[bk][:, lo:hi], F.Identity, [wn], ["Qb%d" % k], n, bias=196096.5, banks=[bk])
         if CFG["TP"] == "V":
-            act(nj[:], jm, F.Identity, [jn], [njn], 256, bias=1.0, scale=-1.0)
-        if t == 0:
-            tt(T.G[:], T.edgi[:].indirect(vm0), jm, A.mult, ["edgi", "vm0", jn], ["G"], 256 * GA)
+            act(nj[:], jm, F.Identity, jns, [njn], 256, bias=1.0, scale=-1.0)
+        ts(wl_, wWi, 4096.0, A.min, pn("wWi"), ["wl_"], 16)
+        cp(bWf, bWi, pn("bWi"), ["bWf"], 16)
+        verK, vk = T.VD[:, 0:256], ["VD"]
+        for a, b in CFG["VT"]:
+            cp(T.VT[:, 16 * a:16 * b], VLw.indirect(su[:, a:b]),
+               [VLn] + ["bla%d" % k for k, (c, d) in enumerate(parts) if c < b and a < d],
+               ["VT%d" % q for q in range(a // 2, b // 2)], (16 * (b - a), GA))
+        if CFG["VD"] == "C" or t == 0:
+            cp(verK, T.VT[:], ["VT%d" % q for q in range(8)], vk, 256)
         else:
-            tt(T.G[:], T.SU[:, 0:4096].indirect(vW), jm, A.mult, ["SU", vWn, jn], ["G"], 256 * GA)
-        P([(ps[1][:, 0:256], BO, T.G[:], True, True, 1024)], ["BO", "G"], ["wR"], [1])
-        V(lambda: g.vector.tensor_tensor_scan(T.sc1[:], ps[1][:, 0:256], T.CS[:], 8192.0, A.min, A.add),
-          ["wR", "CS"], ["sc1"], 256, [1])
-        ts(wWi, T.sc1[:, 15:256:16], offp, A.add, ["sc1", "offp"], ["wWi"], 16)
-        ts(wl_, T.sc1[:, 15:256:16], offp, A.add, ["sc1", "offp"], ["wl_"], 16)
-        ts(bWi, wWi, 1023, A.bitwise_and, ["wWi"], ["bWi"], 16)
-        cp(su[:, 0:16], bWi, ["bWi"], ["bla"], 16)
-        if t == 0 or CFG["VD"] != "W":
-            cp(su[:, 16:18], si[:, 16:18], ["bWi"], ["blb"], 16)
-        cp(bWf, bWi, ["bWi"], ["bWf"], 16)
-        VLw = T.VL[:, 0:1024]
-        verK, vk = T.VD[:, 0:256], ["VD0", "VD1"]
-        if t and CFG["VD"] == "W":
-            cp(T.VD[:, 0:128], VLw.indirect(su[:, 0:8]), ["VL", "bla"], ["VD0"], 128 * GA)
-            act(T.VD[:, 128:256], VLw.indirect(su[:, 8:16]), F.Identity, ["VL", "bla"], ["VD1"], 128 * GA)
-            act(T.VD[:, 256:272], VLw.indirect(su[:, 0:1]), F.Identity, ["VL", "bla"], ["VD2"], 16 * GA)
-        elif t == 0:
-            cp(T.VD[:, 0:272], T.veri[:].indirect(su[:, 0:17]), ["veri", "bla", "blb"], vk, 272 * GA)
-        elif CFG["VD"] == "VS":
-            cp(T.VD[:, 0:128], VLw.indirect(su[:, 0:8]), ["VL", "bla"], ["VD0"], 128 * GA)
-            act(T.VD[:, 128:272], VLw.indirect(su[:, 8:17]), F.Identity, ["VL", "bla", "blb"], ["VD1"], 144 * GA)
-        elif CFG["VD"] == "S":
-            act(T.VD[:, 0:272], VLw.indirect(su[:, 0:17]), F.Identity, ["VL", "bla", "blb"], vk, 272 * GA)
-        else:
-            cp(T.VD[:, 0:272], VLw.indirect(su[:, 0:17]), ["VL", "bla", "blb"], vk, 272 * GA)
-        for h in range(2):
-            V(lambda h=h: g.vector.transpose(T.VX[:, 256 * h:256 * h + 256], T.VD[:, 16 * h:16 * h + 256]),
-              vk + (["VD2"] if h else []), ["VX%d" % h], 256)
-        for lo, hi in CFG["VT"]:
-            cp(T.VT[:, 64 * lo:64 * hi], T.VX[:].indirect(cu[:, 32 + 4 * lo:32 + 4 * hi]), ["VX0", "VX1", "PM"],
-               ["VT%d" % q for q in range(lo, hi)], 64 * (hi - lo) * GA)
-        act(T.xc[:], xb, F.Exp, [xn], ["xc"], 256, bias=-9 * LN256, scale=LN256)
-        P([(ps[2][:, 0:256], Ib, T.xc[:], True, True, 256), (ps[2][:, 256:512], Ib, T.xc[:], True, True, 256)],
+            act(verK, VLw.indirect(su[:, 0:16]), F.Identity, [VLn] + pn("bla"), vk, (256, GA))
+        P([(ps[2][:, 256 + 128 * h:384 + 128 * h], wx[:, 256 + 128 * h:384 + 128 * h], Ib, True, True, 128) for h in range(2)],
+          ["Ib", xn], ["pXT"], [2])
+        act(T.xc[:], ps[2][:, 256:512], F.Exp, ["pXT"], ["xc"], 256, bias=-9 * LN256, scale=LN256, banks=[2])
+        P([(ps[2][:, 128 * h:128 * h + 128], T.xc[:, 128 * h:128 * h + 128], Ib, True, True, 128) for h in range(2)],
           ["Ib", "xc"], ["pX"], [2])
-        act(T.Qb[:], ps[1][:, 0:256], F.Identity, ["wR"], ["Qb"], 256, bias=196096.5, banks=[1])
-        P([(ps[1][:, 256:512], BO, T.G[:], True, True, 1024), (ps[1][:, 256:512], In, T.Qb[:], False, True, 256)],
-          ["In", "Qb", "BO", "G"], ["pb"], [1])
-        ts(T.bR[:], ps[1][:, 256:512], 196608.0, A.add, ["pb"], ["bR"], 256, banks=[1])
-        cp(vWf, vW, [vWn], ["vWf"], 16)
-        zcalls(T.Zv, "Zv", vR, vRn, vWf, "vWf")
-        zcalls(T.Zb, "Zb", T.bR, "bR", bWf, "bWf", ["Zv15"] if CFG["ZO"] else [])
-        zsum(T.Zv, "Zv", WSV, "WSV", 7, 64, "Sv", range(15, -1, -1), True)
-        tt(nfT, ps[7][:, 64:80], thT, A.is_ge, ["Sv", "thT"], ["nfT"], 16, [7])
-        spread(CFG["XF"], T.xf[:], fb[:, 80:112], X2, 8192.0, ["nfT", "X2"], ["xf"], 128)
-        P([(ps[7][:, 80:96], If, vWf, True, False, 256)] + toW(T.xf, 7, 80), ["If", "vWf", "xf", "L8"], ["pF"], [7])
-        tt(lfF, ps[7][:, 80:96], cf[:, 96:112], A.min, ["pF", "DW2"], ["lfF"], 16, [7])
-        cp(lF, lfF, ["lfF"], ["lF"], 16)
-        P([(ps[0][:, 256:512], Ib, T.EF[:, t:4096:16], True, False, 256), (ps[0][:, 256:512], Ib, xb, False, True, 256)],
-          ["Ib", "EF", xn], ["pB"], [0])
-        act(T.sgB[:], ps[0][:, 256:512], F.Sign, ["pB"], ["sgB"], 256, bias=-3.5, banks=[0])
-        P([(ps[0][:, 256:512], Ib, T.EF[:, t:4096:16], True, False, 256), (ps[0][:, 256:512], Ib, xb, False, True, 256),
-           (ps[0][:, 256:512], Im2, T.sgB[:], False, True, 256)], ["Im2", "sgB", "Ib", "EF", xn], ["pB"], [0])
-        act(T.xJ[:, 256:512], ps[0][:, 256:512], F.Identity, ["pB"], ["xB"], 256, bias=-2.0, banks=[0])
-        if CFG["JS"] and t + 1 < NS:
-            jmask(T.xJ[:, 768:1024], "jB", T.xJ[:, 256:512], "xB", T.QJ[:, 256:512], "QB")
-        act(T.ws[:, 0:256], T.SU[:, t:4096:16], F.Identity, ["SU"], ["ws0"], 256)
+        if CFG["BR"] == "G":
+            cp(T.bR[:], T.NUM[:].indirect(su[:, 0:16]), ["NUM"] + pn("bla"), ["bR"], (256, GA))
+        else:
+            P([(ps[1][:, 256:512], BO, T.G[:], True, True, 1024), (ps[1][:, 256:512], In, T.Qb[:], False, True, 256)],
+              ["In", "BO"] + pn("G") + pn("Qb"), ["pb"], [1])
+            ts(T.bR[:], ps[1][:, 256:512], 196608.0, A.add, ["pb"], ["bR"], 256, banks=[1])
+        zcalls(T.Zv, "Zv", vR, vRn, vkb, vo, vkn)
+        split((T.kb[:, 0:16], T.kb[:, 16:32]), bWf, "bWf", "Zb")
+        zcalls(T.Zb, "Zb", T.bR, "bR", T.kb, 0, ["Zbh", "Zbl"], ["Zv15"] if CFG["ZO"] else [])
+        zsum(T.Zv, "Zv", T.M2, ["WSV"], 7, 64, "Sv", range(15, -1, -1), True, True)
+        ts(nfT, ps[7][:, 64:80], thr, A.is_ge, ["Sv", "thr"], ["nfT"], 16, banks=[7])
+        nextx(ps[0][:, 256:512], "pB", 0, T.EF[:, t:4096:16], "EF", T.xJ[:, 256:512], "xB")
+        if CFG["JS"] and u < NS:
+            jmask(T.xJ[:, 768:1024], "jB", T.xJ, 256, "xB")
+        copy(CFG["GS"], T.ws[:, 0:256], T.SU[:, t:4096:16], ["SU"], ["ws0"], 256)
         iota(T.wv[:, 256:512], [[16, 256]], ["wv1"], 256, base=t)
         dma("Y", T.wm[:, 256:512], DG[:, t:t + 256], ["DG"], ["wm1"], 65536)
-        P([(ps[3][:, 0:384], ONE[0:64, 0:128], CK[0:64, 0:384], True, False, 384),
-           (ps[4][:, 0:400], ONE[0:64, 0:128], CK[0:64, 0:400], True, False, 400)], ["ONE", "CK"], ["K0", "K1"], [3, 4], True)
-        Rw = T.R[:, 0:5120]
-        act(T.old[:, 4096:4352], Rw.indirect(wl_), F.Exp, ["R", "R5", "wl_"], ["oldw"], 256 * GA, bias=-9 * LN256,
-            scale=LN256)
+        EB = CFG["EB"]
+        kbk, ko, kn = ((3, 4), (0, 0), ("K0", "K1")) if EB else ((3, 3), (0, 128), ("K0", "K0"))
+        o17 = 384 if EB else 256
+        p17 = ps[kbk[1]][:, o17:o17 + 16]
+        if EB:
+            for h in range(2):
+                P([(ps[3 + h][:, 0:128], ON32, CK[0:32, 0:128], True, False, 128),
+                   (ps[3 + h][:, 128:384], ONE[0:2, 0:128], EC, False, False, 256)] + [(p17, ON32, K17, False, False, 64)] * h,
+                  ["ONE", "KC", "K17", "EC"], [kn[h]], [3 + h], True)
+        else:
+            P([(ps[3][:, 0:256], ON32, KC, True, False, 256), (p17, ON32, K17, False, False, 64)],
+              ["ONE", "KC", "K17"], ["K0"], [3], True)
+            P([(ps[4][:, 256 * h:256 * h + 256], ONE[0:2, 0:128], EC, h == 0, False, 256) for h in range(2)],
+              ["ONE", "EC"], ["K1"], [4], True)
+        act(T.old[:, 4096:4352], T.R[:, 0:4112].indirect(wl_), F.Exp, ["R", "R5", "wl_"], ["oldw"], (256, GA),
+            bias=-9 * LN256, scale=LN256)
         tt(T.eq[:, 4096:4352], ps[2][:, 0:256], T.old[:, 4096:4352], A.is_equal, ["pX", "oldw"], ["eqw"], 256, [2])
         mms = []
         for h in range(2):
-            o = ps[4][:, 384 + 8 * h:392 + 8 * h]
+            o = ps[kbk[1]][:, o17 + 8 * h:o17 + 8 * h + 8]
             cs = slice(4096 + 128 * h, 4224 + 128 * h)
             mms += [(o, T.old[:, cs], WK17, False, False, 64), (o, T.eq[:, cs], WK17, False, False, 64),
                     (o, T.G[:, 128 * h:128 * h + 128], SEL8, False, False, 256)]
-        P(mms, ["oldw", "eqw", "WK17", "G", "SEL8"], ["K1"], [4], True)
-        P([(ps[3 + h][:, 0:128], T.VD[:, 128 * h:128 * h + 128], If, False, False, 512) for h in range(2)],
-          vk + ["If"], ["K0", "K1"], [3, 4], True)
+        key17 = (mms, ["oldw", "eqw", "WK17", "SEL8"] + pn("G"))
+        for h in range(2):
+            P([(ps[kbk[h]][:, ko[h]:ko[h] + 128], T.VD[:, 128 * h:128 * h + 128], If, False, False, 512)],
+              vk + ["If"], [kn[h]], [kbk[h]], True)
+
+        def keys(src, sn, h, lo, hi, stop=False):
+            names = [sn + str(q) for q in range(4 * h + lo // 32, 4 * h + hi // 32)]
+            m = 3 if EB and sn == "eq" else 1
+            for k0 in (0, 8):
+                P([(ps[kbk[h]][lo:hi, ko[h] + k:ko[h] + 128 * m:16], src[:, 2048 * h + 16 * lo + k:2048 * h + 16 * hi:16],
+                    cW[:, 384:384 + 8 * m], False, stop and k == 15, min(64, hi - lo)) for k in range(k0, k0 + 8)],
+                  names + ["WKE0", "WKE1", "WKE2"], [kn[h]], [kbk[h]], True)
+
         for q in range(8):
             cs = slice(512 * q, 512 * q + 512)
-            act(T.old[:, cs], T.R[:, 0:4096].indirect(T.VT[:, 32 * q:32 * q + 32]), F.Exp, ["R", "VT%d" % (q // 2)],
-                ["old%d" % q], 512 * GA, bias=-9 * LN256, scale=LN256)
-            tt(T.eq[:, cs], ps[2][:], T.old[:, cs], A.is_equal, ["pX", "old%d" % q], ["eq%d" % q], 512, [2])
-            m1, m2 = [], []
-            for k in (2 * q, 2 * q + 1):
-                for h in range(2):
-                    c2 = slice(256 * k + 128 * h, 256 * k + 128 * h + 128)
-                    m1.append((ps[3 + h][:, k:128:16], T.old[:, c2], cW[:, 384:392], False, False, 64))
-                    m2.append((ps[3 + h][:, k:384:16], T.eq[:, c2], WKE, False, k == 15, 64))
-            P(m1, ["old%d" % q, "WKE0"], ["K0", "K1"], [3, 4], True)
-            P(m2, ["eq%d" % q, "WKE0", "WKE1", "WKE2"], ["K0", "K1"], [3, 4], True)
-        for h in range(2):
-            V(lambda h=h: g.vector.tensor_tensor_scan(T.sc2[:, 128 * h:128 * h + 128], T.MS[:], ps[3 + h][:, 0:128], 0.0,
-                                                      A.add, A.min), ["MS", "K%d" % h], ["sc2%d" % h], 128, [3 + h])
-        tt(keyT, T.sc2[:, 15:256:16], ps[4][:, 384:400], A.min, ["sc20", "sc21", "K1"], ["keyT"], 16, [4])
+            h, a, bk = q // 4, q % 4, 5 + q % 2
+            act(T.old[:, cs], T.R[:, 0:4096].indirect(T.VT[:, 32 * q:32 * q + 32]), F.Exp, ["R", "VT%d" % q],
+                ["old%d" % q], (512, GA), bias=-9 * LN256, scale=LN256)
+            P([(ps[bk][:], T.xc[32 * a:32 * a + 32, 128 * h:128 * h + 128], T.REP[32 * a:32 * a + 32, :], True, True,
+                512 // CFG["DUP"])] * CFG["DUP"], ["xc", "REP"], alias[bk], [bk])
+            tt(T.eq[:, cs], ps[bk][:], T.old[:, cs], A.is_equal, alias[bk] + ["old%d" % q], ["eq%d" % q], 512, [bk])
+            if q == 3:
+                keys(T.old, "old", 0, 0, 128)
+                keys(T.eq, "eq", 0, 0, 128, EB)
+                P(key17[0], key17[1], [kn[1]], [kbk[1]], True)
+            if CFG["KT"] == 2 and q == 6:
+                keys(T.old, "old", 1, 0, 64)
+                keys(T.old, "old", 1, 64, 96)
+            if CFG["KT"] and q in (5, 6):
+                keys(T.eq, "eq", 1, *((0, 64) if q == 5 else (64, 96)))
+            if q == 7:
+                keys(T.old, "old", 1, 96 if CFG["KT"] == 2 else 0, 128)
+                if CFG["KT"]:
+                    keys(T.eq, "eq", 1, 96, 128)
+                    P([(p17, ONE[32:64, 0:128], cb[32:64, 32:48], False, True, 64)], ["ONE", "zer"], [kn[1]], [kbk[1]], True)
+                else:
+                    keys(T.eq, "eq", 1, 0, 128, True)
+            if a == 3 and not EB:
+                for lo in (0, 8):
+                    P([(ps[4][:, 256 * h + k:256 * h + 256:16], T.eq[:, 2048 * h + k:2048 * h + 2048:16], cW[:, 392:408], False,
+                        False, 64) for k in range(lo, lo + 8)],
+                      ["eq%d" % j for j in range(q - 3, q + 1)] + ["WKE1", "WKE2"], ["K1"], [4], True)
+        if EB:
+            for h in range(2):
+                scan(T.sc2[:, 128 * h:128 * h + 128], T.MS[:, 0:128], ps[3 + h][:, 0:128], 0.0, A.add, A.min, ["MS", kn[h]],
+                     ["sc2%d" % h], 128, [3 + h])
+        else:
+            scan(T.sc2[:], T.MS[:], ps[3][:, 0:256], 0.0, A.add, A.min, ["MS", "K0"], ["sc20", "sc21"], 256, [3])
+        tt(keyT, T.sc2[:, 15:256:16], p17, A.min, ["sc20", "sc21", kn[1]], ["keyT"], 16, [kbk[1]])
         ts(hiT, keyT, 4032, A.bitwise_and, ["keyT"], ["hiT"], 16)
         ts(loT, keyT, 63, A.bitwise_and, ["keyT"], ["loT"], 16)
         cp(hl, si[:, 48:80], ["hiT", "loT"], ["hl"], 32)
-        P([(ps[5][0:32, 0:128], hl, Ib, True, True, 128)], ["hl", "Ib"], ["TT"], [5])
-        act(T.TTs[0:32, :], ps[5][0:32, 0:128], F.Identity, ["TT"], ["TTs"], 128, banks=[5])
-        P([(ps[6][:, 128 * h:128 * h + 128], T.SR[0:32, 128 * h:128 * h + 128], T.TTs[0:32, :], True, True, 128)
-           for h in range(2)], ["SR0", "SR1", "TTs"], ["uR"], [6])
+        if CFG["TT"] == "P":
+            P([(ps[5][0:32, 0:128], hl, Ib, True, True, 128)], ["hl", "Ib"], ["TT"], [5])
+            act(T.TTs[0:32, :], ps[5][0:32, 0:128], F.Identity, ["TT"], ["TTs"], 128, banks=[5])
+            P([(ps[6][:, 128 * h:128 * h + 128], T.SR[0:32, 128 * h:128 * h + 128], T.TTs[0:32, :], True, True, 128)
+               for h in range(2)], ["SR0", "SR1", "TTs"], ["uR"], [6])
+        else:
+            V(lambda: g.vector.transpose(T.TTs[:, 0:32], hl), ["hl"], ["TTs"], 16)
+            P([(ps[6][:, 128 * h + 32 * a:128 * h + 32 * a + 32], T.SR[32 * a:32 * a + 32, 128 * h:128 * h + 128],
+                T.TTs[32 * a:32 * a + 32, 0:32], True, True, 64) for h in range(2) for a in range(4)],
+              ["SR0", "SR1", "TTs"], ["uR"], [6])
         cp(T.cR[:], ps[6][:, 0:256], ["uR"], ["cR"], 256, [6])
         act(T.wv[:, 0:256], ps[6][:, 0:256], F.Identity, ["uR"], ["wv0"], 256, banks=[6])
-        if CFG["XU"] == "U":
-            ts(si[:, 96:112], keyT, 4095, A.bitwise_and, ["keyT"], ["uT"], 16)
-            tt(T.xu[:], si[:, 96:112].indirect(X1), DG[:, 0:256], A.mult, ["uT", "X1", "DG"], ["xu"], 256 * GA)
-            P([(ps[7][:, 8 * h:8 * h + 8], T.xu[:, 128 * h:128 * h + 128], SEL8, True, True, 256) for h in range(2)],
-              ["xu", "SEL8"], ["pU"], [7])
+        spread(CFG["XQ"], T.xq[:], fb[:, 144:192], X3, 1.0, ["hl", "X3"], ["xq"], 256)
+        P(toW(T.xq, 7, 96, 32, 32, 0, True), ["xq", "L8"], ["pH"], [7])
+        if CFG["ZC"] == "S":
+            act(T.kb[:, 32:64], ps[7][:, 96:128], F.Identity, ["pH"], ["Zch"], 32, banks=[7])
         else:
-            spread(CFG["XU"], T.xq[:], fb[:, 144:192], X3, 1.0, ["hl", "X3"], ["xq"], 256)
+            cp(T.kb[:, 32:64], ps[7][:, 96:128], ["pH"], ["Zch"], 32, [7])
+        if CFG["XU"] == "K":
+            P(addkey(7, 0, T.kb, 32, True), ["Ib", "Zch"], ["pU"], [7])
+        else:
             P(toW(T.xq, 7, 0, 16, 32, 0, True) + toW(T.xq, 7, 0, 16, 32, 16), ["xq", "L8"], ["pU"], [7])
         cp(ul, ps[7][:, 0:16], ["pU"], ["ul"], 16, [7])
-        if CFG["UW"] == "V":
-            cp(uWf, ps[7][:, 0:16], ["pU"], ["uWf"], 16, [7])
-        else:
-            act(uWf, ps[7][:, 0:16], F.Identity, ["pU"], ["uWf"], 16, banks=[7])
-        for h in range(2):
-            ts(fb[:, 112 + 8 * h:120 + 8 * h], si[:, 32 + 8 * h:40 + 8 * h], 65536.0, A.is_ge, ["keyT", "thT"], ["thrW%d" % h],
-               16, cf[:, 32 + 8 * h:33 + 8 * h], A.mult)
+        ts(thrW, keyT, KD, A.is_ge, ["keyT", "thr"], ["thrW"], 16, thr, A.mult)
         tt(hardT, keyT, thrA, A.is_ge, ["keyT", "thrA"], ["hardT"], 32)
-        spread(CFG["XW"], T.xw[:], fb[:, 112:144], X2, 1 / 2.55, ["thrW0", "thrW1", "X2"], ["xw"], 128)
+        tt(thrC, thrW, hardT, A.mult, ["thrW", "hardT"], ["thrC"], 32)
+        spread(CFG["XW"], T.xw[:], fb[:, 112:144], X2, 1 / THR, ["thrW", "X2"], ["xw"], 128)
         P([(ps[0][:, k:128:8], T.L8[:, 128 * k:128 * k + 128], T.xw[:, 16 * k:16 * k + 16], True, True, 64)
            for k in range(8)], ["L8", "xw"], ["pY"], [0])
-        act(T.wsel[:], ps[0][:, 0:128], F.Identity, ["pY"], ["wsel"], 128, banks=[0])
-        zsum(T.Zb, "Zb", T.wsel, "wsel", 0, 256, "pB", range(15, -1, -1), True)
-        zcalls(T.Zc, "Zc", T.cR, "cR", ps[7][:, 0:16], "pU", bk=[7])
-        tt(nb, ps[0][:, 256:272], thT, A.is_lt, ["pB", "thT"], ["nb"], 16, [0])
-        tt(thrM, nb, thrW, A.mult, ["nb", "thrW0", "thrW1"], ["thrM"], 32)
-        tt(thrC, thrM, hardT, A.mult, ["thrM", "hardT"], ["thrC"], 32)
-        zsum(T.Zc, "Zc", T.wsel, "wsel", 5, 288, "Sc", range(15, 5, -1), True, True)
-        zsum(T.Zc, "Zc", T.wsel, "wsel", 5, 288, "Sc", range(5, 1, -1), False, True)
-        zsum(T.Zc, "Zc", T.wsel, "wsel", 5, 288, "Sc", (1,), False, True)
-        zsum(T.Zc, "Zc", T.wsel, "wsel", 5, 288, "Sc", (0,), False, True)
+        act(T.wsel[:, 0:128], ps[0][:, 0:128], F.Identity, ["pY"], ["wsel"], 128, banks=[0])
+        act(T.wsel[:, 192:256], ps[0][:, 0:64], F.Sign, ["pY"], ["wsel1"], 64, banks=[0])
+        act(T.wsel[:, 128:192], T.wsel[:, 192:256], F.Identity, ["wsel1"], ["wsel2"], 64, scale=BIG)
+        wsn = ["wsel", "wsel2"]
+        zsum(T.Zb, "Zb", T.wsel, wsn, 5, 288, "Sc", range(15, 7, -1), True, False, True)
+        zsum(T.Zb, "Zb", T.wsel, wsn, 5, 288, "Sc", range(7, -1, -1), False, False, True)
+        zcalls(T.Zc, "Zc", T.cR, "cR", T.kb, 32, ["Zch"])
+        for cs in (range(15, 5, -1), range(5, 1, -1), (1,), (0,)):
+            zsum(T.Zc, "Zc", T.wsel, wsn, 5, 288, "Sc", cs, False, True, True)
         tt(clT, ps[5][:, 288:304], thrC, A.is_lt, ["Sc", "thrC"], ["clT"], 16, [5])
-        tt(nmT, ps[5][:, 288:304], thrM, A.is_ge, ["Sc", "thrM"], ["nmT"], 16, [5])
-        tt(ngT, nmT, clT, A.add, ["nmT", "clT"], ["ngT"], 32)
-        spread(CFG["XL"], T.xl[:], fb[:, 0:32], X2, 256.0, ["clT", "X2"], ["xl"], 128)
+        tt(nmT, ps[5][:, 288:304], thrW, A.is_ge, ["Sc", "thrW"], ["nmT"], 16, [5])
+        spread(CFG["XL"], T.xl[:], fb[:, 0:32], X2, 8192.0, ["clT", "X2"], ["xl"], 128)
         P([(ps[5][:, 320:336], Ib, iWb, True, False, 64)] + toW(T.xl, 5, 320), ["Ib", "iWb", "xl", "L8"], ["pS"], [5])
-        cp(sel, ps[5][:, 320:336], ["pS"], ["sel"], 16, [5])
-        act(T.efu[:], T.EF[:].indirect(ul), F.Identity, ["EF", "ul"], ["efu"], 256 * GA)
-        P([(ps[1][:, 0:256], Ib, T.efu[:], True, False, 256), (ps[1][:, 0:256], Ib, xb, False, True, 256)],
-          ["Ib", "efu", xn], ["wR"], [1])
-        act(T.sgA[:], ps[1][:, 0:256], F.Sign, ["wR"], ["sgA"], 256, bias=-3.5, banks=[1])
-        P([(ps[1][:, 0:256], Ib, T.efu[:], True, False, 256), (ps[1][:, 0:256], Ib, xb, False, True, 256),
-           (ps[1][:, 0:256], Im2, T.sgA[:], False, True, 256)], ["Im2", "sgA", "Ib", "efu", xn], ["wR"], [1])
-        act(T.xJ[:, 0:256], ps[1][:, 0:256], F.Identity, ["wR"], ["xA"], 256, bias=-2.0, banks=[1])
-        u = t + 1
+        ts(sel, ps[5][:, 320:336], 1 / 32, A.mult, ["pS"], ["sel"], 16, banks=[5])
+        act(T.efu[:], T.EF[:].indirect(ul), F.Identity, ["EF", "ul"], ["efu"], (256, GA))
+        nextx(ps[1][:, 0:256], "wR", 1, T.efu[:], "efu", T.xJ[:, 0:256], "xA")
         if u < NS:
             s1, s2 = T["s1_%d" % u], T["s2_%d" % u]
-            act(s1[:, 0:256], T.xJ[:, 0:512].indirect(sel), F.Identity, ["xA", "xB", "sel"], ["s1_%d" % u], 256 * GA)
+            act(s1[:, 0:256], T.xJ[:, 0:512].indirect(sel), F.Identity, ["xA", "xB", "sel"], ["s1_%d" % u], (256, GA))
+            iota(cf[:, 160:176], [[0, 16]], ["nL"], 16, base=t)
+            tt(dn, nHL, T.kb[:, 32:64], A.subtract, ["nH", "nL", "Zch"], ["dn"], 64)
+            ts(clW, ps[5][:, 320:336], 8192.0, A.is_ge, ["pS"], ["clW"], 16, banks=[5])
+            for k in range(2):
+                tt(sf[:, 192 + 16 * k:208 + 16 * k], clW, sf[:, 160 + 16 * k:176 + 16 * k], A.mult, ["clW", "dn"], ["tn%d" % k], 32)
+            tt(s1[:, 256:288], tn, T.kb[:, 32:64], A.add, ["tn0", "tn1", "Zch"], ["s1v%d" % u], 64)
             if CFG["JS"]:
-                jmask(T.xJ[:, 512:768], "jA", T.xJ[:, 0:256], "xA", T.QJ[:, 0:256], "QA")
-                act(s1[:, 256:512], T.xJ[:, 512:1024].indirect(sel), F.Identity, ["jA", "jB", "sel"], ["s1j%d" % u], 256 * GA)
-                send(nxt, T["wx%d" % u][:, 256:768], s1[:], "a1_%d" % u, ["s1_%d" % u, "s1j%d" % u], ["m1_%d" % u])
+                jmask(T.xJ[:, 512:768], "jA", T.xJ, 0, "xA")
+                act(s1[:, 288:544], T.xJ[:, 512:1024].indirect(sel), F.Identity, ["jA", "jB", "sel"], ["s1j%d" % u], (256, GA))
+                send(nxt, T["wx%d" % u][:, 256:800], s1[:], "a1_%d" % u, ["s1_%d" % u, "s1j%d" % u, "s1v%d" % u], ["m1_%d" % u])
             else:
-                send(nxt, T["wx%d" % u][:, 256:512], s1[:, 0:256], "a1_%d" % u, ["s1_%d" % u], ["m1_%d" % u])
+                send(nxt, T["wx%d" % u][:, 256:544], s1[:, 0:288], "a1_%d" % u, ["s1_%d" % u, "s1v%d" % u], ["m1_%d" % u])
             recv(prv, "a1_%d" % u, ["m1_%d" % u], ["xb%d" % u])
-        act(T.vnR[:], T.wv[:].indirect(sel), F.Identity, ["wv0", "wv1", "sel"], ["vnR"], 256 * GA)
+        act(T.vnR[:], T.wv[:].indirect(sel), F.Identity, ["wv0", "wv1", "sel"], ["vnR"], (256, GA))
         if u < NS:
-            if CFG["VN"] == "W":
-                act(nWf, iWf, F.Identity, ["iWf"], ["nWf"], 16, bias=float(t), scale=16.0)
-                ts(clW, ps[5][:, 320:336], 256.0, A.is_ge, ["pS"], ["clW"], 16, banks=[5])
-                tt(dnW, nWf, uWf, A.subtract, ["nWf", "uWf"], ["dnW"], 32)
-                tt(t1, clW, dnW, A.mult, ["clW", "dnW"], ["t1"], 32)
-                tt(vnW, t1, uWf, A.add, ["t1", "uWf"], ["vnW"], 32)
-                cp(s2[:, 256:272], vnW, ["vnW"], ["s2v%d" % u], 16)
-            else:
-                V(lambda: g.vector.tensor_tensor_scan(T.CT[:], T.vnR[:], T.CS[:], 8192.0, A.min, A.add),
-                  ["vnR", "CS"], ["CT"], 256)
-                ts(s2[:, 256:272], T.CT[:, 15:256:16], offp, A.add, ["CT", "offp"], ["s2v%d" % u], 16)
-            if CFG["VR"] == "V":
-                cp(s2[:, 0:256], T.wv[:].indirect(sel), ["wv0", "wv1", "sel"], ["s2_%d" % u], 256 * GA)
-            else:
-                cp(s2[:, 0:256], T.vnR[:], ["vnR"], ["s2_%d" % u], 256)
-            send(nxt, T["l2_%d" % u][:], s2[:], "a2_%d" % u, ["s2_%d" % u, "s2v%d" % u], ["m2_%d" % u])
+            cp(s2[:], T.vnR[:], ["vnR"], ["s2_%d" % u], 256)
+            send(nxt, T["l2_%d" % u][:], s2[:], "a2_%d" % u, ["s2_%d" % u], ["m2_%d" % u])
             recv(prv, "a2_%d" % u, ["m2_%d" % u], ["vR_%d" % u])
         else:
             home, frm = T.cores[(rank - t) % N], T.cores[(rank + t) % N]
-            act(T.xh[:], T.xJ[:, 0:512].indirect(sel), F.Identity, ["xA", "xB", "sel"], ["xh"], 256 * GA)
+            act(T.xh[:], T.xJ[:, 0:512].indirect(sel), F.Identity, ["xA", "xB", "sel"], ["xh"], (256, GA))
             send(home, T.lx[:], T.xh[:], "a1_%d" % u, ["xh"], ["m1_%d" % u])
             recv(frm, "a1_%d" % u, ["m1_%d" % u], ["lx"])
             send(home, T.lv[:], T.vnR[:], "a2_%d" % u, ["vnR"], ["m2_%d" % u])
             recv(frm, "a2_%d" % u, ["m2_%d" % u], ["lv"])
             dma("Y", T.yx[:], T.lx[:], ["lx"], ["yx"], 65536)
             dma("Y", T.yv[:], T.lv[0:128:16, :], ["lv"], ["yv"], 8192)
-        spread(CFG["XM"], T.xg[:], fb[:, 32:80], X3, 8192.0, ["nmT", "ngT", "X3"], ["xg"], 256)
-        P(toW(T.xg, 5, 336, 32, 32, 0, True) + [(ps[5][:, 336:352], If, uWf, False, True, 256),
-                                                (ps[5][:, 352:368], If, bWf, False, True, 256)],
-          ["If", "uWf", "bWf", "xg", "L8"], ["pG"], [5])
-        tt(lfGM, ps[5][:, 336:368], cf[:, 64:96], A.min, ["pG", "DW0", "DW1"], ["lfGM"], 32, [5])
-        cp(su[:, 96:128], lfGM, ["lfGM"], ["lGM"], 32)
-        act(T.wc[:], T.SU[:, 0:4096].indirect(ul), F.Identity, ["SU", "ul"], ["wc"], 256 * GA)
-        act(T.Qc[:], T.wc[:], F.Identity, ["wc"], ["Qc"], 256, bias=196096.5)
-        P([(ps[7][:, 256:512], If, T.wc[:], True, False, 1024), (ps[7][:, 256:512], In, T.Qc[:], False, True, 256)],
-          ["If", "In", "wc", "Qc"], ["pC"], [7])
-        act(T.ws[:, 256:512], ps[7][:, 256:512], F.Identity, ["pC"], ["ws1"], 256, bias=200704.0, banks=[7])
-        act(T.SU[:, t:4096:16], T.ws[:].indirect(sel), F.Identity, ["ws0", "ws1", "sel"], ["SU"], 256 * GA)
-        P([(ps[7][:, 256:512], If, T.vnR[:], True, False, 1024), (ps[7][:, 256:512], I8k, jm, False, True, 256)],
-          ["If", "I8k", "vnR", jn], ["pC"], [7])
-        act(T.u2[:], ps[7][:, 256:512], F.Relu, ["pC"], ["u2"], 256, bias=-8192.0, banks=[7])
+        tt(ngT, nmT, clT, A.add, ["nmT", "clT"], ["ngT"], 32)
+        spread(CFG["XM"], T.xg[:], fb[:, 32:96], X4, 8192.0, ["nmT", "ngT", "nfT", "X4"], ["xg"], 384)
+        P(addkey(5, 368, vkb, vo, True) + addkey(5, 352, T.kb, 0) + addkey(5, 336, T.kb, 32) + toW(T.xg, 5, 336, 48, 48),
+          ["Ib", "Zbh", "Zbl", "Zch", "xg", "L8"] + vkn, ["pG"], [5])
+        tt(lfGM, ps[5][:, 336:384], cf[:, 64:112], A.min, ["pG", "DW0", "DW1", "DW2"], ["lfGM"], 48, [5])
+        cp(su[:, 96:144], lfGM, ["lfGM"], ["lGM"], 48)
+        act(T.ws[:, 256:512], T.SU[:, 0:4096].indirect(ul), F.Identity, ["SU", "ul"], ["ws1"], (256, GA), bias=4096.0)
+        act(T.SU[:, t:4096:16], T.ws[:].indirect(sel), F.Identity, ["ws0", "ws1", "sel"], ["SU"], (256, GA))
         if CFG["TP"] == "V":
-            tt(T.tp[:], T.SU[:, 0:4096].indirect(vW), nj[:], A.mult, ["SU", vWn, njn], ["tp"], 256 * GA)
+            P([(ps[7][:, 256:512], If, T.vnR[:], True, False, 1024), (ps[7][:, 256:512], I8k, jm, False, True, 256)],
+              ["If", "I8k", "vnR"] + jns, ["pC"], [7])
+            act(T.u2[:], ps[7][:, 256:512], F.Relu, ["pC"], ["u2"], 256, bias=-8192.0, banks=[7])
+            tt(T.tp[:], T.SU[:, 0:4096].indirect(vW), nj[:], A.mult, ["SU", vWn, njn], ["tp"], (256, GA))
         else:
-            act(T.sv[:], T.SU[:, 0:4096].indirect(vW), F.Identity, ["SU", vWn], ["sv"], 256 * GA)
-            P([(ps[0][:, 256:512], If, T.sv[:], True, False, 1024), (ps[0][:, 256:512], In8, jm, False, True, 256)],
-              ["If", "In8", "sv", jn], ["pB"], [0])
-            act(T.tp[:], ps[0][:, 256:512], F.Relu, ["pB"], ["tp"], 256, banks=[0])
-        tt(T.SU[:].indirect(lF), T.tp[:], T.u2[:], A.add, ["tp", "u2", "lF"], ["SU"], 256 * SC)
-        if CFG["EQC"] == "V":
-            act(T.rc[:], T.R[:, 0:4096].indirect(ul), F.Exp, ["R", "ul"], ["rc"], 256 * GA, bias=-9 * LN256, scale=LN256)
+            act(T.tp[:], T.SU[:, 0:4096].indirect(vW), F.Identity, ["SU", vWn], ["tp"], (256, GA))
+            P([(ps[7][:, 256:512], If, T.vnR[:], True, False, 1024), (ps[7][:, 256:512], Ifn, T.tp[:], False, True, 1024)],
+              ["If", "Ifn", "vnR", "tp"], ["pC"], [7])
+            tt(T.u2[:], ps[7][:, 256:512], jm, A.mult, ["pC"] + jns, ["u2"], 256, [7])
+        tt(T.SU[:].indirect(lF), T.tp[:], T.u2[:], A.add, ["tp", "u2", "lGM"], ["SU"], (256, SC))
+        if CFG["EQC"] == "X":
+            act(T.rc[:], T.R[:, 0:4096].indirect(ul), F.Exp, ["R", "ul"], ["rc"], (256, GA), bias=-9 * LN256, scale=LN256)
             tt(T.eqc[:], ps[2][:, 0:256], T.rc[:], A.is_equal, ["pX", "rc"], ["eqc"], 256, [2])
         else:
-            act(T.rc[:], T.R[:, 0:4096].indirect(ul), F.Identity, ["R", "ul"], ["rc"], 256 * GA)
-            P([(ps[2][:, 0:256], Ib, T.rc[:], True, False, 256), (ps[2][:, 0:256], In, xb, False, True, 256)],
-              ["Ib", "In", "rc", xn], ["pX"], [2])
-            act(T.ea[:], ps[2][:, 0:256], F.Abs, ["pX"], ["ea"], 256, banks=[2])
-            act(T.eqc[:], T.ea[:], F.Relu, ["ea"], ["eqc"], 256, bias=1.0, scale=-1.0)
-        P([(ps[2][:, 256 * h:256 * h + 256], T.eqc[:, 128 * h:128 * h + 128], WEC, True, True, 256) for h in range(2)],
-          ["eqc", "WEC0", "WEC1"], ["pX"], [2])
-        act(T.Ec[:], ps[2][:], F.Identity, ["pX"], ["Ec"], 512, banks=[2])
-        for h in range(2):
-            tt(T.Xi[:, 256 * h:256 * h + 256], ps[3 + h][:, 128:384], T.Ec[:, 256 * h:256 * h + 256], A.add,
-               ["K%d" % h, "Ec"], ["Xi%d" % h], 256, [3 + h])
+            tt(T.eqc[:], T.R[:, 0:4096].indirect(ul), xb, A.is_equal, ["R", "ul", xn], ["eqc"], (256, GA))
+        if EB:
+            P([(ps[2][:, 256 * h:256 * h + 256], T.eqc[:, 128 * h:128 * h + 128], WEC, True, True, 256) for h in range(2)],
+              ["eqc", "WEC0", "WEC1"], ["pX", "pXT"], [2])
+            act(T.Ec[:], ps[2][:], F.Identity, ["pX", "pXT"], ["Ec"], 512, banks=[2])
+            for h in range(2):
+                tt(T.Xi[:, 256 * h:256 * h + 256], ps[3 + h][:, 128:384], T.Ec[:, 256 * h:256 * h + 256], A.add,
+                   [kn[h], "Ec"], ["Xi%d" % h], 256, [3 + h])
+        else:
+            P([(ps[4][:, 256 * h:256 * h + 256], T.eqc[:, 128 * h:128 * h + 128], WEC, False, h == 1, 256) for h in range(2)],
+              ["eqc", "WEC0", "WEC1"], ["K1"], [4], True)
+            cp(T.Xi[:], ps[4][:], ["K1"], ["Xi0", "Xi1"], 512, [4])
         ts(T.Xa[:], T.Xi[:], 43690, A.bitwise_and, ["Xi0", "Xi1"], ["Xa"], 512)
-        ts(T.ok[:], T.Xa[:], 0.0, A.is_equal, ["Xa"], ["ok"], 512)
-        P([(ps[6][:, 256 + 128 * h:384 + 128 * h], T.ok[:, 256 * h + 128 * q:256 * h + 128 * q + 128], Ib, q == 0, q == 1, 128)
-           for h in range(2) for q in range(2)], ["ok", "Ib"], ["pE"], [6])
-        act(T.wm[:, 0:256], ps[6][:, 256:512], F.Relu, ["pE"], ["wm0"], 256, bias=-1.0, banks=[6])
-        act(T.mm[:], T.wm[:].indirect(sel), F.Identity, ["wm0", "wm1", "sel"], ["mm"], 256 * GA)
+        if CFG["OK"] == "S":
+            act(T.ok[:], T.Xa[:].indirect(ID), F.Relu, ["Xa", "ID"], ["ok"], (512, GA), bias=1.0, scale=-1.0)
+        else:
+            ts(T.ok[:], T.Xa[:], 0.0, A.is_equal, ["Xa"], ["ok"], 512)
+        P([(ps[5][:, 128 * h:128 + 128 * h], T.ok[:, 256 * h + 128 * q:256 * h + 128 * q + 128], Ib, q == 0, q == 1, 128)
+           for h in range(2) for q in range(2)], ["ok", "Ib"], ["TT"], [5])
+        act(T.wm[:, 0:256], ps[5][:, 0:256], F.Relu, ["TT"], ["wm0"], 256, bias=-1.0, banks=[5])
+        act(T.mm[:], T.wm[:].indirect(sel), F.Identity, ["wm0", "wm1", "sel"], ["mm"], (256, GA))
         if CFG["TV"] == "V":
             P([(ps[6][:, 0:256], If, T.vnR[:], True, False, 1024), (ps[6][:, 0:256], Ifn, verK, False, True, 1024)],
               ["If", "Ifn", "vnR"] + vk, ["uR"], [6])
             tt(T.tv[:], ps[6][:, 0:256], T.mm[:], A.mult, ["uR", "mm"], ["tv"], 256, [6])
-            tt(T.VL[:].indirect(lM), verK, T.tv[:], A.add, vk + ["tv", "lGM"], ["VL"], 256 * SC)
+            tt(T.VL[:].indirect(lM), verK, T.tv[:], A.add, vk + ["tv", "lGM"], ["VL"], (256, SC))
         else:
-            P([(ps[6][:, 0:256], If, T.vnR[:], True, False, 1024), (ps[6][:, 0:256], I8k, T.mm[:], False, True, 256),
-               (ps[6][:, 256:512], If, verK, True, False, 1024), (ps[6][:, 256:512], In8, T.mm[:], False, True, 256)],
-              ["If", "I8k", "In8", "vnR", "mm"] + vk, ["uR", "pE"], [6])
+            P([(ps[2][:, 256:512], If, verK, True, False, 1024)], ["If", "eqc"] + vk, ["pXT"], [2], True)
+            P([(ps[6][:, 0:256], If, T.vnR[:], True, False, 1024)], ["If", "vnR"], ["uR"], [6], True)
+            P([(ps[2][:, 256:512], In8, T.mm[:], False, True, 256)], ["In8", "mm"], ["pXT"], [2], True)
+            P([(ps[6][:, 0:256], I8k, T.mm[:], False, True, 256)], ["I8k", "mm"], ["uR"], [6], True)
             act(T.tv[:], ps[6][:, 0:256], F.Relu, ["uR"], ["tv"], 256, bias=-8192.0, banks=[6])
-            act(T.tw[:], ps[6][:, 256:512], F.Relu, ["pE"], ["tw"], 256, banks=[6])
-            tt(T.VL[:].indirect(lM), T.tw[:], T.tv[:], A.add, ["tw", "tv", "lGM"], ["VL"], 256 * SC)
+            act(T.tw[:], ps[2][:, 256:512], F.Relu, ["pXT"], ["tw"], 256, banks=[2])
+            tt(T.VL[:].indirect(lM), T.tw[:], T.tv[:], A.add, ["tw", "tv", "lGM"], ["VL"], (256, SC))
         P([(ps[1][:, 256:512], In, xb, True, False, 256), (ps[1][:, 256:512], I16, T.eqc[:], False, True, 256)],
           ["In", "I16", xn, "eqc"], ["pb"], [1])
-        act(T.ga[:], ps[1][:, 256:512], F.Relu, ["pb"], ["ga"], 256, bias=-7.0, banks=[1])
-        act(T.gn[:], T.ga[:], F.Identity, ["ga"], ["gn"], 256, bias=9.0, scale=-1.0)
-        cp(T.R[:].indirect(lG), T.gn[:], ["gn", "lGM", "R5"], ["R"], 256 * SC)
-        act(wx[:, 0:256], T.R[:, t:4096:16], F.Identity, ["R"], ["wx0_%d" % t], 256)
-        act(T.R[:, t:4096:16], wx[:, 0:512].indirect(sel), F.Identity, ["wx0_%d" % t, xn, "sel"], ["R"], 256 * GA)
+        act(T.ga[:], ps[1][:, 256:512], F.Relu, ["pb"], ["ga"], 256, bias=9.0, banks=[1])
+        tt(T.R[:].indirect(lG), xb, T.ga[:], A.add, ["ga", xn, "lGM", "R5"], ["R"], (256, SC))
+        copy(CFG["GR"] if u < NS else CFG["GRZ"], wx[:, 0:256], T.R[:, t:4096:16], ["R"], ["wx0_%d" % t], 256)
+        act(T.R[:, t:4096:16], wx[:, 0:512].indirect(sel), F.Identity, ["wx0_%d" % t, xn, "sel"], ["R"], (256, GA))
         if u < NS:
-            cnt = lambda o: [(ps[7][:, o + 8 * k:o + 8 * k + 8], ONE[:, 0:128], fb[:, 8 * h:8 * h + 8], h == 0, h == 1, 64)
+            cnt = lambda w: [(ps[7][:, 16 + 8 * k:24 + 8 * k], w, fb[:, 16 + 8 * h:24 + 8 * h], False, False, 64)
                              for k in range(2) for h in range(2)]
-            P(cnt(16), ["ONE", "clT"], ["pA"], [7])
-            act(Q2, ps[7][:, 16:32], F.Identity, ["pA"], ["Q2"], 16, bias=256.0, banks=[7])
-            P([(ps[7][:, 32:48], In, Q2, True, False, 64)] + [m[:3] + (False,) + m[4:] for m in cnt(32)],
-              ["ONE", "clT", "In", "Q2"], ["pT"], [7])
-            act(par2, ps[7][:, 32:48], F.Abs, ["pT"], ["par2"], 16, bias=2.0 ** 24, scale=65536.0, banks=[7])
-            act(thrA, par2, F.Identity, ["par2"], ["thrA"], 16, bias=4.0 * 65536)
+            row = lambda w, m, st: [(ps[7][:, 16:32], w, m, st, False, 64)]
+            P(row(NE32, MK[0:32, 512:528], True) + cnt(ONE[:, 0:128]) + row(ON32, M2p, False) + row(NE32, M2p, False)
+              + cnt(NEG[:]), ["ONE", "NEG", "H64", "M2p", "clT"], ["pA"], [7])
+            act(thrA, ps[7][:, 16:32], F.Identity, ["pA"], ["thrA"], 16, bias=4.0 * 65536 - 2.0 ** 20, scale=-65536.0, banks=[7])
 
     dma("Y", T.yr[:], T.R[:, 0:4096], ["R"], ["yr"], 1048576)
     dma("Y", T.yl[:], T.VL[:, 0:1024], ["VL"], ["yl"], 524288)
-    for q in range(8):
-        P([(ps[1][:, k:256:32], T.SU[:, 128 * k:128 * k + 128], SEL8, True, True, 256) for k in range(4 * q, 4 * q + 4)],
-          ["SU", "SEL8"], ["wR"], [1])
-    act(T.y1[:], ps[1][:, 0:256], F.Identity, ["wR"], ["y1"], 256, banks=[1])
-    P([(ps[0][:, 128 * h:128 * h + 128], T.y1[:, 128 * h:128 * h + 128], If, True, True, 512) for h in range(2)],
-      ["y1", "If"], ["pY"], [0])
-    act(T.y2[:], ps[0][:, 0:256], F.Identity, ["pY"], ["y2"], 256, banks=[0])
-    for h in range(2):
-        dma("Y", T.ys[4 * h:4 * h + 4, :], T.y2[:, 128 * h:128 * h + 128], ["y2"], ["ys%d" % h], 65536)
+    for t in range(NS):
+        ts(T.QZ[:, t:4096:16], T.SU[:, t:4096:16], 196096.5, A.add, ["SU", "QZ"], ["QZ%d" % t], 256, 200704.0, A.max)
+    back = col(33)
+    ts(back, pf, float(NS), A.is_lt, ["pg"], ["back"], 1, 16 * 200704.0, A.mult)
+    if True:
+        pass
+    for h, (bk, bn, b2, n2) in enumerate(((1, "wR", 0, "pY"), (2, "pX", 3, "K0"))):
+        o = lambda k: ps[bk][:, k:128:16]
+        P([(ps[bk][:, 0:128], ON32, T.QZ[0:32, 15:2048:16], True, False, 128)], ["ONE", "QZ"], [bn], [bk], True)
+        for q in range(4):
+            P([(o(k), T.SU[:, 2048 * h + 128 * k:2048 * h + 128 * k + 128], SEL8, False, False, 256)
+               for k in range(4 * q, 4 * q + 4)], ["SU", "SEL8"], [bn], [bk], True)
+        P([(o(k), T.QZ[:, 2048 * h + 128 * k:2048 * h + 128 * k + 128], NS8, False, k == 15, 64) for k in range(16)],
+          ["NS8"] + ["QZ%d" % t for t in range(NS)], [bn], [bk], True)
+        hs = slice(128 * h, 128 * h + 128)
+        act(T.y1[:, hs], ps[bk][:, 0:128], F.Identity, [bn, "back"], ["y1%d" % h], 128, bias=back, banks=[bk])
+        P([(ps[b2][:, 0:128], T.y1[:, hs], If, True, True, 512)], ["y1%d" % h, "If"], [n2], [b2])
+        act(T.y2[:, hs], ps[b2][:, 0:128], F.Identity, [n2], ["y2%d" % h], 128, banks=[b2])
+        dma("Y", T.ys[:, 2048 * h:2048 * h + 2048], T.y2[:, hs], ["y2%d" % h], ["ys%d" % h], 65536)
     return ops
 
 
-HOP, SELF = 110.0, 60.0
+HOP, SELF = CFG["COSTS"][0][7:9]
 
 
-def plan(ops):
+def plan(ops, other):
     lastw, readers = {}, {}
     for o in ops:
         d = set()
@@ -642,59 +692,36 @@ def plan(ops):
         for w in o["w"]:
             lastw[w] = o["i"]
             readers[w] = []
+    n = len(ops)
     succ = [[] for _ in ops]
     for o in ops:
         for d in o["d"]:
             succ[d].append(o["i"])
-    for o in reversed(ops):
-        o["p"] = o["c"] + o.get("lat", 0) + max([HOP + ops[s]["p"] for s in succ[o["i"]]], default=0)
-    left = [len(o["d"]) for o in ops]
-    ready = [o["i"] for o in ops if not o["d"]]
-    free, bank, order = {}, {}, []
-
-    def est(o):
-        s = 0.0 if o["e"] == "X" else free.get(o["e"], 0.0)
-        for d in o["d"]:
-            p = ops[d]
-            s = max(s, p["end"] + (0 if p["e"] == o["e"] == "P" else SELF if p["e"] == o["e"] else HOP))
-        for b in o["b"]:
-            for e, tm in bank.get(b, {}).items():
-                if e != o["e"]:
-                    s = max(s, tm + HOP)
-        return s
-
-    while ready:
-        c = [(est(ops[i]), i) for i in ready]
-        m = min(c)
-        e = ops[m[1]]["e"]
-        s, i = max([x for x in c if ops[x[1]]["e"] == e and x[0] <= m[0] + 70], key=lambda x: (ops[x[1]]["p"], -x[1]))
-        o = ops[i]
-        o["s"] = s
-        o["end"] = s + o["c"] + o.get("lat", 0)
-        free[e] = s + o["c"]
-        for b in o["b"]:
-            bank.setdefault(b, {})[e] = o["end"]
-        order.append(o)
-        ready.remove(i)
-        for j in succ[i]:
-            left[j] -= 1
-            if left[j] == 0:
-                ready.append(j)
 
     def hop(a, b):
         return 1.0 if a["e"] == b["e"] == "P" else SELF if a["e"] == b["e"] else HOP
 
-    def fit(lst, s, c, own):
-        lo, hi = 0, len(lst)
-        while lo < hi:
-            mid = (lo + hi) // 2
-            if lst[mid][0] < s - 6000:
-                lo = mid + 1
-            else:
-                hi = mid
-        pad = 0.0 if own is None else HOP
-        for a, b, e in lst[lo:]:
-            if a - pad >= s + c:
+    c = [o["c"] for o in ops]
+    lat = [o.get("lat", 0) for o in ops]
+    eng_of = [o["e"] for o in ops]
+    banks = [o["b"] for o in ops]
+    pre = [[(j, c[j] + lat[j] + hop(ops[j], o)) for j in o["d"]] for o in ops]
+    post = [[(j, c[j] + hop(o, ops[j]) + lat[o["i"]]) for j in succ[o["i"]]] for o in ops]
+    first = [i for i in range(n) if eng_of[i] == "Y" and not ops[i]["d"]]
+
+    def fit(lst, s, cost, own):
+        lo = len(lst)
+        if own is None:
+            while lo and lst[lo - 1][1] > s:
+                lo -= 1
+            pad = 0.0
+        else:
+            while lo and lst[lo - 1][0] > s - 1400:
+                lo -= 1
+            pad = HOP
+        for k in range(lo, len(lst)):
+            a, b, e = lst[k]
+            if a - pad >= s + cost:
                 break
             if e != own and b + pad > s:
                 s = b + pad
@@ -707,52 +734,133 @@ def plan(ops):
         lst.insert(k, it)
 
     def sweep(seq, back):
-        at, eng, bk = {}, {}, {}
+        at, eng, bk = [0.0] * n, {e: [] for e in "VSPGY"}, [[] for _ in range(8)]
         if not back:
-            first = [o["i"] for o in ops if o["e"] == "Y" and not o["d"]]
             seq = first + [i for i in seq if i not in first]
         for i in seq:
-            o = ops[i]
-            if back:
-                s = max([at[j] + ops[j]["c"] + hop(o, ops[j]) for j in succ[i]], default=0.0) + o.get("lat", 0)
-            else:
-                s = max([at[j] + ops[j]["c"] + ops[j].get("lat", 0) + hop(ops[j], o) for j in o["d"]], default=0.0)
-            if o["e"] != "X":
+            s = lat[i] if back else 0.0
+            for j, d in (post[i] if back else pre[i]):
+                if at[j] + d > s:
+                    s = at[j] + d
+            e = eng_of[i]
+            if e != "X":
                 while True:
-                    s2 = fit(eng.setdefault(o["e"], []), s, o["c"], None)
-                    for b in o["b"]:
-                        s2 = fit(bk.setdefault(b, []), s2, o["c"], o["e"])
+                    s2 = fit(eng[e], s, c[i], None)
+                    for b in banks[i]:
+                        s2 = fit(bk[b], s2, c[i], e)
                     if s2 == s:
                         break
                     s = s2
-                put(eng[o["e"]], (s, s + o["c"], o["e"]))
-                for b in o["b"]:
-                    put(bk[b], (s, s + o["c"], o["e"]))
+                put(eng[e], (s, s + c[i], e))
+                for b in banks[i]:
+                    put(bk[b], (s, s + c[i], e))
             at[i] = s
         return at
 
-    at = {o["i"]: o["s"] for o in ops}
-    best = (1e18, at)
-    for seed in CFG["SEEDS"]:
-        key, sh, part, big = {}, {}, "mmaz"[seed % 4], (1, 3)[seed // 4 % 2]
-        for o in ops:
-            nm = o["e"] + o["w"][0].split("_")[0] + o["t"]
-            if nm not in sh:
-                seed = (seed * 1103515245 + 12345) % 2147483648
-                z = (seed >> 8) % 1000 / 1000.0
-                sh[nm] = (z / CFG["FRAC"] - 0.5) * 2 * CFG["NOISE"] * big if z < CFG["FRAC"] and o["t"] == part else 0.0
-            key[o["i"]] = max([best[1][o["i"]] + sh[nm]] + [key[d] + 0.01 for d in o["d"]])
-        at = sweep(sorted(key, key=lambda i: (key[i], i)), False)
-        for _ in range(CFG["IT"]):
-            bk_ = sweep(sorted(at, key=lambda i: (-(at[i] + ops[i]["c"] + ops[i].get("lat", 0)), -i)), True)
-            at = sweep(sorted(bk_, key=lambda i: (-(bk_[i] + ops[i]["c"]), i)), False)
-            end = max(at[i] + ops[i]["c"] + ops[i].get("lat", 0) for i in at)
+    p = [0.0] * n
+    for i in range(n - 1, -1, -1):
+        p[i] = c[i] + lat[i] + max([HOP + p[j] for j in succ[i]], default=0)
+    at = sweep(sorted(range(n), key=lambda i: (-p[i], i)), False)
+    best = (max(at[i] + c[i] + lat[i] for i in range(n)), at)
+    name = [o["nm"] for o in ops]
+    deps = [list(o["d"]) for o in ops]
+
+    def blocked(at):
+        ends = {}
+        for i in range(n):
+            for r in [eng_of[i]] + list(banks[i]):
+                ends.setdefault(r, []).append((at[i] + c[i], i))
+        for r in ends:
+            ends[r].sort()
+        i, out = max(range(n), key=lambda i: at[i] + c[i] + lat[i]), []
+        while True:
+            ready, j = max([(at[j] + d, j) for j, d in pre[i]], default=(0.0, -1))
+            if at[i] > ready + 1:
+                cand = [x for r in [eng_of[i]] + list(banks[i]) for x in ends[r] if at[i] - HOP - 1 <= x[0] <= at[i] + 1 and x[1] != i]
+                if cand:
+                    j = max(cand)[1]
+                    out.append((i, j, at[i] - ready))
+            if j < 0:
+                return out
+            i = j
+
+    state, pairs = [12345], None
+
+    def rnd():
+        state[0] = (state[0] * 1103515245 + 12345) % 2147483648
+        return (state[0] >> 8) % 100000 / 100000.0
+
+    kind = [[(j, 0 if eng_of[i] == eng_of[j] == "P" else 1 if eng_of[i] == eng_of[j] else 2) for j in deps[i]] for i in range(n)]
+
+    def replay(order, cs, hops):
+        free, bank, end = {}, [{} for _ in range(8)], [0.0] * n
+        for i in order:
+            e = eng_of[i]
+            s = 0.0 if e == "X" else free.get(e, 0.0)
+            for j, k in kind[i]:
+                if end[j] + hops[k] > s:
+                    s = end[j] + hops[k]
+            for b in banks[i]:
+                for e2, x in bank[b].items():
+                    if e2 != e and x + hops[2] > s:
+                        s = x + hops[2]
+            free[e] = s + cs[i]
+            end[i] = s + cs[i] + lat[i]
+            for b in banks[i]:
+                bank[b][e] = end[i]
+        return max(end)
+
+    def value(at, bound=1e18):
+        v = max(at[i] + c[i] + lat[i] for i in range(n)) + CFG["MEAN"] * sum(at) / n
+        order = sorted(range(n), key=lambda i: (at[i], i))
+        for cs, m in zip(other, CFG["COSTS"][1:]):
+            v += m[9] * replay(order, cs, (1.0, m[8], m[7]))
+        return v
+
+    cur = best = (value(best[1]), best[1])
+    for it in range(CFG["ROUNDS"]):
+        sh = {}
+        if pairs is None:
+            pairs = blocked(cur[1])
+        if pairs and rnd() < CFG["PAIR"]:
+            for _ in range(1 + int(2 * rnd())):
+                i, j, w = pairs[int(rnd() * len(pairs))]
+                if rnd() < 0.5:
+                    sh[name[i]] = -(w + 20) * (0.3 + rnd())
+                else:
+                    sh[name[j]] = (c[i] + c[j] + 100) * (1 + 3 * rnd())
+        else:
+            part, big = "mmazc"[int(5 * rnd())], (1, 3)[int(2 * rnd())]
+            for nm in sorted(set(name)):
+                if nm[-1] == part and rnd() < CFG["FRAC"]:
+                    sh[nm] = (rnd() - 0.5) * 2 * CFG["NOISE"] * big
+        if rnd() < CFG["ALL"]:
+            sh = {nm[:-1] + x: v for nm, v in sh.items() for x in ("c" if nm[-1] == "c" else "amz")}
+        key = [cur[1][i] + sh.get(name[i], 0.0) for i in range(n)]
+        up = [sh.get(name[i], 0.0) < 0 for i in range(n)]
+        for i in range(n - 1, -1, -1):
+            if up[i]:
+                for d in deps[i]:
+                    if key[d] > key[i] - 0.01:
+                        key[d], up[d] = key[i] - 0.01, True
+        for i in range(n):
+            for d in deps[i]:
+                if key[d] + 0.005 > key[i]:
+                    key[i] = key[d] + 0.005
+        at = sweep(sorted(range(n), key=lambda i: (key[i], i)), False)
+        end = value(at)
+        if end < cur[0] + CFG["SLACK"]:
+            bk_ = sweep(sorted(range(n), key=lambda i: (-(at[i] + c[i] + lat[i]), -i)), True)
+            at2 = sweep(sorted(range(n), key=lambda i: (-(bk_[i] + c[i]), i)), False)
+            end2 = value(at2)
+            if end2 < end:
+                at, end = at2, end2
+        if end < cur[0] + CFG["HEAT"] * rnd() * (1 - it / CFG["ROUNDS"]):
+            cur, pairs = (end, at), None
             if end < best[0]:
-                best = (end, at)
-    for o in ops:
-        o["s"] = best[1][o["i"]]
-        o["end"] = o["s"] + o["c"] + o.get("lat", 0)
-    return sorted(ops, key=lambda o: (o["s"], o["i"]))
+                best = cur
+    ORDER["end"], ORDER["at"] = max(best[1][i] + c[i] + lat[i] for i in range(n)), best[1]
+    return sorted(ops, key=lambda o: (best[1][o["i"]], o["i"]))
 
 
 def emit(g, T, ops, order):
@@ -818,9 +926,10 @@ def rank_program(g, core, T, topo):
     rank = T.rank_of(core)
     if rank is None:
         return
-    ops = build(g, core, T, topo, rank)
+    ops = build(g, core, T, topo, rank, CFG["COSTS"][0])
     if "o" not in ORDER:
-        ORDER["o"] = [(o["i"], o["d"]) for o in plan(ops)]
+        other = [[o["c"] for o in build(g, core, T, topo, rank, m)] for m in CFG["COSTS"][1:]]
+        ORDER["o"] = [(o["i"], o["d"]) for o in plan(ops, other)]
     for i, d in ORDER["o"]:
         ops[i]["d"] = d
     emit(g, T, ops, [ops[i] for i, d in ORDER["o"]])

@@ -8,10 +8,12 @@ NS = 6
 BF, F32, I32, U16 = "bfloat16", "float32", "int32", "uint16"
 
 CFG = dict(EQC="X", TV="S", XU="K", XW="S", XL="S", XM="S", XF="S", XQ="S", VD="C", ZO=1, IT=1, TP="V", JS=0,
-           PARTS=((0, 4), (4, 16)), VT=((0, 4), (4, 16)), GS="G", GR="G", GRZ="S", BR="G", KT=0, TT="P", OK="V", CVT="G", DUP=1, ZC="S", EB=0, CUT=800,
-           COSTS=((0.92, 0.48, 1.4, 3.0, 4000, 500, 400, 110, 60, 1.0, 8), (0.83, 0.45, 1.1, 1.8, 4500, 700, 700, 130, 80, 1.1, 15),
-                  (1.15, 0.6, 1.9, 5.0, 3500, 500, 250, 110, 60, 0.75, 5)),
-           ROUNDS=3800, NOISE=600, FRAC=0.05, PAIR=0.85, SLACK=1500, HEAT=1000, ALL=0.5, MEAN=0.5)
+           PARTS=((0, 4), (4, 16)), VT=((0, 4), (4, 16)), GS="G", GR="G", GRZ="S", BR="G", KT=2, TT="P", OK="V", CVT="G", DUP=1, ZC="S", EB=0, CUT=800, TZ=2, SEED=12345, KB="V", ZS=0, WHOLE=("Sv", "pC", "pG", "pA"), XB=(5, 6, 1, 5, 6, 1, 5, 6), UL=0, H1=0, H2=0, WS="S", XA="S", JM="S", S1="S",
+           OLD=((0, 1), (1, 2), (2, 4), (4, 6), (6, 7), (7, 8)),
+           COSTS=((0.97, 0.49, 1.5, 3.5, 4000, 500, 400, 180, 90, 1.0, 0), (0.85, 0.44, 1.15, 2.0, 4500, 700, 600, 200, 100, 0.9, 0),
+                  (1.2, 0.6, 1.85, 5.0, 3500, 500, 250, 150, 80, 0.9, 0)),
+           ROUNDS=6500, NOISE=600, FRAC=0.05, PAIR=0.85, SLACK=1500, HEAT=1000, ALL=0.5, MEAN=0.5, KIN=0.12, BACK=0.4, RANKS=0, LATE={},
+           STARTS=5, SHORT=800)
 
 
 def _buffers():
@@ -20,9 +22,9 @@ def _buffers():
         (BF, dict(R=4368, EF=4096, ef0=512, old=4352, eq=4352, Zb=4096, Zc=4096, Zv=4096, QZ=4096, Q0=512, jm0=256, jm1=256,
                   nj0=256, nj1=256, Qb=256, xc=256, TTs=128, xw=128, xl=128, xg=384, xq=256, wsel=256, efu=256,
                   rc=256, eqc=256, ga=256, ok=512, wm=512, mm=256, xh=256, lx=256, fb=192, kb=96, xJ=1024,
-                  cI=512, cW=640, L8=1152, DG=272, M2=384, CK=656, MK=784, ONE=256, NEG=128, REP=512, SR=256, cb=64)),
+                  cI=512, cW=640, L8=1152, DG=272, M2=384, CK=656, MK=784, ONE=256, NEG=128, REP=512, SR=256, SQ=1024, cb=64)),
         (F32, dict(VL=1280, SU=4352, v8f=256, G=256, sc1=256, sc2=256, VD=256, sf=512, wv=512, vnR=256, ws=512, u2=256,
-                   tp=256, tv=256, tw=256, lv=256, y1=256, y2=256, io_f=768, cf=256, cI32=512, CS=256, MS=256, NUM=1024, Ec=512)),
+                   tp=256, tv=256, tw=256, lv=256, y1=256, y2=256, io_f=768, cf=256, cI32=512, CS=256, MS=256, NUM=1024, Ec=512, sv=256)),
         (I32, dict(veri=1024, edgi=1024, v8i=256, si=128, Xi=512, Xa=512, io_i=8)),
         (U16, dict(VT=256, bR=256, cR=256, su=256, vR0=256, cu=96)),
     ):
@@ -32,8 +34,12 @@ def _buffers():
         s["wx%d" % t] = ("sbuf", [128, 800], BF)
     for t in range(1, NS):
         s["s1_%d" % t] = ("sbuf", [128, 544], BF)
-        s["s2_%d" % t] = ("sbuf", [128, 256], U16)
-        s["l2_%d" % t] = ("sbuf", [128, 256], U16)
+        s["s2_%d" % t] = ("sbuf", [128, 16], BF)
+        if not CFG["ZS"]:
+            s["s3_%d" % t] = ("sbuf", [128, 256], U16)
+            s["l3_%d" % t] = ("sbuf", [128, 256], U16)
+    for t in range(NS):
+        s["l2_%d" % t] = ("sbuf", [128, 64], BF)
     for b in range(8):
         s["ps%d" % b] = ("psum", [128, 512], F32)
     return s
@@ -56,14 +62,14 @@ def build(g, core, T, topo, rank, costs):
     N = len(T.cores)
     nxt, prv = T.cores[(rank + 1) % N], T.cores[(rank - 1) % N]
     ops = []
-    nd, phase = [0], ["c", {}]
+    nd, phase = [0], ["c", {}, -1]
     ps = [T["ps%d" % b] for b in range(8)]
 
     def add(e, f, r, w, c, banks=(), **kw):
         nm = e + "".join(x for x in w[0] if not x.isdigit())
         phase[1][nm] = phase[1].get(nm, 0) + 1
         o = dict(e=e, f=f, r=list(r) + ([] if e == "P" else ["B%d" % b for b in banks]), w=list(w), c=c, b=tuple(banks),
-                 i=len(ops), nm="%s%d%s" % (nm, phase[1][nm], phase[0]))
+                 i=len(ops), step=phase[2], nm="%s%d%s" % (nm, phase[1][nm], phase[0]))
         o.update(kw)
         ops.append(o)
 
@@ -77,7 +83,7 @@ def build(g, core, T, topo, rank, costs):
         add("S", f, r, w, cost(n, 18), banks)
 
     def P(mms, r, w, banks, grp=False, given=False):
-        if CFG["CUT"] and len(mms) > 1 and sum(m[5] for m in mms) > CFG["CUT"]:
+        if CFG["CUT"] and len(mms) > 1 and sum(m[5] for m in mms) > CFG["CUT"] and w[0] not in CFG["WHOLE"]:
             if not (grp or given):
                 mms = [m[:4] + (n + 1 == len(mms) or mms[n + 1][3], m[5]) for n, m in enumerate(mms)]
             part, tot = [], 0
@@ -156,13 +162,13 @@ def build(g, core, T, topo, rank, costs):
     dma("Y", T.wx0[:, 256:512], T.x0[:], [], ["xb0"], 65536)
     dma("Y", T.edgi[:], T.edge0[:], [], ["edgi"], 524288)
     dma("Y", T.veri[:], T.ver0[:], [], ["veri"], 524288)
-    dma("Y", T.R[:, 0:4096], T.rec0[:], [], ["R"], 1048576)
     dma("Y", T.ef0[:], T.eff[:], [], ["ef0"], 131072)
+    dma("Y", T.R[:, 0:4096], T.rec0[:], [], ["R"], 1048576)
 
     io, cf, cb, ii = T.io_f, T.cf, T.cb, T.io_i
     col = lambda j: cf[:, j:j + 1]
     partf, pf, gf, p7, wl, wh, offp, wt, bT_, bV_, x2s, nwt, nwl, nwh, p4, pf1 = [col(j) for j in range(16)]
-    cm_, p32 = col(128), cb[:, 2:3]
+    cm_, p32, k4, nk4 = col(128), cb[:, 2:3], col(129), col(130)
     add("G", lambda: g.iota(ii[:, 0:1], [[0, 1]], 0, 1), [], ["ii0"], 132)
     F128, CG, DI, HI, C16, H16 = (io[:, 0:128], io[:, 128:256], io[:, 256:528], io[:, 528:544], io[:, 544:672],
                                   io[:, 672:688])
@@ -181,6 +187,7 @@ def build(g, core, T, topo, rank, costs):
     cp(p32, ii[:, 4:5], ["ii4"], ["p32"], 1)
     ts(cm_, p7, gf, A.is_equal, ["pg"], ["cm_"], 1)
     for ap, nm, src, sc_, bi in ((wt, "wt", pf, 2.0, 1.0), (nwt, "nwt", pf, -2.0, -1.0), (pf1, "pf1", pf, 1.0, 1.0),
+                                 (k4, "k4", pf, 4096.0, 0.0), (nk4, "nk4", pf, -4096.0, 0.0),
                                  (bT_, "bT_", partf, -FALL, TOP + math.log(THR)), (bV_, "bV_", pf, -FALL, TOP + math.log(1.5))):
         act(ap, src, F.Identity, ["pg"], [nm], 1, bias=bi, scale=sc_)
     ts(offp, pf, 0.0, A.is_equal, ["pg"], ["offp0"], 1, -65536.0, A.mult)
@@ -209,14 +216,15 @@ def build(g, core, T, topo, rank, costs):
     iota(M4, [[0, 256]], ["M4"], 256, base=3 * 2 ** 19)
     iota(M2p, [[0, 16]], ["M2p"], 16, base=3 * 2 ** 18)
     KC, K17, EC, JC = CK[0:32, 0:256], CK[0:32, 256:272], CK[0:2, 272:528], CK[0:32, 528:656]
-    iota(KC, [[0, 16], [128, 16]], ["KC"], 256)
     iota(K17, [[0, 16]], ["K17"], 16, base=31 * 2 ** 16)
-    iota(EC, [[0, 256]], ["EC"], 256, base=85, cm=21760 - 85)
+    if CFG["EB"]:
+        iota(KC, [[0, 256]], ["KC"], 256)
+        iota(EC, [[0, 256]], ["EC"], 256, base=85, cm=21760 - 85)
     iota(JC, [[0, 8], [-2, 16]], ["JC"], 128, base=-15)
     iota(T.Q0[:], [[1, 32], [0, 16]], ["Q00", "Q01"], 512)
     ts(T.REP[:], T.Q0[:], p32, A.is_equal, ["Q00", "Q01", "p32"], ["REP"], 256)
     iota(T.QZ[:, 0:512], [[0, 512]], ["QZa"], 512)
-    dma("Y", T.QZ[:, 512:1024], T.QZ[:, 0:512], ["QZa"], ["QZb"], 131072)
+    dma("Y", T.QZ[:, 512:1024], T.QZ[:, 0:512], ["QZa", "ef0", "R"], ["QZb"], 131072)
     for k in range(1, 4):
         dma("Y", T.QZ[:, 1024 * k:1024 * k + 1024], T.QZ[:, 0:1024], ["QZa", "QZb"], ["QZc%d" % k], 262144)
     add("X", None, ["QZa", "QZb", "QZc1", "QZc2", "QZc3"], ["QZ"], 1, join=True)
@@ -270,10 +278,18 @@ def build(g, core, T, topo, rank, costs):
         ts(ID, io[:, 0:32], 16.0, A.mult, ["F128", "pg"], ["ID"], 32, pf, A.add)
     X4 = cu[:, 24:48]
     ts(X4, H3, x2s, A.add, ["H3", "x2s", "cm_"], ["X4"], 24, cm_, A.mult)
-    iota(T.fb[:], [[0, 192]], ["clT", "nmT", "ngT", "nfT", "thrW", "hl"], 192)
+    iota(T.fb[:], [[0, 192]], ["clT", "thrW", "hl"], 192)
+    for t in range(NS):
+        iota(T["l2_%d" % t][:, 0:16], [[0, 16]], ["lz%d" % t], 16)
     iota(zer, [[0, 16]], ["zer"], 16)
     for h in range(2):
         ts(T.SR[:, 128 * h:128 * h + 128], CG, float(8 * h), A.add, ["CG", "pg"], ["SR%d" % h], 128, pf, A.is_equal)
+    if CFG["TT"] == "V":
+        for k in range(2):
+            dma("Y", T.SQ[:, 512 * k:512 * k + 512], T.QZ[:, 0:512], ["QZa"], ["SQz%d" % k], 131072)
+        for a in range(4):
+            dma("Y", T.SQ[32 * a:32 * a + 32, 256 * a:256 * a + 256], T.SR[32 * a:32 * a + 32, :],
+                ["SR0", "SR1", "SQz0", "SQz1"], ["SQ%d" % a], 16384)
     iota(T.R[:, 4096:4112], [[0, 16]], ["R5"], 16, base=5)
     copy(CFG["CVT"], T.SU[:, 0:1024], T.edgi[:], ["edgi"], ["SU0"], 1024)
     for k in range(1, 4):
@@ -292,13 +308,13 @@ def build(g, core, T, topo, rank, costs):
     lfGM, dn, tn = sf[:, 224:272], sf[:, 160:192], sf[:, 192:224]
     wWi, bWi, keyT, hiT, loT, vWi = [si[:, 16 * j:16 * j + 16] for j in range(6)]
     wl_, ul, sel, lG, lM, lF, vm0 = [su[:, 16 * j:16 * j + 16] for j in (2, 4, 5, 6, 7, 8, 10)]
-    clT, ngT, nmT, nfT, thrW, hl = fb[:, 16:32], fb[:, 48:64], fb[:, 64:80], fb[:, 80:96], fb[:, 128:144], fb[:, 160:192]
-    alias = {5: ["TT", "Sc", "pS", "pG"], 6: ["uR"]}
+    clT, thrW, hl = fb[:, 16:32], fb[:, 128:144], fb[:, 160:192]
+    alias = {5: ["TT", "Sc", "pS", "pG"], 6: ["uR"], 1: ["wR", "pb"], 0: ["pY", "pB"]}
 
     cp(T.v8f[0:8, :], T.v8i[0:8, :], ["v8i"], ["v8f"], 256)
     P([(ps[1][:, 0:256], T.cI32[0:8, 384:512], T.v8f[0:8, :], True, True, 1024)], ["SB", "v8f"], ["wR"], [1])
     scan(T.sc2[:], ps[1][:, 0:256], T.CS[:], 32768.0, A.min, A.add, ["wR", "CS"], ["sc20", "sc21"], 256, [1])
-    cp(T.vR0[:], ps[1][:, 0:256], ["wR"], ["vR_0"], 256, [1])
+    cp(T.vR0[:], ps[1][:, 0:256], ["wR"], ["vR"], 256, [1])
     ts(vWi, T.sc2[:, 15:256:16], offp, A.add, ["sc20", "sc21", "offp"], ["vWi"], 16)
     cp(su[:, 176:192], vWi, ["vWi"], ["vW0"], 16)
     cp(vWf, vWi, ["vWi"], ["vWf"], 16)
@@ -310,27 +326,34 @@ def build(g, core, T, topo, rank, costs):
         return 128 * (c // 8) + (0 if q < 4 else 64 if q < 6 else 96)
 
     def split(kb, keyW, keyWn, nm):
-        act(kb[0], keyW, F.Identity, [keyWn], [nm + "h"], 16)
+        copy(CFG["KB"], kb[0], keyW, [keyWn], [nm + "h"], 16)
         tt(kb[1], keyW, kb[0], A.subtract, [keyWn, nm + "h"], [nm + "l"], 32)
 
     def zcalls(Z, nm, keyR, keyRn, buf, o, kn, more=()):
         for c in range(16):
             s = zstart(c)
             ts(Z[:, 256 * c + s:256 * c + 256], keyR[:, s:256], buf[:, o + c:o + c + 1], A.subtract,
-               [keyRn] + kn + list(more), ["%s%d" % (nm, c)], (256 - s) // 2, buf[:, o + 16 + c:o + 17 + c], A.is_equal)
+               [keyRn] + kn + list(more) * (c < CFG["UL"]), ["%s%d" % (nm, c)], (256 - s) // 2, buf[:, o + 16 + c:o + 17 + c], A.is_equal)
 
-    def zsum(Z, nm, wsel, wn, bk, o, on, cs, first, last, grp=False):
+    def zsum(Z, nm, wsel, wn, bk, o, on, cs, first, last, grp=False, only=None):
         mms = []
         if first:
             mms.append((ps[bk][:, o:o + 16], ONE[32:64, 0:128], cb[32:64, 32:48], True, False, 64))
         for c in cs:
             s = zstart(c)
             for h in range(c // 8, 2):
+                if only is not None and only != (h > c // 8):
+                    continue
                 lo = max(s, 128 * h)
                 at = 8 * c + (128 if h > c // 8 else 0)
                 mms.append((ps[bk][lo - 128 * h:128, o + 8 * h:o + 8 * h + 8], Z[:, 256 * c + lo:256 * c + 128 * h + 128],
                             wsel[:, at:at + 8], False, last and c == 0 and h == 1, min(64, 128 * h + 128 - lo)))
         P(mms, ["%s%d" % (nm, c) for c in cs] + wn + ["ONE", "zer"], [on], [bk], grp, True)
+
+    def firsts(buf, o, kn, out, on, row=T.vR0, rown="vR"):
+        zcalls(T.Zv, "Zv", row, rown, buf, o, kn)
+        zsum(T.Zv, "Zv", T.M2, ["WSV"], 7, 64, "Sv", range(15, -1, -1), True, True)
+        ts(out, ps[7][:, 64:80], thr, A.is_ge, ["Sv", "thr"], [on], 16, banks=[7])
 
     def toW(xp, bk, o, n=16, st=16, at=0, first=False):
         return [(ps[bk][:, o:o + n], T.L8[:, 128 * k:128 * k + 128], xp[:, st * k + at:st * k + at + n], first and k == 0,
@@ -342,16 +365,17 @@ def build(g, core, T, topo, rank, costs):
     for t in range(NS):
         par, u = t % 2, t + 1
         phase[0] = "a" if t == 0 else "z" if t == NS - 1 else "m"
-        phase[1] = {}
+        phase[1], phase[2] = {}, t
         wx = T["wx%d" % t]
         xb, xn = wx[:, 256:512], "xb%d" % t
         jb, nj, jn, njn = T["jm%d" % par], T["nj%d" % par], "jm%d" % par, "nj%d" % par
         vW, vWn = su[:, 176 + 16 * par:192 + 16 * par], "vW%d" % par
         if t == 0:
-            vR, vRn, vkb, vo, vkn = T.vR0, "vR_0", T.kb, 64, ["Zvh", "Zvl"]
+            vkb, vo, vkn = T.kb, 64, ["Zvh", "Zvl"]
             split((T.kb[:, 64:80], T.kb[:, 80:96]), vWf, "vWf", "Zv")
+            firsts(vkb, vo, vkn, T.l2_0[:, 48:64], "nf_0")
         else:
-            vR, vRn, vkb, vo, vkn = T["l2_%d" % t], "vR_%d" % t, wx, 512, [xn]
+            vkb, vo, vkn = wx, 512, [xn]
             P(addkey(7, 32, wx, 512, True), ["Ib", xn], ["pV"], [7])
             cp(vW, ps[7][:, 32:48], ["pV"], [vWn], 16, [7])
 
@@ -359,8 +383,11 @@ def build(g, core, T, topo, rank, costs):
             o, x, n = ps[bk][:, at:at + hi - lo], xbuf[:, xo + lo:xo + hi], hi - lo
             P([(o, JC, MK[0:32, 512:512 + n], True, False, n), (o, WT, x, False, False, n),
                (o, ON32, MK[0:32, 0:n], False, False, n), (o, NE32, MK[0:32, 0:n], False, False, n), (o, WTn, x, False, True, n)],
-              ["JC", "H64", "ONE", "NEG", "WT", "WTn", "MJ", xname], [pn], [bk])
-            act(out, o, F.Relu, [pn, "pf1"], [on], n, bias=pf1, banks=[bk])
+              ["JC", "H64", "ONE", "NEG", "WT", "WTn", "MJ", xname] + (["K1"] if lo and CFG["H1"] else []), [pn], [bk])
+            if CFG["JM"] == "V" and n < 128:
+                ts(out, o, pf1, A.add, [pn, "pf1"], [on], n, 0.0, A.max, banks=[bk])
+            else:
+                act(out, o, F.Relu, [pn, "pf1"], [on], n, bias=pf1, banks=[bk])
 
         def nextx(o, on, bk, ef, efn, out, outn):
             P([(o, In, xb, True, False, 256), (o, In, ef, False, False, 256), (o, ON32, M4, False, False, 256),
@@ -394,16 +421,12 @@ def build(g, core, T, topo, rank, costs):
         if CFG["TP"] == "V":
             act(nj[:], jm, F.Identity, jns, [njn], 256, bias=1.0, scale=-1.0)
         ts(wl_, wWi, 4096.0, A.min, pn("wWi"), ["wl_"], 16)
-        cp(bWf, bWi, pn("bWi"), ["bWf"], 16)
         verK, vk = T.VD[:, 0:256], ["VD"]
         for a, b in CFG["VT"]:
             cp(T.VT[:, 16 * a:16 * b], VLw.indirect(su[:, a:b]),
                [VLn] + ["bla%d" % k for k, (c, d) in enumerate(parts) if c < b and a < d],
                ["VT%d" % q for q in range(a // 2, b // 2)], (16 * (b - a), GA))
-        if CFG["VD"] == "C" or t == 0:
-            cp(verK, T.VT[:], ["VT%d" % q for q in range(8)], vk, 256)
-        else:
-            act(verK, VLw.indirect(su[:, 0:16]), F.Identity, [VLn] + pn("bla"), vk, (256, GA))
+        ts(verK, T.VT[:], k4, A.add, ["k4"] + ["VT%d" % q for q in range(8)], vk, 256)
         P([(ps[2][:, 256 + 128 * h:384 + 128 * h], wx[:, 256 + 128 * h:384 + 128 * h], Ib, True, True, 128) for h in range(2)],
           ["Ib", xn], ["pXT"], [2])
         act(T.xc[:], ps[2][:, 256:512], F.Exp, ["pXT"], ["xc"], 256, bias=-9 * LN256, scale=LN256, banks=[2])
@@ -415,17 +438,19 @@ def build(g, core, T, topo, rank, costs):
             P([(ps[1][:, 256:512], BO, T.G[:], True, True, 1024), (ps[1][:, 256:512], In, T.Qb[:], False, True, 256)],
               ["In", "BO"] + pn("G") + pn("Qb"), ["pb"], [1])
             ts(T.bR[:], ps[1][:, 256:512], 196608.0, A.add, ["pb"], ["bR"], 256, banks=[1])
-        zcalls(T.Zv, "Zv", vR, vRn, vkb, vo, vkn)
-        split((T.kb[:, 0:16], T.kb[:, 16:32]), bWf, "bWf", "Zb")
-        zcalls(T.Zb, "Zb", T.bR, "bR", T.kb, 0, ["Zbh", "Zbl"], ["Zv15"] if CFG["ZO"] else [])
-        zsum(T.Zv, "Zv", T.M2, ["WSV"], 7, 64, "Sv", range(15, -1, -1), True, True)
-        ts(nfT, ps[7][:, 64:80], thr, A.is_ge, ["Sv", "thr"], ["nfT"], 16, banks=[7])
+        cp(T.kb[:, 0:16], bWi, pn("bWi"), ["Zbh"], 16)
+        tt(T.kb[:, 16:32], bWi, T.kb[:, 0:16], A.subtract, pn("bWi") + ["Zbh"], ["Zbl"], 32)
+        zcalls(T.Zb, "Zb", T.bR, "bR", T.kb, 0, ["Zbh", "Zbl"])
+        if t and not CFG["ZS"]:
+            firsts(vkb, vo, vkn, T["l2_%d" % t][:, 48:64], "nf_%d" % t, T["l3_%d" % t], "vR_%d" % t)
+        l2 = T["l2_%d" % t]
+        ngT, nmT = l2[:, 16:32], l2[:, 32:48]
         nextx(ps[0][:, 256:512], "pB", 0, T.EF[:, t:4096:16], "EF", T.xJ[:, 256:512], "xB")
         if CFG["JS"] and u < NS:
             jmask(T.xJ[:, 768:1024], "jB", T.xJ, 256, "xB")
         copy(CFG["GS"], T.ws[:, 0:256], T.SU[:, t:4096:16], ["SU"], ["ws0"], 256)
         iota(T.wv[:, 256:512], [[16, 256]], ["wv1"], 256, base=t)
-        dma("Y", T.wm[:, 256:512], DG[:, t:t + 256], ["DG"], ["wm1"], 65536)
+        dma("Y", T.wm[:, 256:512], DG[:, t:t + 256], ["DG"] + ["R"] * (t == 0), ["wm1"], 65536)
         EB = CFG["EB"]
         kbk, ko, kn = ((3, 4), (0, 0), ("K0", "K1")) if EB else ((3, 3), (0, 128), ("K0", "K0"))
         o17 = 384 if EB else 256
@@ -436,10 +461,7 @@ def build(g, core, T, topo, rank, costs):
                    (ps[3 + h][:, 128:384], ONE[0:2, 0:128], EC, False, False, 256)] + [(p17, ON32, K17, False, False, 64)] * h,
                   ["ONE", "KC", "K17", "EC"], [kn[h]], [3 + h], True)
         else:
-            P([(ps[3][:, 0:256], ON32, KC, True, False, 256), (p17, ON32, K17, False, False, 64)],
-              ["ONE", "KC", "K17"], ["K0"], [3], True)
-            P([(ps[4][:, 256 * h:256 * h + 256], ONE[0:2, 0:128], EC, h == 0, False, 256) for h in range(2)],
-              ["ONE", "EC"], ["K1"], [4], True)
+            P([(p17, ON32, K17, True, False, 64)], ["ONE", "K17"], ["K0"], [3], True)
         act(T.old[:, 4096:4352], T.R[:, 0:4112].indirect(wl_), F.Exp, ["R", "R5", "wl_"], ["oldw"], (256, GA),
             bias=-9 * LN256, scale=LN256)
         tt(T.eq[:, 4096:4352], ps[2][:, 0:256], T.old[:, 4096:4352], A.is_equal, ["pX", "oldw"], ["eqw"], 256, [2])
@@ -455,7 +477,7 @@ def build(g, core, T, topo, rank, costs):
               vk + ["If"], [kn[h]], [kbk[h]], True)
 
         def keys(src, sn, h, lo, hi, stop=False):
-            names = [sn + str(q) for q in range(4 * h + lo // 32, 4 * h + hi // 32)]
+            names = [sn + str(q) for q in range(4 * h + lo // 32, 4 * h + hi // 32)] + [sn + "7a"] * (h == 1 and hi == 128)
             m = 3 if EB and sn == "eq" else 1
             for k0 in (0, 8):
                 P([(ps[kbk[h]][lo:hi, ko[h] + k:ko[h] + 128 * m:16], src[:, 2048 * h + 16 * lo + k:2048 * h + 16 * hi:16],
@@ -464,21 +486,32 @@ def build(g, core, T, topo, rank, costs):
 
         for q in range(8):
             cs = slice(512 * q, 512 * q + 512)
-            h, a, bk = q // 4, q % 4, 5 + q % 2
-            act(T.old[:, cs], T.R[:, 0:4096].indirect(T.VT[:, 32 * q:32 * q + 32]), F.Exp, ["R", "VT%d" % q],
-                ["old%d" % q], (512, GA), bias=-9 * LN256, scale=LN256)
-            P([(ps[bk][:], T.xc[32 * a:32 * a + 32, 128 * h:128 * h + 128], T.REP[32 * a:32 * a + 32, :], True, True,
-                512 // CFG["DUP"])] * CFG["DUP"], ["xc", "REP"], alias[bk], [bk])
-            tt(T.eq[:, cs], ps[bk][:], T.old[:, cs], A.is_equal, alias[bk] + ["old%d" % q], ["eq%d" % q], 512, [bk])
+            h, a, bk = q // 4, q % 4, CFG["XB"][q]
+            if q == 7:
+                P([(ps[bk][:], T.xc[96:128, 128:256], T.REP[96:128, :], True, True, 512)], ["xc", "REP"], alias[bk], [bk])
+                for k, nm in enumerate(("7a", "7")):
+                    c2 = slice(3584 + 256 * k, 3840 + 256 * k)
+                    act(T.old[:, c2], T.R[:, 0:4096].indirect(T.VT[:, 224 + 16 * k:240 + 16 * k]), F.Exp, ["R", "VT7"],
+                        ["old" + nm], (256, GA), bias=-9 * LN256, scale=LN256)
+                    tt(T.eq[:, c2], ps[bk][:, 256 * k:256 * k + 256], T.old[:, c2], A.is_equal, alias[bk] + ["old" + nm],
+                       ["eq" + nm], 256, [bk])
+            for lo, hi in CFG["OLD"]:
+                if lo == q < 7:
+                    act(T.old[:, 512 * lo:512 * hi], T.R[:, 0:4096].indirect(T.VT[:, 32 * lo:32 * hi]), F.Exp,
+                        ["R"] + ["VT%d" % j for j in range(lo, hi)], ["old%d" % j for j in range(lo, hi)], (512 * (hi - lo), GA),
+                        bias=-9 * LN256, scale=LN256)
+            if q < 7:
+                P([(ps[bk][:], T.xc[32 * a:32 * a + 32, 128 * h:128 * h + 128], T.REP[32 * a:32 * a + 32, :], True, True, 512)],
+                  ["xc", "REP"], alias[bk], [bk])
+                tt(T.eq[:, cs], ps[bk][:], T.old[:, cs], A.is_equal, alias[bk] + ["old%d" % q], ["eq%d" % q], 512, [bk])
             if q == 3:
                 keys(T.old, "old", 0, 0, 128)
                 keys(T.eq, "eq", 0, 0, 128, EB)
                 P(key17[0], key17[1], [kn[1]], [kbk[1]], True)
-            if CFG["KT"] == 2 and q == 6:
-                keys(T.old, "old", 1, 0, 64)
-                keys(T.old, "old", 1, 64, 96)
-            if CFG["KT"] and q in (5, 6):
-                keys(T.eq, "eq", 1, *((0, 64) if q == 5 else (64, 96)))
+            if CFG["KT"] and q == 6:
+                if CFG["KT"] == 2:
+                    keys(T.old, "old", 1, 0, 96)
+                keys(T.eq, "eq", 1, 0, 96)
             if q == 7:
                 keys(T.old, "old", 1, 96 if CFG["KT"] == 2 else 0, 128)
                 if CFG["KT"]:
@@ -488,9 +521,9 @@ def build(g, core, T, topo, rank, costs):
                     keys(T.eq, "eq", 1, 0, 128, True)
             if a == 3 and not EB:
                 for lo in (0, 8):
-                    P([(ps[4][:, 256 * h + k:256 * h + 256:16], T.eq[:, 2048 * h + k:2048 * h + 2048:16], cW[:, 392:408], False,
-                        False, 64) for k in range(lo, lo + 8)],
-                      ["eq%d" % j for j in range(q - 3, q + 1)] + ["WKE1", "WKE2"], ["K1"], [4], True)
+                    P([(ps[4][:, 256 * h + k:256 * h + 256:16], T.eq[:, 2048 * h + k:2048 * h + 2048:16], cW[:, 392:408],
+                        h == 0 and k == 0, False, 64) for k in range(lo, lo + 8)],
+                      ["eq%d" % j for j in range(q - 3, q + 1)] + ["eq7a"] * h + ["WKE1", "WKE2"], ["K1"], [4], True)
         if EB:
             for h in range(2):
                 scan(T.sc2[:, 128 * h:128 * h + 128], T.MS[:, 0:128], ps[3 + h][:, 0:128], 0.0, A.add, A.min, ["MS", kn[h]],
@@ -508,12 +541,14 @@ def build(g, core, T, topo, rank, costs):
                for h in range(2)], ["SR0", "SR1", "TTs"], ["uR"], [6])
         else:
             V(lambda: g.vector.transpose(T.TTs[:, 0:32], hl), ["hl"], ["TTs"], 16)
-            P([(ps[6][:, 128 * h + 32 * a:128 * h + 32 * a + 32], T.SR[32 * a:32 * a + 32, 128 * h:128 * h + 128],
-                T.TTs[32 * a:32 * a + 32, 0:32], True, True, 64) for h in range(2) for a in range(4)],
-              ["SR0", "SR1", "TTs"], ["uR"], [6])
+            P([(ps[6][:, 128 * h + 32 * a:128 * h + 32 * a + 32], T.SQ[:, 256 * a + 128 * h:256 * a + 128 * h + 128],
+                T.TTs[:, 0:32], True, True, 64) for h in range(2) for a in range(4)],
+              ["SQ0", "SQ1", "SQ2", "SQ3", "TTs"], ["uR"], [6])
         cp(T.cR[:], ps[6][:, 0:256], ["uR"], ["cR"], 256, [6])
         act(T.wv[:, 0:256], ps[6][:, 0:256], F.Identity, ["uR"], ["wv0"], 256, banks=[6])
-        spread(CFG["XQ"], T.xq[:], fb[:, 144:192], X3, 1.0, ["hl", "X3"], ["xq"], 256)
+        ts(thrW, keyT, KD, A.is_ge, ["keyT", "thr"], ["thrW"], 16, thr, A.mult)
+        spread(CFG["XW"], T.xw[:], fb[:, 112:144], X2, 1 / THR, ["thrW", "X2"], ["xw"], 128)
+        spread(CFG["XQ"], T.xq[:], fb[:, 144:192], X3, 1.0, ["hl", "X3"] + ["xw"] * CFG["H2"], ["xq"], 256)
         P(toW(T.xq, 7, 96, 32, 32, 0, True), ["xq", "L8"], ["pH"], [7])
         if CFG["ZC"] == "S":
             act(T.kb[:, 32:64], ps[7][:, 96:128], F.Identity, ["pH"], ["Zch"], 32, banks=[7])
@@ -524,19 +559,20 @@ def build(g, core, T, topo, rank, costs):
         else:
             P(toW(T.xq, 7, 0, 16, 32, 0, True) + toW(T.xq, 7, 0, 16, 32, 16), ["xq", "L8"], ["pU"], [7])
         cp(ul, ps[7][:, 0:16], ["pU"], ["ul"], 16, [7])
-        ts(thrW, keyT, KD, A.is_ge, ["keyT", "thr"], ["thrW"], 16, thr, A.mult)
         tt(hardT, keyT, thrA, A.is_ge, ["keyT", "thrA"], ["hardT"], 32)
         tt(thrC, thrW, hardT, A.mult, ["thrW", "hardT"], ["thrC"], 32)
-        spread(CFG["XW"], T.xw[:], fb[:, 112:144], X2, 1 / THR, ["thrW", "X2"], ["xw"], 128)
         P([(ps[0][:, k:128:8], T.L8[:, 128 * k:128 * k + 128], T.xw[:, 16 * k:16 * k + 16], True, True, 64)
            for k in range(8)], ["L8", "xw"], ["pY"], [0])
         act(T.wsel[:, 0:128], ps[0][:, 0:128], F.Identity, ["pY"], ["wsel"], 128, banks=[0])
-        act(T.wsel[:, 192:256], ps[0][:, 0:64], F.Sign, ["pY"], ["wsel1"], 64, banks=[0])
-        act(T.wsel[:, 128:192], T.wsel[:, 192:256], F.Identity, ["wsel1"], ["wsel2"], 64, scale=BIG)
+        if CFG["WS"] == "V":
+            ts(T.wsel[:, 128:192], T.wsel[:, 0:64], 0.0, A.is_gt, ["wsel"], ["wsel2"], 32, BIG, A.mult)
+        else:
+            act(T.wsel[:, 192:256], T.wsel[:, 0:64], F.Sign, ["wsel"], ["wsel1"], 64)
+            act(T.wsel[:, 128:192], T.wsel[:, 192:256], F.Identity, ["wsel1"], ["wsel2"], 64, scale=BIG)
         wsn = ["wsel", "wsel2"]
-        zsum(T.Zb, "Zb", T.wsel, wsn, 5, 288, "Sc", range(15, 7, -1), True, False, True)
-        zsum(T.Zb, "Zb", T.wsel, wsn, 5, 288, "Sc", range(7, -1, -1), False, False, True)
-        zcalls(T.Zc, "Zc", T.cR, "cR", T.kb, 32, ["Zch"])
+        zsum(T.Zb, "Zb", T.wsel, wsn[:1], 5, 288, "Sc", range(15, -1, -1), True, False, True, False)
+        zsum(T.Zb, "Zb", T.wsel, wsn, 5, 288, "Sc", range(7, -1, -1), False, False, True, True)
+        zcalls(T.Zc, "Zc", T.cR, "cR", T.kb, 32, ["Zch"], ["ul"])
         for cs in (range(15, 5, -1), range(5, 1, -1), (1,), (0,)):
             zsum(T.Zc, "Zc", T.wsel, wsn, 5, 288, "Sc", cs, False, True, True)
         tt(clT, ps[5][:, 288:304], thrC, A.is_lt, ["Sc", "thrC"], ["clT"], 16, [5])
@@ -544,11 +580,18 @@ def build(g, core, T, topo, rank, costs):
         spread(CFG["XL"], T.xl[:], fb[:, 0:32], X2, 8192.0, ["clT", "X2"], ["xl"], 128)
         P([(ps[5][:, 320:336], Ib, iWb, True, False, 64)] + toW(T.xl, 5, 320), ["Ib", "iWb", "xl", "L8"], ["pS"], [5])
         ts(sel, ps[5][:, 320:336], 1 / 32, A.mult, ["pS"], ["sel"], 16, banks=[5])
-        act(T.efu[:], T.EF[:].indirect(ul), F.Identity, ["EF", "ul"], ["efu"], (256, GA))
-        nextx(ps[1][:, 0:256], "wR", 1, T.efu[:], "efu", T.xJ[:, 0:256], "xA")
+        if CFG["XA"] == "V":
+            tt(T.efu[:], T.EF[:].indirect(ul), xb, A.add, ["EF", "ul", xn], ["efu"], (256, GA))
+            ts(T.rc[:], T.efu[:], 2.0, A.is_ge, ["efu"], ["rc"], 128, -4.0, A.mult)
+            P([(ps[1][:, 0:256], Ib, T.efu[:], True, False, 256), (ps[1][:, 0:256], Ib, T.rc[:], False, True, 256)],
+              ["Ib", "efu", "rc"], ["wR"], [1])
+            act(T.xJ[:, 0:256], ps[1][:, 0:256], F.Identity, ["wR"], ["xA"], 256, bias=1.5, banks=[1])
+        else:
+            act(T.efu[:], T.EF[:].indirect(ul), F.Identity, ["EF", "ul"], ["efu"], (256, GA))
+            nextx(ps[1][:, 0:256], "wR", 1, T.efu[:], "efu", T.xJ[:, 0:256], "xA")
         if u < NS:
             s1, s2 = T["s1_%d" % u], T["s2_%d" % u]
-            act(s1[:, 0:256], T.xJ[:, 0:512].indirect(sel), F.Identity, ["xA", "xB", "sel"], ["s1_%d" % u], (256, GA))
+            spread(CFG["S1"], s1[:, 0:256], T.xJ[:, 0:512], sel, 1.0, ["xA", "xB", "sel"], ["s1_%d" % u], 256)
             iota(cf[:, 160:176], [[0, 16]], ["nL"], 16, base=t)
             tt(dn, nHL, T.kb[:, 32:64], A.subtract, ["nH", "nL", "Zch"], ["dn"], 64)
             ts(clW, ps[5][:, 320:336], 8192.0, A.is_ge, ["pS"], ["clW"], 16, banks=[5])
@@ -564,9 +607,15 @@ def build(g, core, T, topo, rank, costs):
             recv(prv, "a1_%d" % u, ["m1_%d" % u], ["xb%d" % u])
         act(T.vnR[:], T.wv[:].indirect(sel), F.Identity, ["wv0", "wv1", "sel"], ["vnR"], (256, GA))
         if u < NS:
-            cp(s2[:], T.vnR[:], ["vnR"], ["s2_%d" % u], 256)
-            send(nxt, T["l2_%d" % u][:], s2[:], "a2_%d" % u, ["s2_%d" % u], ["m2_%d" % u])
-            recv(prv, "a2_%d" % u, ["m2_%d" % u], ["vR_%d" % u])
+            if CFG["ZS"]:
+                cp(T.vR0[:], T.vnR[:], ["vnR"], ["vR"], 256)
+                firsts(s1, 256, ["s1v%d" % u], s2[:], "s2_%d" % u)
+                send(nxt, T["l2_%d" % u][:, 48:64], s2[:], "a2_%d" % u, ["s2_%d" % u], ["m2_%d" % u])
+                recv(prv, "a2_%d" % u, ["m2_%d" % u], ["nf_%d" % u])
+            else:
+                cp(T["s3_%d" % u][:], T.vnR[:], ["vnR"], ["s2_%d" % u], 256)
+                send(nxt, T["l3_%d" % u][:], T["s3_%d" % u][:], "a2_%d" % u, ["s2_%d" % u], ["m2_%d" % u])
+                recv(prv, "a2_%d" % u, ["m2_%d" % u], ["vR_%d" % u])
         else:
             home, frm = T.cores[(rank - t) % N], T.cores[(rank + t) % N]
             act(T.xh[:], T.xJ[:, 0:512].indirect(sel), F.Identity, ["xA", "xB", "sel"], ["xh"], (256, GA))
@@ -577,17 +626,28 @@ def build(g, core, T, topo, rank, costs):
             dma("Y", T.yx[:], T.lx[:], ["lx"], ["yx"], 65536)
             dma("Y", T.yv[:], T.lv[0:128:16, :], ["lv"], ["yv"], 8192)
         tt(ngT, nmT, clT, A.add, ["nmT", "clT"], ["ngT"], 32)
-        spread(CFG["XM"], T.xg[:], fb[:, 32:96], X4, 8192.0, ["nmT", "ngT", "nfT", "X4"], ["xg"], 384)
+        spread(CFG["XM"], T.xg[:], l2[:], X4, 8192.0, ["nmT", "ngT", "nf_%d" % t, "lz%d" % t, "X4"], ["xg"], 384)
         P(addkey(5, 368, vkb, vo, True) + addkey(5, 352, T.kb, 0) + addkey(5, 336, T.kb, 32) + toW(T.xg, 5, 336, 48, 48),
           ["Ib", "Zbh", "Zbl", "Zch", "xg", "L8"] + vkn, ["pG"], [5])
         tt(lfGM, ps[5][:, 336:384], cf[:, 64:112], A.min, ["pG", "DW0", "DW1", "DW2"], ["lfGM"], 48, [5])
         cp(su[:, 96:144], lfGM, ["lfGM"], ["lGM"], 48)
         act(T.ws[:, 256:512], T.SU[:, 0:4096].indirect(ul), F.Identity, ["SU", "ul"], ["ws1"], (256, GA), bias=4096.0)
         act(T.SU[:, t:4096:16], T.ws[:].indirect(sel), F.Identity, ["ws0", "ws1", "sel"], ["SU"], (256, GA))
-        if CFG["TP"] == "V":
+        if CFG["TP"] == "S":
             P([(ps[7][:, 256:512], If, T.vnR[:], True, False, 1024), (ps[7][:, 256:512], I8k, jm, False, True, 256)],
               ["If", "I8k", "vnR"] + jns, ["pC"], [7])
             act(T.u2[:], ps[7][:, 256:512], F.Relu, ["pC"], ["u2"], 256, bias=-8192.0, banks=[7])
+            act(T.sv[:], T.SU[:, 0:4096].indirect(vW), F.Identity, ["SU", vWn], ["sv"], (256, GA), scale=0.25)
+            P([(ps[0][:, 256:512], In8, jm, True, False, 256), (ps[0][:, 256:512], If, T.sv[:], False, True, 1024)],
+              ["If", "In8", "sv"] + jns, ["pB"], [0])
+            act(T.tp[:], ps[0][:, 256:512], F.Relu, ["pB"], ["tp"], 256, scale=4.0, banks=[0])
+        elif CFG["TP"] == "V":
+            if u == NS and CFG["TZ"] == 2:
+                tt(T.u2[:], T.vnR[:], jm, A.mult, ["vnR"] + jns, ["u2"], 512)
+            else:
+                P([(ps[7][:, 256:512], If, T.vnR[:], True, False, 1024), (ps[7][:, 256:512], I8k, jm, False, True, 256)],
+                  ["If", "I8k", "vnR"] + jns, ["pC"], [7])
+                act(T.u2[:], ps[7][:, 256:512], F.Relu, ["pC"], ["u2"], 256, bias=-8192.0, banks=[7])
             tt(T.tp[:], T.SU[:, 0:4096].indirect(vW), nj[:], A.mult, ["SU", vWn, njn], ["tp"], (256, GA))
         else:
             act(T.tp[:], T.SU[:, 0:4096].indirect(vW), F.Identity, ["SU", vWn], ["tp"], (256, GA))
@@ -598,6 +658,12 @@ def build(g, core, T, topo, rank, costs):
         if CFG["EQC"] == "X":
             act(T.rc[:], T.R[:, 0:4096].indirect(ul), F.Exp, ["R", "ul"], ["rc"], (256, GA), bias=-9 * LN256, scale=LN256)
             tt(T.eqc[:], ps[2][:, 0:256], T.rc[:], A.is_equal, ["pX", "rc"], ["eqc"], 256, [2])
+        elif CFG["EQC"] == "S":
+            act(T.rc[:], T.R[:, 0:4096].indirect(ul), F.Identity, ["R", "ul"], ["rc"], (256, GA))
+            P([(ps[2][:, 0:256], In, xb, True, False, 256), (ps[2][:, 0:256], Ib, T.rc[:], False, True, 256)],
+              ["Ib", "In", "rc", xn], ["pX"], [2])
+            act(T.Qb[:], ps[2][:, 0:256], F.Abs, ["pX"], ["ea"], 256, banks=[2])
+            act(T.eqc[:], T.Qb[:], F.Relu, ["ea"], ["eqc"], 256, bias=1.0, scale=-1.0)
         else:
             tt(T.eqc[:], T.R[:, 0:4096].indirect(ul), xb, A.is_equal, ["R", "ul", xn], ["eqc"], (256, GA))
         if EB:
@@ -610,7 +676,7 @@ def build(g, core, T, topo, rank, costs):
         else:
             P([(ps[4][:, 256 * h:256 * h + 256], T.eqc[:, 128 * h:128 * h + 128], WEC, False, h == 1, 256) for h in range(2)],
               ["eqc", "WEC0", "WEC1"], ["K1"], [4], True)
-            cp(T.Xi[:], ps[4][:], ["K1"], ["Xi0", "Xi1"], 512, [4])
+            ts(T.Xi[:], ps[4][:], 21845.0, A.add, ["K1"], ["Xi0", "Xi1"], 512, banks=[4])
         ts(T.Xa[:], T.Xi[:], 43690, A.bitwise_and, ["Xi0", "Xi1"], ["Xa"], 512)
         if CFG["OK"] == "S":
             act(T.ok[:], T.Xa[:].indirect(ID), F.Relu, ["Xa", "ID"], ["ok"], (512, GA), bias=1.0, scale=-1.0)
@@ -620,18 +686,18 @@ def build(g, core, T, topo, rank, costs):
            for h in range(2) for q in range(2)], ["ok", "Ib"], ["TT"], [5])
         act(T.wm[:, 0:256], ps[5][:, 0:256], F.Relu, ["TT"], ["wm0"], 256, bias=-1.0, banks=[5])
         act(T.mm[:], T.wm[:].indirect(sel), F.Identity, ["wm0", "wm1", "sel"], ["mm"], (256, GA))
-        if CFG["TV"] == "V":
-            P([(ps[6][:, 0:256], If, T.vnR[:], True, False, 1024), (ps[6][:, 0:256], Ifn, verK, False, True, 1024)],
-              ["If", "Ifn", "vnR"] + vk, ["uR"], [6])
-            tt(T.tv[:], ps[6][:, 0:256], T.mm[:], A.mult, ["uR", "mm"], ["tv"], 256, [6])
-            tt(T.VL[:].indirect(lM), verK, T.tv[:], A.add, vk + ["tv", "lGM"], ["VL"], (256, SC))
+        if u == NS and CFG["TZ"]:
+            act(T.tw[:], verK, F.Identity, vk + ["nk4"], ["tw"], 256, bias=nk4)
+            tt(T.sc1[:], T.vnR[:], T.tw[:], A.subtract, ["vnR", "tw"], pn("sc1"), 512)
+            tt(T.tv[:], T.sc1[:], T.mm[:], A.mult, pn("sc1") + ["mm"], ["tv"], 512)
+            tt(T.VL[:].indirect(lM), T.tw[:], T.tv[:], A.add, ["tw", "tv", "lGM"], ["VL"], (256, SC))
         else:
             P([(ps[2][:, 256:512], If, verK, True, False, 1024)], ["If", "eqc"] + vk, ["pXT"], [2], True)
             P([(ps[6][:, 0:256], If, T.vnR[:], True, False, 1024)], ["If", "vnR"], ["uR"], [6], True)
             P([(ps[2][:, 256:512], In8, T.mm[:], False, True, 256)], ["In8", "mm"], ["pXT"], [2], True)
             P([(ps[6][:, 0:256], I8k, T.mm[:], False, True, 256)], ["I8k", "mm"], ["uR"], [6], True)
             act(T.tv[:], ps[6][:, 0:256], F.Relu, ["uR"], ["tv"], 256, bias=-8192.0, banks=[6])
-            act(T.tw[:], ps[2][:, 256:512], F.Relu, ["pXT"], ["tw"], 256, banks=[2])
+            act(T.tw[:], ps[2][:, 256:512], F.Relu, ["pXT", "nk4"], ["tw"], 256, bias=nk4, banks=[2])
             tt(T.VL[:].indirect(lM), T.tw[:], T.tv[:], A.add, ["tw", "tv", "lGM"], ["VL"], (256, SC))
         P([(ps[1][:, 256:512], In, xb, True, False, 256), (ps[1][:, 256:512], I16, T.eqc[:], False, True, 256)],
           ["In", "I16", xn, "eqc"], ["pb"], [1])
@@ -658,11 +724,13 @@ def build(g, core, T, topo, rank, costs):
     for h, (bk, bn, b2, n2) in enumerate(((1, "wR", 0, "pY"), (2, "pX", 3, "K0"))):
         o = lambda k: ps[bk][:, k:128:16]
         P([(ps[bk][:, 0:128], ON32, T.QZ[0:32, 15:2048:16], True, False, 128)], ["ONE", "QZ"], [bn], [bk], True)
-        for q in range(4):
-            P([(o(k), T.SU[:, 2048 * h + 128 * k:2048 * h + 128 * k + 128], SEL8, False, False, 256)
-               for k in range(4 * q, 4 * q + 4)], ["SU", "SEL8"], [bn], [bk], True)
-        P([(o(k), T.QZ[:, 2048 * h + 128 * k:2048 * h + 128 * k + 128], NS8, False, k == 15, 64) for k in range(16)],
-          ["NS8"] + ["QZ%d" % t for t in range(NS)], [bn], [bk], True)
+        for q in range(5):
+            if q == 4 - 3 * h:
+                P([(o(k), T.QZ[:, 2048 * h + 128 * k:2048 * h + 128 * k + 128], NS8, False, k == 15 and h == 0, 64)
+                   for k in range(16)], ["NS8"] + ["QZ%d" % t for t in range(NS)], [bn], [bk], True)
+            if q < 4:
+                P([(o(k), T.SU[:, 2048 * h + 128 * k:2048 * h + 128 * k + 128], SEL8, False, k == 15 and h == 1, 256)
+                   for k in range(4 * q, 4 * q + 4)], ["SU", "SEL8"], [bn], [bk], True)
         hs = slice(128 * h, 128 * h + 128)
         act(T.y1[:, hs], ps[bk][:, 0:128], F.Identity, [bn, "back"], ["y1%d" % h], 128, bias=back, banks=[bk])
         P([(ps[b2][:, 0:128], T.y1[:, hs], If, True, True, 512)], ["y1%d" % h, "If"], [n2], [b2])
@@ -760,23 +828,26 @@ def plan(ops, other):
     p = [0.0] * n
     for i in range(n - 1, -1, -1):
         p[i] = c[i] + lat[i] + max([HOP + p[j] for j in succ[i]], default=0)
+    for i in range(n):
+        p[i] -= CFG["LATE"].get(ops[i]["w"][0][:2], 0) if ops[i]["nm"][-1] != "c" else 0
+    for i in range(n - 1, -1, -1):
+        p[i] = max([p[i]] + [p[j] + 1 for j in succ[i]])
     at = sweep(sorted(range(n), key=lambda i: (-p[i], i)), False)
     best = (max(at[i] + c[i] + lat[i] for i in range(n)), at)
     name = [o["nm"] for o in ops]
     deps = [list(o["d"]) for o in ops]
 
     def blocked(at):
-        ends = {}
-        for i in range(n):
-            for r in [eng_of[i]] + list(banks[i]):
-                ends.setdefault(r, []).append((at[i] + c[i], i))
-        for r in ends:
-            ends[r].sort()
+        last, before = {}, [None] * n
+        for i in sorted(range(n), key=lambda i: at[i]):
+            before[i] = [last[r] for r in (eng_of[i],) + banks[i] if r in last]
+            for r in (eng_of[i],) + banks[i]:
+                last[r] = i
         i, out = max(range(n), key=lambda i: at[i] + c[i] + lat[i]), []
         while True:
             ready, j = max([(at[j] + d, j) for j, d in pre[i]], default=(0.0, -1))
             if at[i] > ready + 1:
-                cand = [x for r in [eng_of[i]] + list(banks[i]) for x in ends[r] if at[i] - HOP - 1 <= x[0] <= at[i] + 1 and x[1] != i]
+                cand = [(at[x] + c[x], x) for x in before[i] if at[i] - HOP - 1 <= at[x] + c[x] <= at[i] + 1]
                 if cand:
                     j = max(cand)[1]
                     out.append((i, j, at[i] - ready))
@@ -784,7 +855,7 @@ def plan(ops, other):
                 return out
             i = j
 
-    state, pairs = [12345], None
+    state, pairs = [CFG["SEED"]], None
 
     def rnd():
         state[0] = (state[0] * 1103515245 + 12345) % 2147483648
@@ -811,14 +882,69 @@ def plan(ops, other):
         return max(end)
 
     def value(at, bound=1e18):
-        v = max(at[i] + c[i] + lat[i] for i in range(n)) + CFG["MEAN"] * sum(at) / n
+        v = own(at)
+        if v > bound:
+            return 1e18
         order = sorted(range(n), key=lambda i: (at[i], i))
         for cs, m in zip(other, CFG["COSTS"][1:]):
             v += m[9] * replay(order, cs, (1.0, m[8], m[7]))
         return v
 
-    cur = best = (value(best[1]), best[1])
-    for it in range(CFG["ROUNDS"]):
+    tails = [i for i in range(n) if not succ[i]]
+
+    def own(at):
+        return max(at[i] + c[i] + lat[i] for i in tails) + CFG["MEAN"] * sum(at) / n
+
+    kin = {}
+    for nm in sorted(set(name)):
+        kin.setdefault("".join(x for x in nm if not x.isdigit()), []).append(nm)
+
+    nxt_kin, seen = [None] * n, {}
+    for i in range(n - 1, -1, -1):
+        k = ("".join(x for x in name[i] if not x.isdigit()), ops[i]["step"])
+        if eng_of[i] in "VS" and k[0][1:-1] in ("old", "eq", "Zb", "Zc", "Zv"):
+            nxt_kin[i], seen[k] = seen.get(k), i
+    for i in range(n - 1, -1, -1):
+        p[i] = c[i] + lat[i] + max([HOP + p[j] for j in succ[i]] + ([p[nxt_kin[i]]] if nxt_kin[i] else []), default=0)
+
+    def ranked(off):
+        key = [off.get(name[i], 0.0) - p[i] for i in range(n)]
+        for i in range(n):
+            for d in deps[i]:
+                if key[d] + 0.005 > key[i]:
+                    key[i] = key[d] + 0.005
+        return key, sweep(sorted(range(n), key=lambda i: (key[i], i)), False)
+
+    off = {}
+    key, at = ranked(off)
+    cur = best = min((value(at), at), (value(best[1]), best[1])) if not CFG["RANKS"] else (value(at), at)
+    for it in range(CFG["RANKS"]):
+        if pairs is None:
+            pairs = blocked(cur[1])
+        new = dict(off)
+        for _ in range(1 + int(2 * rnd())):
+            if pairs and rnd() < 0.8:
+                i, j, w = pairs[int(rnd() * len(pairs))]
+                d = max(key[i] - key[j], 0.0) + 300 * rnd()
+                i, d = (i, -d) if rnd() < 0.5 else (j, d)
+            else:
+                i, d = int(rnd() * n), (rnd() - 0.5) * 4000 * rnd()
+            who = kin["".join(y for y in name[i] if not y.isdigit())] if rnd() < CFG["KIN"] else [name[i]]
+            if rnd() < CFG["ALL"] and name[i][-1] != "c":
+                who = [nm[:-1] + x for nm in who for x in "amz"]
+            for nm in who:
+                new[nm] = new.get(nm, 0.0) + d
+        key2, at = ranked(new)
+        end = value(at, own(cur[1]) + CFG["SLACK"])
+        if end < cur[0] + CFG["HEAT"] * rnd() * (1 - it / CFG["RANKS"]):
+            cur, pairs, off, key = (end, at), None, new, key2
+            if end < best[0]:
+                best = cur
+    cur, pairs, start = best, None, best
+    runs = [CFG["SHORT"]] * CFG["STARTS"] + [CFG["ROUNDS"]]
+    for run, it in [(r, k) for r in range(len(runs)) for k in range(runs[r])]:
+        if it == 0:
+            cur, pairs = (start if run + 1 < len(runs) else best), None
         sh = {}
         if pairs is None:
             pairs = blocked(cur[1])
@@ -834,6 +960,9 @@ def plan(ops, other):
             for nm in sorted(set(name)):
                 if nm[-1] == part and rnd() < CFG["FRAC"]:
                     sh[nm] = (rnd() - 0.5) * 2 * CFG["NOISE"] * big
+        if rnd() < CFG["KIN"]:
+            far = 1 + 6 * rnd() ** 2
+            sh = {x: v * far for nm, v in sh.items() for x in kin["".join(y for y in nm if not y.isdigit())]}
         if rnd() < CFG["ALL"]:
             sh = {nm[:-1] + x: v for nm, v in sh.items() for x in ("c" if nm[-1] == "c" else "amz")}
         key = [cur[1][i] + sh.get(name[i], 0.0) for i in range(n)]
@@ -848,14 +977,15 @@ def plan(ops, other):
                 if key[d] + 0.005 > key[i]:
                     key[i] = key[d] + 0.005
         at = sweep(sorted(range(n), key=lambda i: (key[i], i)), False)
-        end = value(at)
-        if end < cur[0] + CFG["SLACK"]:
+        bound = own(cur[1]) + CFG["SLACK"]
+        end = value(at, bound)
+        if end < cur[0] + CFG["SLACK"] and rnd() < CFG["BACK"]:
             bk_ = sweep(sorted(range(n), key=lambda i: (-(at[i] + c[i] + lat[i]), -i)), True)
             at2 = sweep(sorted(range(n), key=lambda i: (-(bk_[i] + c[i]), i)), False)
-            end2 = value(at2)
+            end2 = value(at2, bound)
             if end2 < end:
                 at, end = at2, end2
-        if end < cur[0] + CFG["HEAT"] * rnd() * (1 - it / CFG["ROUNDS"]):
+        if end < cur[0] + CFG["HEAT"] * rnd() * (1 - it / runs[run]):
             cur, pairs = (end, at), None
             if end < best[0]:
                 best = cur

import math
from concourse.bass import DstId, RemoteDMATransfer
from concourse.mybir import dt, AluOpType, AxisListType, ActivationFunctionType

A = AluOpType
F = ActivationFunctionType
NS = 6
BF, F32, I32, U16 = "bfloat16", "float32", "int32", "uint16"

CFG = dict(EQC="X", TV="S", XU="K", XW="S", XL="S", XM="S", XF="S", XQ="S", VD="C", ZO=1, IT=1, TP="V", JS=0,
           PARTS=((0, 4), (4, 16)), VT=((0, 4), (4, 16)), GS="G", GR="G", GRZ="S", BR="G", KT=2, TT="P", OK="V", CVT="G", DUP=1, ZC="S", EB=0, CUT=800, TZ=2, SEED=12345, KB="V", ZS=0, WHOLE=("Sv", "pC", "pG", "pA"), XB=(5, 6, 1, 5, 6, 1, 5, 6), UL=0, H1=0, H2=0, WS="S", XA="S", JM="S", S1="S",
           OLD=((0, 1), (1, 2), (2, 4), (4, 6), (6, 7), (7, 8)),
           COSTS=((0.97, 0.49, 1.5, 3.5, 4000, 500, 400, 180, 90, 1.0, 0), (0.85, 0.44, 1.15, 2.0, 4500, 700, 600, 200, 100, 0.9, 0),
                  (1.2, 0.6, 1.85, 5.0, 3500, 500, 250, 150, 80, 0.9, 0)),
           ROUNDS=6500, NOISE=600, FRAC=0.05, PAIR=0.85, SLACK=1500, HEAT=1000, ALL=0.5, MEAN=0.5, KIN=0.12, BACK=0.4, RANKS=0, LATE={},
           STARTS=5, SHORT=800)


def _buffers():
    s = {}
    for dtype, names in (
        (BF, dict(R=4368, EF=4096, ef0=512, old=4352, eq=4352, Zb=4096, Zc=4096, Zv=4096, QZ=4096, Q0=512, jm0=256, jm1=256,
                  nj0=256, nj1=256, Qb=256, xc=256, TTs=128, xw=128, xl=128, xg=384, xq=256, wsel=256, efu=256,
                  rc=256, eqc=256, ga=256, ok=512, wm=512, mm=256, xh=256, lx=256, fb=192, kb=96, xJ=1024,
                  cI=512, cW=640, L8=1152, DG=272, M2=384, CK=656, MK=784, ONE=256, NEG=128, REP=512, SR=256, SQ=1024, cb=64)),
        (F32, dict(VL=1280, SU=4352, v8f=256, G=256, sc1=256, sc2=256, VD=256, sf=512, wv=512, vnR=256, ws=512, u2=256,
                   tp=256, tv=256, tw=256, lv=256, y1=256, y2=256, io_f=768, cf=256, cI32=512, CS=256, MS=256, NUM=1024, Ec=512, sv=256)),
        (I32, dict(veri=1024, edgi=1024, v8i=256, si=128, Xi=512, Xa=512, io_i=8)),
        (U16, dict(VT=256, bR=256, cR=256, su=256, vR0=256, cu=96)),
    ):
        for n, c in names.items():
            s[n] = ("sbuf", [128, c], dtype)
    for t in range(NS):
        s["wx%d" % t] = ("sbuf", [128, 800], BF)
    for t in range(1, NS):
        s["s1_%d" % t] = ("sbuf", [128, 544], BF)
        s["s2_%d" % t] = ("sbuf", [128, 16], BF)
        if not CFG["ZS"]:
            s["s3_%d" % t] = ("sbuf", [128, 256], U16)
            s["l3_%d" % t] = ("sbuf", [128, 256], U16)
    for t in range(NS):
        s["l2_%d" % t] = ("sbuf", [128, 64], BF)
    for b in range(8):
        s["ps%d" % b] = ("psum", [128, 512], F32)
    return s


SCRATCH = _buffers()
ORDER = {}

NDMA = 40
SEMAPHORES = (["sV", "sS", "sP", "sG", "sent"] + ["d%d" % i for i in range(NDMA)]
              + ["a1_%d" % t for t in range(1, NS + 1)] + ["a2_%d" % t for t in range(1, NS + 1)])

OV = 22.0
LN256 = math.log(256.0)
FALL, TOP, THR, BIG = math.log(2.5), 58.0, 3.9, 2.0 ** 88


def build(g, core, T, topo, rank, costs):
    CV, CP, GA, SC, FAR, CALL, RATE = costs[:7]
    N = len(T.cores)
    nxt, prv = T.cores[(rank + 1) % N], T.cores[(rank - 1) % N]
    ops = []
    nd, phase = [0], ["c", {}, -1]
    ps = [T["ps%d" % b] for b in range(8)]

    def add(e, f, r, w, c, banks=(), **kw):
        nm = e + "".join(x for x in w[0] if not x.isdigit())
        phase[1][nm] = phase[1].get(nm, 0) + 1
        o = dict(e=e, f=f, r=list(r) + ([] if e == "P" else ["B%d" % b for b in banks]), w=list(w), c=c, b=tuple(banks),
                 i=len(ops), step=phase[2], nm="%s%d%s" % (nm, phase[1][nm], phase[0]))
        o.update(kw)
        ops.append(o)

    def cost(n, extra):
        return n[0] * n[1] * CV + 58 + extra if isinstance(n, tuple) else max(64, n) * CV + OV + extra

    def V(f, r, w, n, banks=()):
        add("V", f, r, w, cost(n, 0), banks)

    def S(f, r, w, n, banks=()):
        add("S", f, r, w, cost(n, 18), banks)

    def P(mms, r, w, banks, grp=False, given=False):
        if CFG["CUT"] and len(mms) > 1 and sum(m[5] for m in mms) > CFG["CUT"] and w[0] not in CFG["WHOLE"]:
            if not (grp or given):
                mms = [m[:4] + (n + 1 == len(mms) or mms[n + 1][3], m[5]) for n, m in enumerate(mms)]
            part, tot = [], 0
            for m in mms:
                if part and tot + m[5] > CFG["CUT"]:
                    P(part, r, w, banks, True)
                    part, tot = [], 0
                part, tot = part + [m], tot + m[5]
            return P(part, r, w, banks, True) if len(part) < len(mms) else None

        def f():
            for n, m in enumerate(mms):
                stop = m[4] if grp or given else (n + 1 == len(mms) or mms[n + 1][3])
                ins = g.tensor.matmul(m[0], m[1], m[2], bool(m[3]), bool(stop))
            return ins
        bn = ["B%d" % b for b in banks]
        add("P", f, list(r) + ([] if grp else bn), list(w) + (bn if grp else []), sum(m[5] * CP + costs[10] for m in mms) + 10, banks)

    def spread(e, out, win, lst, scale, r, w, n):
        if e == "S":
            act(out, win.indirect(lst), F.Identity, r, w, (n, GA), scale=scale)
        else:
            ts(out, win.indirect(lst), scale, A.mult, r, w, (n, GA))

    def ts(out, in0, s1, op0, r, w, n, s2=None, op1=None, banks=()):
        if op1 is None:
            V(lambda: g.vector.tensor_scalar(out, in0, s1, None, op0), r, w, n, banks)
        else:
            V(lambda: g.vector.tensor_scalar(out, in0, s1, s2, op0, op1), r, w, n, banks)

    def tt(out, a, b, op, r, w, n, banks=()):
        V(lambda: g.vector.tensor_tensor(out, a, b, op), r, w, n, banks)

    def cp(out, a, r, w, n, banks=()):
        V(lambda: g.vector.tensor_copy(out, a), r, w, n, banks)

    def fill(out, val, w, n):
        V(lambda: g.vector.memset(out, val), [], w, n)

    def scan(out, a, b, init, op0, op1, r, w, n, banks=()):
        V(lambda: g.vector.tensor_tensor_scan(out, a, b, init, op0, op1), r, w, n, banks)

    def act(out, a, func, r, w, n, bias=0.0, scale=1.0, banks=()):
        S(lambda: g.scalar.activation(out, a, func, bias=bias, scale=scale), r, w, n, banks)

    def iota(out, pat, w, n, cm=0, base=0, r=()):
        add("G", lambda: g.iota(out, pat, base, cm, allow_small_or_imprecise_dtypes=True), r, w, 130 + 2 * n * CV)

    def select(out, a, pat, op, other, base, cm, r, w, n):
        add("G", lambda: g.affine_select(out, a, pat, op, other, base, cm), r, w, 170 + 2 * n * CV)

    def copy(e, out, a, r, w, n):
        if e == "G":
            select(out, a, [[0, n]], A.is_ge, 0.0, 0, 0, r, w, n)
        elif e == "S":
            act(out, a, F.Identity, r, w, n)
        else:
            cp(out, a, r, w, n)

    def dma(q, out, in_, r, w, nbytes):
        sem = "d%d" % nd[0]
        nd[0] += 1
        eng = g.sync if q == "Y" else g.scalar
        add(q, lambda: eng.dma_start(out, in_), r, w, 60 + nbytes / RATE, lat=1800, sem=sem)

    def send(dst, out, in_, sem, r, w):
        rid, pid, _ = topo.addr(dst)
        m = topo.mask(core, dst)
        add("G", lambda: g.remote_dma(out, in_, T.sem[sem], T.sem.sent, pid, rid, m), r, w, CALL,
            send=len(topo.engines(core, dst)))

    def recv(src, sem, r, w):
        add("X", None, r, w, FAR, sem=sem, val=len(topo.engines(src, core)))

    dma("Y", T.v8i[0:8, :], T.v0[:], [], ["v8i"], 8192)
    dma("Y", T.wx0[:, 256:512], T.x0[:], [], ["xb0"], 65536)
    dma("Y", T.edgi[:], T.edge0[:], [], ["edgi"], 524288)
    dma("Y", T.veri[:], T.ver0[:], [], ["veri"], 524288)
    dma("Y", T.ef0[:], T.eff[:], [], ["ef0"], 131072)
    dma("Y", T.R[:, 0:4096], T.rec0[:], [], ["R"], 1048576)

    io, cf, cb, ii = T.io_f, T.cf, T.cb, T.io_i
    col = lambda j: cf[:, j:j + 1]
    partf, pf, gf, p7, wl, wh, offp, wt, bT_, bV_, x2s, nwt, nwl, nwh, p4, pf1 = [col(j) for j in range(16)]
    cm_, p32, k4, nk4 = col(128), cb[:, 2:3], col(129), col(130)
    add("G", lambda: g.iota(ii[:, 0:1], [[0, 1]], 0, 1), [], ["ii0"], 132)
    F128, CG, DI, HI, C16, H16 = (io[:, 0:128], io[:, 128:256], io[:, 256:528], io[:, 528:544], io[:, 544:672],
                                  io[:, 672:688])
    iota(F128, [[1, 128]], ["F128"], 128)
    iota(CG, [[1, 8], [0, 16]], ["CG"], 128)
    iota(DI, [[0, 17], [1, 16]], ["DI"], 272)
    iota(HI, [[1, 8], [16, 2]], ["HI"], 16, base=16)
    iota(C16, [[0, 2], [1, 8], [0, 8]], ["C16"], 128)
    H3 = io[:, 672:696]
    iota(H3, [[1, 8], [16, 3]], ["H3"], 24, base=16)
    ts(ii[:, 1:2], ii[:, 0:1], 15, A.bitwise_and, ["ii0"], ["ii1"], 1)
    ts(ii[:, 2:3], ii[:, 0:1], 4, A.arith_shift_right, ["ii0"], ["ii2"], 1)
    ts(ii[:, 3:4], ii[:, 0:1], 7, A.bitwise_and, ["ii0"], ["ii3"], 1)
    ts(ii[:, 4:5], ii[:, 0:1], 31, A.bitwise_and, ["ii0"], ["ii4"], 1)
    cp(cf[:, 0:4], ii[:, 0:4], ["ii0", "ii1", "ii2", "ii3"], ["pg"], 4)
    cp(p32, ii[:, 4:5], ["ii4"], ["p32"], 1)
    ts(cm_, p7, gf, A.is_equal, ["pg"], ["cm_"], 1)
    for ap, nm, src, sc_, bi in ((wt, "wt", pf, 2.0, 1.0), (nwt, "nwt", pf, -2.0, -1.0), (pf1, "pf1", pf, 1.0, 1.0),
                                 (k4, "k4", pf, 4096.0, 0.0), (nk4, "nk4", pf, -4096.0, 0.0),
                                 (bT_, "bT_", partf, -FALL, TOP + math.log(THR)), (bV_, "bV_", pf, -FALL, TOP + math.log(1.5))):
        act(ap, src, F.Identity, ["pg"], [nm], 1, bias=bi, scale=sc_)
    ts(offp, pf, 0.0, A.is_equal, ["pg"], ["offp0"], 1, -65536.0, A.mult)
    act(offp, offp, F.Identity, ["offp0"], ["offp"], 1, bias=32768.0)
    ts(x2s, pf, 8.0, A.is_ge, ["pg"], ["x2s"], 1, 8.0, A.mult)
    act(cb[:, 0:1], pf, F.Exp, ["pg"], ["p4b"], 1, scale=math.log(4.0))
    act(p4, cb[:, 0:1], F.Identity, ["p4b"], ["p4"], 1)
    ts(wl, pf, 8.0, A.is_lt, ["pg", "p4"], ["wl"], 1, p4, A.mult)
    ts(wh, x2s, p4, A.mult, ["x2s", "p4"], ["wh"], 1, 2.0 ** -19, A.mult)
    act(cf[:, 12:14], cf[:, 4:6], F.Identity, ["wl", "wh"], ["nw"], 2, scale=-1.0)
    Ib, In, I16, I8k = [T.cI[:, 128 * j:128 * j + 128] for j in range(4)]
    If, Ifn, BO, SB = [T.cI32[:, 128 * j:128 * j + 128] for j in range(4)]
    In8 = T.L8[:, 1024:1152]
    ts(If, F128, partf, A.is_equal, ["F128", "pg"], ["If"], 128)
    for ap, nm, val in ((Ib, "Ib", 1.0), (In, "In", -1.0), (I16, "I16", -16.0), (I8k, "I8k", 8192.0), (In8, "In8", -8192.0)):
        act(ap, If, F.Identity, ["If"], [nm], 128, scale=val)
    if CFG["TV"] == "V" or CFG["TP"] == "D":
        act(Ifn, If, F.Identity, ["If"], ["Ifn"], 128, scale=-1.0)
    ONE, NEG, MK, CK = T.ONE, T.NEG, T.MK, T.CK
    ON32, NE32 = ONE[0:32, 0:128], NEG[0:32, :]
    MJ, M4, H64, M2p = MK[0:32, 0:256], MK[0:32, 256:512], MK[0:32, 512:768], MK[0:32, 768:784]
    fill(ONE[:], 1.0, ["ONE"], 128)
    fill(NEG[:], -1.0, ["NEG"], 64)
    fill(MJ, 1.5 * 2 ** 22, ["MJ"], 128)
    fill(H64, 1 / 64, ["H64"], 128)
    iota(M4, [[0, 256]], ["M4"], 256, base=3 * 2 ** 19)
    iota(M2p, [[0, 16]], ["M2p"], 16, base=3 * 2 ** 18)
    KC, K17, EC, JC = CK[0:32, 0:256], CK[0:32, 256:272], CK[0:2, 272:528], CK[0:32, 528:656]
    iota(K17, [[0, 16]], ["K17"], 16, base=31 * 2 ** 16)
    if CFG["EB"]:
        iota(KC, [[0, 256]], ["KC"], 256)
        iota(EC, [[0, 256]], ["EC"], 256, base=85, cm=21760 - 85)
    iota(JC, [[0, 8], [-2, 16]], ["JC"], 128, base=-15)
    iota(T.Q0[:], [[1, 32], [0, 16]], ["Q00", "Q01"], 512)
    ts(T.REP[:], T.Q0[:], p32, A.is_equal, ["Q00", "Q01", "p32"], ["REP"], 256)
    iota(T.QZ[:, 0:512], [[0, 512]], ["QZa"], 512)
    dma("Y", T.QZ[:, 512:1024], T.QZ[:, 0:512], ["QZa", "ef0", "R"], ["QZb"], 131072)
    for k in range(1, 4):
        dma("Y", T.QZ[:, 1024 * k:1024 * k + 1024], T.QZ[:, 0:1024], ["QZa", "QZb"], ["QZc%d" % k], 262144)
    add("X", None, ["QZa", "QZb", "QZc1", "QZc2", "QZc3"], ["QZ"], 1, join=True)
    ts(BO, CG, gf, A.is_equal, ["CG", "pg"], ["BO"], 128)
    ts(SB, CG, partf, A.is_equal, ["CG", "pg"], ["SB"], 128)
    cW = T.cW
    WT, WEC, WK17, NS8, WTn = cW[:, 0:128], cW[:, 128:384], cW[:, 408:416], cW[:, 416:424], cW[:, 512:640]
    act(WT, BO, F.Identity, ["BO", "wt"], ["WT"], 128, scale=wt)
    act(WTn, BO, F.Identity, ["BO", "nwt"], ["WTn"], 128, scale=nwt)
    act(cW[:, 128:256], BO, F.Identity, ["BO", "wl"], ["WEC0"], 128, scale=wl)
    act(cW[:, 256:384], BO, F.Identity, ["BO", "wh"], ["WEC1"], 128, scale=wh)
    SEL8, thT, iWf, thrA = cf[:, 16:24], cf[:, 32:48], cf[:, 48:64], cf[:, 112:128]
    nHL = cf[:, 144:176]
    act(SEL8, T.cI32[:, 256:384:16], F.Identity, ["BO"], ["SEL8"], 8)
    for ap, nm, val, vn in ((cW[:, 384:392], "WKE0", -65536.0, []), (cW[:, 392:400], "WKE1", nwl, ["nw"]),
                            (cW[:, 400:408], "WKE2", nwh, ["nw"]), (WK17, "WK17", -2.0 ** 22, []), (NS8, "NS8", -1.0, [])):
        act(ap, SEL8, F.Identity, ["SEL8"] + vn, [nm], 8, scale=val)
    thr = col(32)
    act(thr, bT_, F.Exp, ["bT_"], ["thr"], 1)
    act(iWf, io[:, 0:16], F.Identity, ["F128", "pg"], ["iWf"], 16, bias=pf, scale=16.0)
    iWb, zer = cb[:, 16:32], cb[:, 32:48]
    act(iWb, iWf, F.Identity, ["iWf"], ["iWb"], 16, scale=32.0)
    act(nHL[:, 0:16] if False else cf[:, 144:160], iWf, F.Identity, ["iWf"], ["nH"], 16, scale=16.0)
    for j, base in enumerate((4112.0 - 8192, 1024.0 - 8192, 4096.0)):
        act(cf[:, 64 + 16 * j:80 + 16 * j], iWf, F.Identity, ["iWf"], ["DW%d" % j], 16, bias=base + (8192 if j < 2 else 0))
    KD = 65536.0 - 2.0 ** 20
    iota(thrA, [[0, 16]], ["thrA"], 16, base=4 * 65536 - 2 ** 20)
    DG = T.DG
    ts(DG[:], DI, pf, A.is_equal, ["DI", "pg"], ["DG"], 272)
    for k in range(2):
        dma("Y", T.L8[:, 512 * k:512 * k + 512], T.QZ[:, 0:512], ["QZa"], ["L8z%d" % k], 131072)
    for k in range(8):
        copy("G", T.L8[:, 144 * k:144 * k + 16], DG[:, 0:16], ["DG", "L8", "L8z0", "L8z1"], ["L8"], 16)
    WSV, M2t = T.M2[:, 0:192], T.M2[:, 192:384]
    act(T.M2[:, 192:320], C16, F.Exp, ["C16", "bV_"], ["M2t"], 128, bias=bV_, scale=-FALL * 16)
    act(T.M2[:, 320:384], ONE[:, 0:64], F.Identity, ["ONE"], ["M2u"], 64, scale=BIG)
    select(WSV, M2t, [[0, 24], [-16, 8]], A.is_ge, 0.0, 0, 1, ["M2t", "M2u"], ["WSV"], 192)
    select(WSV, WSV, [[0, 24], [16, 8]], A.is_ge, 0.0, 15, -1, ["WSV"], ["WSV"], 192)
    P([(ps[0][:, 256:512], In8, DG[:, 0:256], True, False, 256), (ps[0][:, 256:512], I8k, DG[:, 1:257], False, False, 256),
       (ps[0][:, 256:512], I8k, DG[:, 1:257], False, True, 256)], ["In8", "I8k", "DG"], ["pB"], [0])
    act(T.CS[:], ps[0][:, 256:512], F.Identity, ["pB"], ["CS"], 256, scale=4.0, banks=[0])
    iota(T.MS[:], [[0, 256]], ["MS"], 256)
    iota(T.MS[:, 0:256:16], [[0, 16]], ["MS"], 16, base=2 ** 23)
    if CFG["BR"] == "G":
        iota(T.NUM[:], [[1, 1024]], ["NUM"], 1024)
    cu = T.cu
    X2, X3, ID = cu[:, 16:24], cu[:, 48:64], cu[:, 64:96]
    ts(X2, io[:, 16:24], x2s, A.add, ["F128", "x2s", "cm_"], ["X2"], 8, cm_, A.mult)
    ts(X3, HI, x2s, A.add, ["HI", "x2s", "cm_"], ["X3"], 16, cm_, A.mult)
    if CFG["OK"] == "S":
        ts(ID, io[:, 0:32], 16.0, A.mult, ["F128", "pg"], ["ID"], 32, pf, A.add)
    X4 = cu[:, 24:48]
    ts(X4, H3, x2s, A.add, ["H3", "x2s", "cm_"], ["X4"], 24, cm_, A.mult)
    iota(T.fb[:], [[0, 192]], ["clT", "thrW", "hl"], 192)
    for t in range(NS):
        iota(T["l2_%d" % t][:, 0:16], [[0, 16]], ["lz%d" % t], 16)
    iota(zer, [[0, 16]], ["zer"], 16)
    for h in range(2):
        ts(T.SR[:, 128 * h:128 * h + 128], CG, float(8 * h), A.add, ["CG", "pg"], ["SR%d" % h], 128, pf, A.is_equal)
    if CFG["TT"] == "V":
        for k in range(2):
            dma("Y", T.SQ[:, 512 * k:512 * k + 512], T.QZ[:, 0:512], ["QZa"], ["SQz%d" % k], 131072)
        for a in range(4):
            dma("Y", T.SQ[32 * a:32 * a + 32, 256 * a:256 * a + 256], T.SR[32 * a:32 * a + 32, :],
                ["SR0", "SR1", "SQz0", "SQz1"], ["SQ%d" % a], 16384)
    iota(T.R[:, 4096:4112], [[0, 16]], ["R5"], 16, base=5)
    copy(CFG["CVT"], T.SU[:, 0:1024], T.edgi[:], ["edgi"], ["SU0"], 1024)
    for k in range(1, 4):
        dma("Y", T.SU[:, 1024 * k:1024 * k + 1024], T.SU[:, 0:1024], ["SU0"], ["SU%d" % k], 524288)
    add("X", None, ["SU0", "SU1", "SU2", "SU3"], ["SU"], 1, join=True)
    copy(CFG["CVT"], T.VL[:, 0:1024], T.veri[:], ["veri"], ["VL"], 1024)
    act(T.EF[:, 0:512], T.ef0[:], F.Identity, ["ef0"], ["EF0"], 512, bias=-1.5)
    dma("Y", T.EF[:, 512:1024], T.EF[:, 0:512], ["EF0"], ["EF1"], 131072)
    for k in range(1, 4):
        dma("Y", T.EF[:, 1024 * k:1024 * k + 1024], T.EF[:, 0:1024], ["EF0", "EF1"], ["EF%d" % (k + 1)], 262144)
    add("X", None, ["EF0", "EF1", "EF2", "EF3", "EF4"], ["EF"], 1, join=True)

    sf, si, su, fb = T.sf, T.si, T.su, T.fb
    f16 = lambda j: sf[:, 16 * j:16 * j + 16]
    bWf, vWf, hardT, nb, thrM, thrC, clW, lfF = [f16(j) for j in range(8)]
    lfGM, dn, tn = sf[:, 224:272], sf[:, 160:192], sf[:, 192:224]
    wWi, bWi, keyT, hiT, loT, vWi = [si[:, 16 * j:16 * j + 16] for j in range(6)]
    wl_, ul, sel, lG, lM, lF, vm0 = [su[:, 16 * j:16 * j + 16] for j in (2, 4, 5, 6, 7, 8, 10)]
    clT, thrW, hl = fb[:, 16:32], fb[:, 128:144], fb[:, 160:192]
    alias = {5: ["TT", "Sc", "pS", "pG"], 6: ["uR"], 1: ["wR", "pb"], 0: ["pY", "pB"]}

    cp(T.v8f[0:8, :], T.v8i[0:8, :], ["v8i"], ["v8f"], 256)
    P([(ps[1][:, 0:256], T.cI32[0:8, 384:512], T.v8f[0:8, :], True, True, 1024)], ["SB", "v8f"], ["wR"], [1])
    scan(T.sc2[:], ps[1][:, 0:256], T.CS[:], 32768.0, A.min, A.add, ["wR", "CS"], ["sc20", "sc21"], 256, [1])
    cp(T.vR0[:], ps[1][:, 0:256], ["wR"], ["vR"], 256, [1])
    ts(vWi, T.sc2[:, 15:256:16], offp, A.add, ["sc20", "sc21", "offp"], ["vWi"], 16)
    cp(su[:, 176:192], vWi, ["vWi"], ["vW0"], 16)
    cp(vWf, vWi, ["vWi"], ["vWf"], 16)
    ts(hiT, vWi, 1023, A.bitwise_and, ["vWi"], ["hiT"], 16)
    cp(vm0, hiT, ["hiT"], ["vm0"], 16)

    def zstart(c):
        q = c % 8
        return 128 * (c // 8) + (0 if q < 4 else 64 if q < 6 else 96)

    def split(kb, keyW, keyWn, nm):
        copy(CFG["KB"], kb[0], keyW, [keyWn], [nm + "h"], 16)
        tt(kb[1], keyW, kb[0], A.subtract, [keyWn, nm + "h"], [nm + "l"], 32)

    def zcalls(Z, nm, keyR, keyRn, buf, o, kn, more=()):
        for c in range(16):
            s = zstart(c)
            ts(Z[:, 256 * c + s:256 * c + 256], keyR[:, s:256], buf[:, o + c:o + c + 1], A.subtract,
               [keyRn] + kn + list(more) * (c < CFG["UL"]), ["%s%d" % (nm, c)], (256 - s) // 2, buf[:, o + 16 + c:o + 17 + c], A.is_equal)

    def zsum(Z, nm, wsel, wn, bk, o, on, cs, first, last, grp=False, only=None):
        mms = []
        if first:
            mms.append((ps[bk][:, o:o + 16], ONE[32:64, 0:128], cb[32:64, 32:48], True, False, 64))
        for c in cs:
            s = zstart(c)
            for h in range(c // 8, 2):
                if only is not None and only != (h > c // 8):
                    continue
                lo = max(s, 128 * h)
                at = 8 * c + (128 if h > c // 8 else 0)
                mms.append((ps[bk][lo - 128 * h:128, o + 8 * h:o + 8 * h + 8], Z[:, 256 * c + lo:256 * c + 128 * h + 128],
                            wsel[:, at:at + 8], False, last and c == 0 and h == 1, min(64, 128 * h + 128 - lo)))
        P(mms, ["%s%d" % (nm, c) for c in cs] + wn + ["ONE", "zer"], [on], [bk], grp, True)

    def firsts(buf, o, kn, out, on, row=T.vR0, rown="vR"):
        zcalls(T.Zv, "Zv", row, rown, buf, o, kn)
        zsum(T.Zv, "Zv", T.M2, ["WSV"], 7, 64, "Sv", range(15, -1, -1), True, True)
        ts(out, ps[7][:, 64:80], thr, A.is_ge, ["Sv", "thr"], [on], 16, banks=[7])

    def toW(xp, bk, o, n=16, st=16, at=0, first=False):
        return [(ps[bk][:, o:o + n], T.L8[:, 128 * k:128 * k + 128], xp[:, st * k + at:st * k + at + n], first and k == 0,
                 False, 64) for k in range(8)]

    def addkey(bk, o, buf, at, first=False):
        return [(ps[bk][:, o:o + 16], Ib, buf[:, at + 16 * k:at + 16 * k + 16], first and k == 0, False, 64) for k in range(2)]

    for t in range(NS):
        par, u = t % 2, t + 1
        phase[0] = "a" if t == 0 else "z" if t == NS - 1 else "m"
        phase[1], phase[2] = {}, t
        wx = T["wx%d" % t]
        xb, xn = wx[:, 256:512], "xb%d" % t
        jb, nj, jn, njn = T["jm%d" % par], T["nj%d" % par], "jm%d" % par, "nj%d" % par
        vW, vWn = su[:, 176 + 16 * par:192 + 16 * par], "vW%d" % par
        if t == 0:
            vkb, vo, vkn = T.kb, 64, ["Zvh", "Zvl"]
            split((T.kb[:, 64:80], T.kb[:, 80:96]), vWf, "vWf", "Zv")
            firsts(vkb, vo, vkn, T.l2_0[:, 48:64], "nf_0")
        else:
            vkb, vo, vkn = wx, 512, [xn]
            P(addkey(7, 32, wx, 512, True), ["Ib", xn], ["pV"], [7])
            cp(vW, ps[7][:, 32:48], ["pV"], [vWn], 16, [7])

        def jmask(out, on, xbuf, xo, xname, lo=0, hi=256, bk=0, at=0, pn="pY"):
            o, x, n = ps[bk][:, at:at + hi - lo], xbuf[:, xo + lo:xo + hi], hi - lo
            P([(o, JC, MK[0:32, 512:512 + n], True, False, n), (o, WT, x, False, False, n),
               (o, ON32, MK[0:32, 0:n], False, False, n), (o, NE32, MK[0:32, 0:n], False, False, n), (o, WTn, x, False, True, n)],
              ["JC", "H64", "ONE", "NEG", "WT", "WTn", "MJ", xname] + (["K1"] if lo and CFG["H1"] else []), [pn], [bk])
            if CFG["JM"] == "V" and n < 128:
                ts(out, o, pf1, A.add, [pn, "pf1"], [on], n, 0.0, A.max, banks=[bk])
            else:
                act(out, o, F.Relu, [pn, "pf1"], [on], n, bias=pf1, banks=[bk])

        def nextx(o, on, bk, ef, efn, out, outn):
            P([(o, In, xb, True, False, 256), (o, In, ef, False, False, 256), (o, ON32, M4, False, False, 256),
               (o, NE32, M4, False, False, 256), (o, Ib, xb, False, False, 256), (o, Ib, ef, False, True, 256)],
              ["Ib", "In", "ONE", "NEG", "M4", efn, xn], [on], [bk])
            act(out, o, F.Identity, [on], [outn], 256, bias=1.5, banks=[bk])

        js = CFG["JS"] and t
        jbuf, jo = (wx, 544) if js else (jb, 0)
        jm = jbuf[:, jo:jo + 256]
        parts = CFG["PARTS"]
        pn = lambda s: [s + str(k) for k in range(len(parts))]
        jns = [xn] if js else pn(jn)
        VLw, VLn = (T.VL[:, 0:1024], "VL") if t else (T.veri[:], "veri")
        for k, (a, b) in enumerate(parts):
            lo, hi, n = 16 * a, 16 * b, 16 * (b - a)
            head = k + 1 < len(parts)
            if not js:
                jmask(jb[:, lo:hi], jns[k], wx, 256, xn, lo, hi, *((3, 400, "pJ") if head else (0, lo, "pY")))
            src, lst, rn = ((T.SU[:, 0:4096], su[:, 176 + 16 * par + a:176 + 16 * par + b], ["SU", vWn]) if t
                            else (T.edgi[:], su[:, 160 + a:160 + b], ["edgi", "vm0"]))
            tt(T.G[:, lo:hi], src.indirect(lst), jbuf[:, jo + lo:jo + hi], A.mult, rn + [jns[k % len(jns)]], ["G%d" % k], (n, GA))
            bk, wn = (4, "K1") if head else (1, "wR")
            P([(ps[bk][:, lo:hi], BO, T.G[:, lo:hi], True, True, 4 * n)], ["BO", "G%d" % k], [wn], [bk])
            scan(T.sc1[:, lo:hi], ps[bk][:, lo:hi], T.CS[:, lo:hi], 32768.0, A.min, A.add, [wn, "CS"], ["sc1%d" % k], n, [bk])
            ts(si[:, a:b], T.sc1[:, lo + 15:hi:16], offp, A.add, ["sc1%d" % k, "offp"], ["wWi%d" % k], 16)
            ts(si[:, 16 + a:16 + b], si[:, a:b], 1023, A.bitwise_and, ["wWi%d" % k], ["bWi%d" % k], 16)
            cp(su[:, a:b], si[:, 16 + a:16 + b], ["bWi%d" % k], ["bla%d" % k], 16)
            if CFG["BR"] != "G":
                act(T.Qb[:, lo:hi], ps[bk][:, lo:hi], F.Identity, [wn], ["Qb%d" % k], n, bias=196096.5, banks=[bk])
        if CFG["TP"] == "V":
            act(nj[:], jm, F.Identity, jns, [njn], 256, bias=1.0, scale=-1.0)
        ts(wl_, wWi, 4096.0, A.min, pn("wWi"), ["wl_"], 16)
        verK, vk = T.VD[:, 0:256], ["VD"]
        for a, b in CFG["VT"]:
            cp(T.VT[:, 16 * a:16 * b], VLw.indirect(su[:, a:b]),
               [VLn] + ["bla%d" % k for k, (c, d) in enumerate(parts) if c < b and a < d],
               ["VT%d" % q for q in range(a // 2, b // 2)], (16 * (b - a), GA))
        ts(verK, T.VT[:], k4, A.add, ["k4"] + ["VT%d" % q for q in range(8)], vk, 256)
        P([(ps[2][:, 256 + 128 * h:384 + 128 * h], wx[:, 256 + 128 * h:384 + 128 * h], Ib, True, True, 128) for h in range(2)],
          ["Ib", xn], ["pXT"], [2])
        act(T.xc[:], ps[2][:, 256:512], F.Exp, ["pXT"], ["xc"], 256, bias=-9 * LN256, scale=LN256, banks=[2])
        P([(ps[2][:, 128 * h:128 * h + 128], T.xc[:, 128 * h:128 * h + 128], Ib, True, True, 128) for h in range(2)],
          ["Ib", "xc"], ["pX"], [2])
        if CFG["BR"] == "G":
            cp(T.bR[:], T.NUM[:].indirect(su[:, 0:16]), ["NUM"] + pn("bla"), ["bR"], (256, GA))
        else:
            P([(ps[1][:, 256:512], BO, T.G[:], True, True, 1024), (ps[1][:, 256:512], In, T.Qb[:], False, True, 256)],
              ["In", "BO"] + pn("G") + pn("Qb"), ["pb"], [1])
            ts(T.bR[:], ps[1][:, 256:512], 196608.0, A.add, ["pb"], ["bR"], 256, banks=[1])
        cp(T.kb[:, 0:16], bWi, pn("bWi"), ["Zbh"], 16)
        tt(T.kb[:, 16:32], bWi, T.kb[:, 0:16], A.subtract, pn("bWi") + ["Zbh"], ["Zbl"], 32)
        zcalls(T.Zb, "Zb", T.bR, "bR", T.kb, 0, ["Zbh", "Zbl"])
        if t and not CFG["ZS"]:
            firsts(vkb, vo, vkn, T["l2_%d" % t][:, 48:64], "nf_%d" % t, T["l3_%d" % t], "vR_%d" % t)
        l2 = T["l2_%d" % t]
        ngT, nmT = l2[:, 16:32], l2[:, 32:48]
        nextx(ps[0][:, 256:512], "pB", 0, T.EF[:, t:4096:16], "EF", T.xJ[:, 256:512], "xB")
        if CFG["JS"] and u < NS:
            jmask(T.xJ[:, 768:1024], "jB", T.xJ, 256, "xB")
        copy(CFG["GS"], T.ws[:, 0:256], T.SU[:, t:4096:16], ["SU"], ["ws0"], 256)
        iota(T.wv[:, 256:512], [[16, 256]], ["wv1"], 256, base=t)
        dma("Y", T.wm[:, 256:512], DG[:, t:t + 256], ["DG"] + ["R"] * (t == 0), ["wm1"], 65536)
        EB = CFG["EB"]
        kbk, ko, kn = ((3, 4), (0, 0), ("K0", "K1")) if EB else ((3, 3), (0, 128), ("K0", "K0"))
        o17 = 384 if EB else 256
        p17 = ps[kbk[1]][:, o17:o17 + 16]
        if EB:
            for h in range(2):
                P([(ps[3 + h][:, 0:128], ON32, CK[0:32, 0:128], True, False, 128),
                   (ps[3 + h][:, 128:384], ONE[0:2, 0:128], EC, False, False, 256)] + [(p17, ON32, K17, False, False, 64)] * h,
                  ["ONE", "KC", "K17", "EC"], [kn[h]], [3 + h], True)
        else:
            P([(p17, ON32, K17, True, False, 64)], ["ONE", "K17"], ["K0"], [3], True)
        act(T.old[:, 4096:4352], T.R[:, 0:4112].indirect(wl_), F.Exp, ["R", "R5", "wl_"], ["oldw"], (256, GA),
            bias=-9 * LN256, scale=LN256)
        tt(T.eq[:, 4096:4352], ps[2][:, 0:256], T.old[:, 4096:4352], A.is_equal, ["pX", "oldw"], ["eqw"], 256, [2])
        mms = []
        for h in range(2):
            o = ps[kbk[1]][:, o17 + 8 * h:o17 + 8 * h + 8]
            cs = slice(4096 + 128 * h, 4224 + 128 * h)
            mms += [(o, T.old[:, cs], WK17, False, False, 64), (o, T.eq[:, cs], WK17, False, False, 64),
                    (o, T.G[:, 128 * h:128 * h + 128], SEL8, False, False, 256)]
        key17 = (mms, ["oldw", "eqw", "WK17", "SEL8"] + pn("G"))
        for h in range(2):
            P([(ps[kbk[h]][:, ko[h]:ko[h] + 128], T.VD[:, 128 * h:128 * h + 128], If, False, False, 512)],
              vk + ["If"], [kn[h]], [kbk[h]], True)

        def keys(src, sn, h, lo, hi, stop=False):
            names = [sn + str(q) for q in range(4 * h + lo // 32, 4 * h + hi // 32)] + [sn + "7a"] * (h == 1 and hi == 128)
            m = 3 if EB and sn == "eq" else 1
            for k0 in (0, 8):
                P([(ps[kbk[h]][lo:hi, ko[h] + k:ko[h] + 128 * m:16], src[:, 2048 * h + 16 * lo + k:2048 * h + 16 * hi:16],
                    cW[:, 384:384 + 8 * m], False, stop and k == 15, min(64, hi - lo)) for k in range(k0, k0 + 8)],
                  names + ["WKE0", "WKE1", "WKE2"], [kn[h]], [kbk[h]], True)

        for q in range(8):
            cs = slice(512 * q, 512 * q + 512)
            h, a, bk = q // 4, q % 4, CFG["XB"][q]
            if q == 7:
                P([(ps[bk][:], T.xc[96:128, 128:256], T.REP[96:128, :], True, True, 512)], ["xc", "REP"], alias[bk], [bk])
                for k, nm in enumerate(("7a", "7")):
                    c2 = slice(3584 + 256 * k, 3840 + 256 * k)
                    act(T.old[:, c2], T.R[:, 0:4096].indirect(T.VT[:, 224 + 16 * k:240 + 16 * k]), F.Exp, ["R", "VT7"],
                        ["old" + nm], (256, GA), bias=-9 * LN256, scale=LN256)
                    tt(T.eq[:, c2], ps[bk][:, 256 * k:256 * k + 256], T.old[:, c2], A.is_equal, alias[bk] + ["old" + nm],
                       ["eq" + nm], 256, [bk])
            for lo, hi in CFG["OLD"]:
                if lo == q < 7:
                    act(T.old[:, 512 * lo:512 * hi], T.R[:, 0:4096].indirect(T.VT[:, 32 * lo:32 * hi]), F.Exp,
                        ["R"] + ["VT%d" % j for j in range(lo, hi)], ["old%d" % j for j in range(lo, hi)], (512 * (hi - lo), GA),
                        bias=-9 * LN256, scale=LN256)
            if q < 7:
                P([(ps[bk][:], T.xc[32 * a:32 * a + 32, 128 * h:128 * h + 128], T.REP[32 * a:32 * a + 32, :], True, True, 512)],
                  ["xc", "REP"], alias[bk], [bk])
                tt(T.eq[:, cs], ps[bk][:], T.old[:, cs], A.is_equal, alias[bk] + ["old%d" % q], ["eq%d" % q], 512, [bk])
            if q == 3:
                keys(T.old, "old", 0, 0, 128)
                keys(T.eq, "eq", 0, 0, 128, EB)
                P(key17[0], key17[1], [kn[1]], [kbk[1]], True)
            if CFG["KT"] and q == 6:
                if CFG["KT"] == 2:
                    keys(T.old, "old", 1, 0, 96)
                keys(T.eq, "eq", 1, 0, 96)
            if q == 7:
                keys(T.old, "old", 1, 96 if CFG["KT"] == 2 else 0, 128)
                if CFG["KT"]:
                    keys(T.eq, "eq", 1, 96, 128)
                    P([(p17, ONE[32:64, 0:128], cb[32:64, 32:48], False, True, 64)], ["ONE", "zer"], [kn[1]], [kbk[1]], True)
                else:
                    keys(T.eq, "eq", 1, 0, 128, True)
            if a == 3 and not EB:
                for lo in (0, 8):
                    P([(ps[4][:, 256 * h + k:256 * h + 256:16], T.eq[:, 2048 * h + k:2048 * h + 2048:16], cW[:, 392:408],
                        h == 0 and k == 0, False, 64) for k in range(lo, lo + 8)],
                      ["eq%d" % j for j in range(q - 3, q + 1)] + ["eq7a"] * h + ["WKE1", "WKE2"], ["K1"], [4], True)
        if EB:
            for h in range(2):
                scan(T.sc2[:, 128 * h:128 * h + 128], T.MS[:, 0:128], ps[3 + h][:, 0:128], 0.0, A.add, A.min, ["MS", kn[h]],
                     ["sc2%d" % h], 128, [3 + h])
        else:
            scan(T.sc2[:], T.MS[:], ps[3][:, 0:256], 0.0, A.add, A.min, ["MS", "K0"], ["sc20", "sc21"], 256, [3])
        tt(keyT, T.sc2[:, 15:256:16], p17, A.min, ["sc20", "sc21", kn[1]], ["keyT"], 16, [kbk[1]])
        ts(hiT, keyT, 4032, A.bitwise_and, ["keyT"], ["hiT"], 16)
        ts(loT, keyT, 63, A.bitwise_and, ["keyT"], ["loT"], 16)
        cp(hl, si[:, 48:80], ["hiT", "loT"], ["hl"], 32)
        if CFG["TT"] == "P":
            P([(ps[5][0:32, 0:128], hl, Ib, True, True, 128)], ["hl", "Ib"], ["TT"], [5])
            act(T.TTs[0:32, :], ps[5][0:32, 0:128], F.Identity, ["TT"], ["TTs"], 128, banks=[5])
            P([(ps[6][:, 128 * h:128 * h + 128], T.SR[0:32, 128 * h:128 * h + 128], T.TTs[0:32, :], True, True, 128)
               for h in range(2)], ["SR0", "SR1", "TTs"], ["uR"], [6])
        else:
            V(lambda: g.vector.transpose(T.TTs[:, 0:32], hl), ["hl"], ["TTs"], 16)
            P([(ps[6][:, 128 * h + 32 * a:128 * h + 32 * a + 32], T.SQ[:, 256 * a + 128 * h:256 * a + 128 * h + 128],
                T.TTs[:, 0:32], True, True, 64) for h in range(2) for a in range(4)],
              ["SQ0", "SQ1", "SQ2", "SQ3", "TTs"], ["uR"], [6])
        cp(T.cR[:], ps[6][:, 0:256], ["uR"], ["cR"], 256, [6])
        act(T.wv[:, 0:256], ps[6][:, 0:256], F.Identity, ["uR"], ["wv0"], 256, banks=[6])
        ts(thrW, keyT, KD, A.is_ge, ["keyT", "thr"], ["thrW"], 16, thr, A.mult)
        spread(CFG["XW"], T.xw[:], fb[:, 112:144], X2, 1 / THR, ["thrW", "X2"], ["xw"], 128)
        spread(CFG["XQ"], T.xq[:], fb[:, 144:192], X3, 1.0, ["hl", "X3"] + ["xw"] * CFG["H2"], ["xq"], 256)
        P(toW(T.xq, 7, 96, 32, 32, 0, True), ["xq", "L8"], ["pH"], [7])
        if CFG["ZC"] == "S":
            act(T.kb[:, 32:64], ps[7][:, 96:128], F.Identity, ["pH"], ["Zch"], 32, banks=[7])
        else:
            cp(T.kb[:, 32:64], ps[7][:, 96:128], ["pH"], ["Zch"], 32, [7])
        if CFG["XU"] == "K":
            P(addkey(7, 0, T.kb, 32, True), ["Ib", "Zch"], ["pU"], [7])
        else:
            P(toW(T.xq, 7, 0, 16, 32, 0, True) + toW(T.xq, 7, 0, 16, 32, 16), ["xq", "L8"], ["pU"], [7])
        cp(ul, ps[7][:, 0:16], ["pU"], ["ul"], 16, [7])
        tt(hardT, keyT, thrA, A.is_ge, ["keyT", "thrA"], ["hardT"], 32)
        tt(thrC, thrW, hardT, A.mult, ["thrW", "hardT"], ["thrC"], 32)
        P([(ps[0][:, k:128:8], T.L8[:, 128 * k:128 * k + 128], T.xw[:, 16 * k:16 * k + 16], True, True, 64)
           for k in range(8)], ["L8", "xw"], ["pY"], [0])
        act(T.wsel[:, 0:128], ps[0][:, 0:128], F.Identity, ["pY"], ["wsel"], 128, banks=[0])
        if CFG["WS"] == "V":
            ts(T.wsel[:, 128:192], T.wsel[:, 0:64], 0.0, A.is_gt, ["wsel"], ["wsel2"], 32, BIG, A.mult)
        else:
            act(T.wsel[:, 192:256], T.wsel[:, 0:64], F.Sign, ["wsel"], ["wsel1"], 64)
            act(T.wsel[:, 128:192], T.wsel[:, 192:256], F.Identity, ["wsel1"], ["wsel2"], 64, scale=BIG)
        wsn = ["wsel", "wsel2"]
        zsum(T.Zb, "Zb", T.wsel, wsn[:1], 5, 288, "Sc", range(15, -1, -1), True, False, True, False)
        zsum(T.Zb, "Zb", T.wsel, wsn, 5, 288, "Sc", range(7, -1, -1), False, False, True, True)
        zcalls(T.Zc, "Zc", T.cR, "cR", T.kb, 32, ["Zch"], ["ul"])
        for cs in (range(15, 5, -1), range(5, 1, -1), (1,), (0,)):
            zsum(T.Zc, "Zc", T.wsel, wsn, 5, 288, "Sc", cs, False, True, True)
        tt(clT, ps[5][:, 288:304], thrC, A.is_lt, ["Sc", "thrC"], ["clT"], 16, [5])
        tt(nmT, ps[5][:, 288:304], thrW, A.is_ge, ["Sc", "thrW"], ["nmT"], 16, [5])
        spread(CFG["XL"], T.xl[:], fb[:, 0:32], X2, 8192.0, ["clT", "X2"], ["xl"], 128)
        P([(ps[5][:, 320:336], Ib, iWb, True, False, 64)] + toW(T.xl, 5, 320), ["Ib", "iWb", "xl", "L8"], ["pS"], [5])
        ts(sel, ps[5][:, 320:336], 1 / 32, A.mult, ["pS"], ["sel"], 16, banks=[5])
        if CFG["XA"] == "V":
            tt(T.efu[:], T.EF[:].indirect(ul), xb, A.add, ["EF", "ul", xn], ["efu"], (256, GA))
            ts(T.rc[:], T.efu[:], 2.0, A.is_ge, ["efu"], ["rc"], 128, -4.0, A.mult)
            P([(ps[1][:, 0:256], Ib, T.efu[:], True, False, 256), (ps[1][:, 0:256], Ib, T.rc[:], False, True, 256)],
              ["Ib", "efu", "rc"], ["wR"], [1])
            act(T.xJ[:, 0:256], ps[1][:, 0:256], F.Identity, ["wR"], ["xA"], 256, bias=1.5, banks=[1])
        else:
            act(T.efu[:], T.EF[:].indirect(ul), F.Identity, ["EF", "ul"], ["efu"], (256, GA))
            nextx(ps[1][:, 0:256], "wR", 1, T.efu[:], "efu", T.xJ[:, 0:256], "xA")
        if u < NS:
            s1, s2 = T["s1_%d" % u], T["s2_%d" % u]
            spread(CFG["S1"], s1[:, 0:256], T.xJ[:, 0:512], sel, 1.0, ["xA", "xB", "sel"], ["s1_%d" % u], 256)
            iota(cf[:, 160:176], [[0, 16]], ["nL"], 16, base=t)
            tt(dn, nHL, T.kb[:, 32:64], A.subtract, ["nH", "nL", "Zch"], ["dn"], 64)
            ts(clW, ps[5][:, 320:336], 8192.0, A.is_ge, ["pS"], ["clW"], 16, banks=[5])
            for k in range(2):
                tt(sf[:, 192 + 16 * k:208 + 16 * k], clW, sf[:, 160 + 16 * k:176 + 16 * k], A.mult, ["clW", "dn"], ["tn%d" % k], 32)
            tt(s1[:, 256:288], tn, T.kb[:, 32:64], A.add, ["tn0", "tn1", "Zch"], ["s1v%d" % u], 64)
            if CFG["JS"]:
                jmask(T.xJ[:, 512:768], "jA", T.xJ, 0, "xA")
                act(s1[:, 288:544], T.xJ[:, 512:1024].indirect(sel), F.Identity, ["jA", "jB", "sel"], ["s1j%d" % u], (256, GA))
                send(nxt, T["wx%d" % u][:, 256:800], s1[:], "a1_%d" % u, ["s1_%d" % u, "s1j%d" % u, "s1v%d" % u], ["m1_%d" % u])
            else:
                send(nxt, T["wx%d" % u][:, 256:544], s1[:, 0:288], "a1_%d" % u, ["s1_%d" % u, "s1v%d" % u], ["m1_%d" % u])
            recv(prv, "a1_%d" % u, ["m1_%d" % u], ["xb%d" % u])
        act(T.vnR[:], T.wv[:].indirect(sel), F.Identity, ["wv0", "wv1", "sel"], ["vnR"], (256, GA))
        if u < NS:
            if CFG["ZS"]:
                cp(T.vR0[:], T.vnR[:], ["vnR"], ["vR"], 256)
                firsts(s1, 256, ["s1v%d" % u], s2[:], "s2_%d" % u)
                send(nxt, T["l2_%d" % u][:, 48:64], s2[:], "a2_%d" % u, ["s2_%d" % u], ["m2_%d" % u])
                recv(prv, "a2_%d" % u, ["m2_%d" % u], ["nf_%d" % u])
            else:
                cp(T["s3_%d" % u][:], T.vnR[:], ["vnR"], ["s2_%d" % u], 256)
                send(nxt, T["l3_%d" % u][:], T["s3_%d" % u][:], "a2_%d" % u, ["s2_%d" % u], ["m2_%d" % u])
                recv(prv, "a2_%d" % u, ["m2_%d" % u], ["vR_%d" % u])
        else:
            home, frm = T.cores[(rank - t) % N], T.cores[(rank + t) % N]
            act(T.xh[:], T.xJ[:, 0:512].indirect(sel), F.Identity, ["xA", "xB", "sel"], ["xh"], (256, GA))
            send(home, T.lx[:], T.xh[:], "a1_%d" % u, ["xh"], ["m1_%d" % u])
            recv(frm, "a1_%d" % u, ["m1_%d" % u], ["lx"])
            send(home, T.lv[:], T.vnR[:], "a2_%d" % u, ["vnR"], ["m2_%d" % u])
            recv(frm, "a2_%d" % u, ["m2_%d" % u], ["lv"])
            dma("Y", T.yx[:], T.lx[:], ["lx"], ["yx"], 65536)
            dma("Y", T.yv[:], T.lv[0:128:16, :], ["lv"], ["yv"], 8192)
        tt(ngT, nmT, clT, A.add, ["nmT", "clT"], ["ngT"], 32)
        spread(CFG["XM"], T.xg[:], l2[:], X4, 8192.0, ["nmT", "ngT", "nf_%d" % t, "lz%d" % t, "X4"], ["xg"], 384)
        P(addkey(5, 368, vkb, vo, True) + addkey(5, 352, T.kb, 0) + addkey(5, 336, T.kb, 32) + toW(T.xg, 5, 336, 48, 48),
          ["Ib", "Zbh", "Zbl", "Zch", "xg", "L8"] + vkn, ["pG"], [5])
        tt(lfGM, ps[5][:, 336:384], cf[:, 64:112], A.min, ["pG", "DW0", "DW1", "DW2"], ["lfGM"], 48, [5])
        cp(su[:, 96:144], lfGM, ["lfGM"], ["lGM"], 48)
        act(T.ws[:, 256:512], T.SU[:, 0:4096].indirect(ul), F.Identity, ["SU", "ul"], ["ws1"], (256, GA), bias=4096.0)
        act(T.SU[:, t:4096:16], T.ws[:].indirect(sel), F.Identity, ["ws0", "ws1", "sel"], ["SU"], (256, GA))
        if CFG["TP"] == "S":
            P([(ps[7][:, 256:512], If, T.vnR[:], True, False, 1024), (ps[7][:, 256:512], I8k, jm, False, True, 256)],
              ["If", "I8k", "vnR"] + jns, ["pC"], [7])
            act(T.u2[:], ps[7][:, 256:512], F.Relu, ["pC"], ["u2"], 256, bias=-8192.0, banks=[7])
            act(T.sv[:], T.SU[:, 0:4096].indirect(vW), F.Identity, ["SU", vWn], ["sv"], (256, GA), scale=0.25)
            P([(ps[0][:, 256:512], In8, jm, True, False, 256), (ps[0][:, 256:512], If, T.sv[:], False, True, 1024)],
              ["If", "In8", "sv"] + jns, ["pB"], [0])
            act(T.tp[:], ps[0][:, 256:512], F.Relu, ["pB"], ["tp"], 256, scale=4.0, banks=[0])
        elif CFG["TP"] == "V":
            if u == NS and CFG["TZ"] == 2:
                tt(T.u2[:], T.vnR[:], jm, A.mult, ["vnR"] + jns, ["u2"], 512)
            else:
                P([(ps[7][:, 256:512], If, T.vnR[:], True, False, 1024), (ps[7][:, 256:512], I8k, jm, False, True, 256)],
                  ["If", "I8k", "vnR"] + jns, ["pC"], [7])
                act(T.u2[:], ps[7][:, 256:512], F.Relu, ["pC"], ["u2"], 256, bias=-8192.0, banks=[7])
            tt(T.tp[:], T.SU[:, 0:4096].indirect(vW), nj[:], A.mult, ["SU", vWn, njn], ["tp"], (256, GA))
        else:
            act(T.tp[:], T.SU[:, 0:4096].indirect(vW), F.Identity, ["SU", vWn], ["tp"], (256, GA))
            P([(ps[7][:, 256:512], If, T.vnR[:], True, False, 1024), (ps[7][:, 256:512], Ifn, T.tp[:], False, True, 1024)],
              ["If", "Ifn", "vnR", "tp"], ["pC"], [7])
            tt(T.u2[:], ps[7][:, 256:512], jm, A.mult, ["pC"] + jns, ["u2"], 256, [7])
        tt(T.SU[:].indirect(lF), T.tp[:], T.u2[:], A.add, ["tp", "u2", "lGM"], ["SU"], (256, SC))
        if CFG["EQC"] == "X":
            act(T.rc[:], T.R[:, 0:4096].indirect(ul), F.Exp, ["R", "ul"], ["rc"], (256, GA), bias=-9 * LN256, scale=LN256)
            tt(T.eqc[:], ps[2][:, 0:256], T.rc[:], A.is_equal, ["pX", "rc"], ["eqc"], 256, [2])
        elif CFG["EQC"] == "S":
            act(T.rc[:], T.R[:, 0:4096].indirect(ul), F.Identity, ["R", "ul"], ["rc"], (256, GA))
            P([(ps[2][:, 0:256], In, xb, True, False, 256), (ps[2][:, 0:256], Ib, T.rc[:], False, True, 256)],
              ["Ib", "In", "rc", xn], ["pX"], [2])
            act(T.Qb[:], ps[2][:, 0:256], F.Abs, ["pX"], ["ea"], 256, banks=[2])
            act(T.eqc[:], T.Qb[:], F.Relu, ["ea"], ["eqc"], 256, bias=1.0, scale=-1.0)
        else:
            tt(T.eqc[:], T.R[:, 0:4096].indirect(ul), xb, A.is_equal, ["R", "ul", xn], ["eqc"], (256, GA))
        if EB:
            P([(ps[2][:, 256 * h:256 * h + 256], T.eqc[:, 128 * h:128 * h + 128], WEC, True, True, 256) for h in range(2)],
              ["eqc", "WEC0", "WEC1"], ["pX", "pXT"], [2])
            act(T.Ec[:], ps[2][:], F.Identity, ["pX", "pXT"], ["Ec"], 512, banks=[2])
            for h in range(2):
                tt(T.Xi[:, 256 * h:256 * h + 256], ps[3 + h][:, 128:384], T.Ec[:, 256 * h:256 * h + 256], A.add,
                   [kn[h], "Ec"], ["Xi%d" % h], 256, [3 + h])
        else:
            P([(ps[4][:, 256 * h:256 * h + 256], T.eqc[:, 128 * h:128 * h + 128], WEC, False, h == 1, 256) for h in range(2)],
              ["eqc", "WEC0", "WEC1"], ["K1"], [4], True)
            ts(T.Xi[:], ps[4][:], 21845.0, A.add, ["K1"], ["Xi0", "Xi1"], 512, banks=[4])
        ts(T.Xa[:], T.Xi[:], 43690, A.bitwise_and, ["Xi0", "Xi1"], ["Xa"], 512)
        if CFG["OK"] == "S":
            act(T.ok[:], T.Xa[:].indirect(ID), F.Relu, ["Xa", "ID"], ["ok"], (512, GA), bias=1.0, scale=-1.0)
        else:
            ts(T.ok[:], T.Xa[:], 0.0, A.is_equal, ["Xa"], ["ok"], 512)
        P([(ps[5][:, 128 * h:128 + 128 * h], T.ok[:, 256 * h + 128 * q:256 * h + 128 * q + 128], Ib, q == 0, q == 1, 128)
           for h in range(2) for q in range(2)], ["ok", "Ib"], ["TT"], [5])
        act(T.wm[:, 0:256], ps[5][:, 0:256], F.Relu, ["TT"], ["wm0"], 256, bias=-1.0, banks=[5])
        act(T.mm[:], T.wm[:].indirect(sel), F.Identity, ["wm0", "wm1", "sel"], ["mm"], (256, GA))
        if u == NS and CFG["TZ"]:
            act(T.tw[:], verK, F.Identity, vk + ["nk4"], ["tw"], 256, bias=nk4)
            tt(T.sc1[:], T.vnR[:], T.tw[:], A.subtract, ["vnR", "tw"], pn("sc1"), 512)
            tt(T.tv[:], T.sc1[:], T.mm[:], A.mult, pn("sc1") + ["mm"], ["tv"], 512)
            tt(T.VL[:].indirect(lM), T.tw[:], T.tv[:], A.add, ["tw", "tv", "lGM"], ["VL"], (256, SC))
        else:
            P([(ps[2][:, 256:512], If, verK, True, False, 1024)], ["If", "eqc"] + vk, ["pXT"], [2], True)
            P([(ps[6][:, 0:256], If, T.vnR[:], True, False, 1024)], ["If", "vnR"], ["uR"], [6], True)
            P([(ps[2][:, 256:512], In8, T.mm[:], False, True, 256)], ["In8", "mm"], ["pXT"], [2], True)
            P([(ps[6][:, 0:256], I8k, T.mm[:], False, True, 256)], ["I8k", "mm"], ["uR"], [6], True)
            act(T.tv[:], ps[6][:, 0:256], F.Relu, ["uR"], ["tv"], 256, bias=-8192.0, banks=[6])
            act(T.tw[:], ps[2][:, 256:512], F.Relu, ["pXT", "nk4"], ["tw"], 256, bias=nk4, banks=[2])
            tt(T.VL[:].indirect(lM), T.tw[:], T.tv[:], A.add, ["tw", "tv", "lGM"], ["VL"], (256, SC))
        P([(ps[1][:, 256:512], In, xb, True, False, 256), (ps[1][:, 256:512], I16, T.eqc[:], False, True, 256)],
          ["In", "I16", xn, "eqc"], ["pb"], [1])
        act(T.ga[:], ps[1][:, 256:512], F.Relu, ["pb"], ["ga"], 256, bias=9.0, banks=[1])
        tt(T.R[:].indirect(lG), xb, T.ga[:], A.add, ["ga", xn, "lGM", "R5"], ["R"], (256, SC))
        copy(CFG["GR"] if u < NS else CFG["GRZ"], wx[:, 0:256], T.R[:, t:4096:16], ["R"], ["wx0_%d" % t], 256)
        act(T.R[:, t:4096:16], wx[:, 0:512].indirect(sel), F.Identity, ["wx0_%d" % t, xn, "sel"], ["R"], (256, GA))
        if u < NS:
            cnt = lambda w: [(ps[7][:, 16 + 8 * k:24 + 8 * k], w, fb[:, 16 + 8 * h:24 + 8 * h], False, False, 64)
                             for k in range(2) for h in range(2)]
            row = lambda w, m, st: [(ps[7][:, 16:32], w, m, st, False, 64)]
            P(row(NE32, MK[0:32, 512:528], True) + cnt(ONE[:, 0:128]) + row(ON32, M2p, False) + row(NE32, M2p, False)
              + cnt(NEG[:]), ["ONE", "NEG", "H64", "M2p", "clT"], ["pA"], [7])
            act(thrA, ps[7][:, 16:32], F.Identity, ["pA"], ["thrA"], 16, bias=4.0 * 65536 - 2.0 ** 20, scale=-65536.0, banks=[7])

    dma("Y", T.yr[:], T.R[:, 0:4096], ["R"], ["yr"], 1048576)
    dma("Y", T.yl[:], T.VL[:, 0:1024], ["VL"], ["yl"], 524288)
    for t in range(NS):
        ts(T.QZ[:, t:4096:16], T.SU[:, t:4096:16], 196096.5, A.add, ["SU", "QZ"], ["QZ%d" % t], 256, 200704.0, A.max)
    back = col(33)
    ts(back, pf, float(NS), A.is_lt, ["pg"], ["back"], 1, 16 * 200704.0, A.mult)
    if True:
        pass
    for h, (bk, bn, b2, n2) in enumerate(((1, "wR", 0, "pY"), (2, "pX", 3, "K0"))):
        o = lambda k: ps[bk][:, k:128:16]
        P([(ps[bk][:, 0:128], ON32, T.QZ[0:32, 15:2048:16], True, False, 128)], ["ONE", "QZ"], [bn], [bk], True)
        for q in range(5):
            if q == 4 - 3 * h:
                P([(o(k), T.QZ[:, 2048 * h + 128 * k:2048 * h + 128 * k + 128], NS8, False, k == 15 and h == 0, 64)
                   for k in range(16)], ["NS8"] + ["QZ%d" % t for t in range(NS)], [bn], [bk], True)
            if q < 4:
                P([(o(k), T.SU[:, 2048 * h + 128 * k:2048 * h + 128 * k + 128], SEL8, False, k == 15 and h == 1, 256)
                   for k in range(4 * q, 4 * q + 4)], ["SU", "SEL8"], [bn], [bk], True)
        hs = slice(128 * h, 128 * h + 128)
        act(T.y1[:, hs], ps[bk][:, 0:128], F.Identity, [bn, "back"], ["y1%d" % h], 128, bias=back, banks=[bk])
        P([(ps[b2][:, 0:128], T.y1[:, hs], If, True, True, 512)], ["y1%d" % h, "If"], [n2], [b2])
        act(T.y2[:, hs], ps[b2][:, 0:128], F.Identity, [n2], ["y2%d" % h], 128, banks=[b2])
        dma("Y", T.ys[:, 2048 * h:2048 * h + 2048], T.y2[:, hs], ["y2%d" % h], ["ys%d" % h], 65536)
    return ops


HOP, SELF = CFG["COSTS"][0][7:9]


def plan(ops, other):
    lastw, readers = {}, {}
    for o in ops:
        d = set()
        for r in o["r"]:
            if r in lastw:
                d.add(lastw[r])
        for w in o["w"]:
            if w in lastw:
                d.add(lastw[w])
            d.update(readers.get(w, ()))
        d.discard(o["i"])
        o["d"] = d
        for r in o["r"]:
            readers.setdefault(r, []).append(o["i"])
        for w in o["w"]:
            lastw[w] = o["i"]
            readers[w] = []
    n = len(ops)
    succ = [[] for _ in ops]
    for o in ops:
        for d in o["d"]:
            succ[d].append(o["i"])

    def hop(a, b):
        return 1.0 if a["e"] == b["e"] == "P" else SELF if a["e"] == b["e"] else HOP

    c = [o["c"] for o in ops]
    lat = [o.get("lat", 0) for o in ops]
    eng_of = [o["e"] for o in ops]
    banks = [o["b"] for o in ops]
    pre = [[(j, c[j] + lat[j] + hop(ops[j], o)) for j in o["d"]] for o in ops]
    post = [[(j, c[j] + hop(o, ops[j]) + lat[o["i"]]) for j in succ[o["i"]]] for o in ops]
    first = [i for i in range(n) if eng_of[i] == "Y" and not ops[i]["d"]]

    def fit(lst, s, cost, own):
        lo = len(lst)
        if own is None:
            while lo and lst[lo - 1][1] > s:
                lo -= 1
            pad = 0.0
        else:
            while lo and lst[lo - 1][0] > s - 1400:
                lo -= 1
            pad = HOP
        for k in range(lo, len(lst)):
            a, b, e = lst[k]
            if a - pad >= s + cost:
                break
            if e != own and b + pad > s:
                s = b + pad
        return s

    def put(lst, it):
        k = len(lst)
        while k and lst[k - 1][0] > it[0]:
            k -= 1
        lst.insert(k, it)

    def sweep(seq, back):
        at, eng, bk = [0.0] * n, {e: [] for e in "VSPGY"}, [[] for _ in range(8)]
        if not back:
            seq = first + [i for i in seq if i not in first]
        for i in seq:
            s = lat[i] if back else 0.0
            for j, d in (post[i] if back else pre[i]):
                if at[j] + d > s:
                    s = at[j] + d
            e = eng_of[i]
            if e != "X":
                while True:
                    s2 = fit(eng[e], s, c[i], None)
                    for b in banks[i]:
                        s2 = fit(bk[b], s2, c[i], e)
                    if s2 == s:
                        break
                    s = s2
                put(eng[e], (s, s + c[i], e))
                for b in banks[i]:
                    put(bk[b], (s, s + c[i], e))
            at[i] = s
        return at

    p = [0.0] * n
    for i in range(n - 1, -1, -1):
        p[i] = c[i] + lat[i] + max([HOP + p[j] for j in succ[i]], default=0)
    for i in range(n):
        p[i] -= CFG["LATE"].get(ops[i]["w"][0][:2], 0) if ops[i]["nm"][-1] != "c" else 0
    for i in range(n - 1, -1, -1):
        p[i] = max([p[i]] + [p[j] + 1 for j in succ[i]])
    at = sweep(sorted(range(n), key=lambda i: (-p[i], i)), False)
    best = (max(at[i] + c[i] + lat[i] for i in range(n)), at)
    name = [o["nm"] for o in ops]
    deps = [list(o["d"]) for o in ops]

    def blocked(at):
        last, before = {}, [None] * n
        for i in sorted(range(n), key=lambda i: at[i]):
            before[i] = [last[r] for r in (eng_of[i],) + banks[i] if r in last]
            for r in (eng_of[i],) + banks[i]:
                last[r] = i
        i, out = max(range(n), key=lambda i: at[i] + c[i] + lat[i]), []
        while True:
            ready, j = max([(at[j] + d, j) for j, d in pre[i]], default=(0.0, -1))
            if at[i] > ready + 1:
                cand = [(at[x] + c[x], x) for x in before[i] if at[i] - HOP - 1 <= at[x] + c[x] <= at[i] + 1]
                if cand:
                    j = max(cand)[1]
                    out.append((i, j, at[i] - ready))
            if j < 0:
                return out
            i = j

    state, pairs = [CFG["SEED"]], None

    def rnd():
        state[0] = (state[0] * 1103515245 + 12345) % 2147483648
        return (state[0] >> 8) % 100000 / 100000.0

    kind = [[(j, 0 if eng_of[i] == eng_of[j] == "P" else 1 if eng_of[i] == eng_of[j] else 2) for j in deps[i]] for i in range(n)]

    def replay(order, cs, hops):
        free, bank, end = {}, [{} for _ in range(8)], [0.0] * n
        for i in order:
            e = eng_of[i]
            s = 0.0 if e == "X" else free.get(e, 0.0)
            for j, k in kind[i]:
                if end[j] + hops[k] > s:
                    s = end[j] + hops[k]
            for b in banks[i]:
                for e2, x in bank[b].items():
                    if e2 != e and x + hops[2] > s:
                        s = x + hops[2]
            free[e] = s + cs[i]
            end[i] = s + cs[i] + lat[i]
            for b in banks[i]:
                bank[b][e] = end[i]
        return max(end)

    def value(at, bound=1e18):
        v = own(at)
        if v > bound:
            return 1e18
        order = sorted(range(n), key=lambda i: (at[i], i))
        for cs, m in zip(other, CFG["COSTS"][1:]):
            v += m[9] * replay(order, cs, (1.0, m[8], m[7]))
        return v

    tails = [i for i in range(n) if not succ[i]]

    def own(at):
        return max(at[i] + c[i] + lat[i] for i in tails) + CFG["MEAN"] * sum(at) / n

    kin = {}
    for nm in sorted(set(name)):
        kin.setdefault("".join(x for x in nm if not x.isdigit()), []).append(nm)

    nxt_kin, seen = [None] * n, {}
    for i in range(n - 1, -1, -1):
        k = ("".join(x for x in name[i] if not x.isdigit()), ops[i]["step"])
        if eng_of[i] in "VS" and k[0][1:-1] in ("old", "eq", "Zb", "Zc", "Zv"):
            nxt_kin[i], seen[k] = seen.get(k), i
    for i in range(n - 1, -1, -1):
        p[i] = c[i] + lat[i] + max([HOP + p[j] for j in succ[i]] + ([p[nxt_kin[i]]] if nxt_kin[i] else []), default=0)

    def ranked(off):
        key = [off.get(name[i], 0.0) - p[i] for i in range(n)]
        for i in range(n):
            for d in deps[i]:
                if key[d] + 0.005 > key[i]:
                    key[i] = key[d] + 0.005
        return key, sweep(sorted(range(n), key=lambda i: (key[i], i)), False)

    off = {}
    key, at = ranked(off)
    cur = best = min((value(at), at), (value(best[1]), best[1])) if not CFG["RANKS"] else (value(at), at)
    for it in range(CFG["RANKS"]):
        if pairs is None:
            pairs = blocked(cur[1])
        new = dict(off)
        for _ in range(1 + int(2 * rnd())):
            if pairs and rnd() < 0.8:
                i, j, w = pairs[int(rnd() * len(pairs))]
                d = max(key[i] - key[j], 0.0) + 300 * rnd()
                i, d = (i, -d) if rnd() < 0.5 else (j, d)
            else:
                i, d = int(rnd() * n), (rnd() - 0.5) * 4000 * rnd()
            who = kin["".join(y for y in name[i] if not y.isdigit())] if rnd() < CFG["KIN"] else [name[i]]
            if rnd() < CFG["ALL"] and name[i][-1] != "c":
                who = [nm[:-1] + x for nm in who for x in "amz"]
            for nm in who:
                new[nm] = new.get(nm, 0.0) + d
        key2, at = ranked(new)
        end = value(at, own(cur[1]) + CFG["SLACK"])
        if end < cur[0] + CFG["HEAT"] * rnd() * (1 - it / CFG["RANKS"]):
            cur, pairs, off, key = (end, at), None, new, key2
            if end < best[0]:
                best = cur
    cur, pairs, start = best, None, best
    runs = [CFG["SHORT"]] * CFG["STARTS"] + [CFG["ROUNDS"]]
    for run, it in [(r, k) for r in range(len(runs)) for k in range(runs[r])]:
        if it == 0:
            cur, pairs = (start if run + 1 < len(runs) else best), None
        sh = {}
        if pairs is None:
            pairs = blocked(cur[1])
        if pairs and rnd() < CFG["PAIR"]:
            for _ in range(1 + int(2 * rnd())):
                i, j, w = pairs[int(rnd() * len(pairs))]
                if rnd() < 0.5:
                    sh[name[i]] = -(w + 20) * (0.3 + rnd())
                else:
                    sh[name[j]] = (c[i] + c[j] + 100) * (1 + 3 * rnd())
        else:
            part, big = "mmazc"[int(5 * rnd())], (1, 3)[int(2 * rnd())]
            for nm in sorted(set(name)):
                if nm[-1] == part and rnd() < CFG["FRAC"]:
                    sh[nm] = (rnd() - 0.5) * 2 * CFG["NOISE"] * big
        if rnd() < CFG["KIN"]:
            far = 1 + 6 * rnd() ** 2
            sh = {x: v * far for nm, v in sh.items() for x in kin["".join(y for y in nm if not y.isdigit())]}
        if rnd() < CFG["ALL"]:
            sh = {nm[:-1] + x: v for nm, v in sh.items() for x in ("c" if nm[-1] == "c" else "amz")}
        key = [cur[1][i] + sh.get(name[i], 0.0) for i in range(n)]
        up = [sh.get(name[i], 0.0) < 0 for i in range(n)]
        for i in range(n - 1, -1, -1):
            if up[i]:
                for d in deps[i]:
                    if key[d] > key[i] - 0.01:
                        key[d], up[d] = key[i] - 0.01, True
        for i in range(n):
            for d in deps[i]:
                if key[d] + 0.005 > key[i]:
                    key[i] = key[d] + 0.005
        at = sweep(sorted(range(n), key=lambda i: (key[i], i)), False)
        bound = own(cur[1]) + CFG["SLACK"]
        end = value(at, bound)
        if end < cur[0] + CFG["SLACK"] and rnd() < CFG["BACK"]:
            bk_ = sweep(sorted(range(n), key=lambda i: (-(at[i] + c[i] + lat[i]), -i)), True)
            at2 = sweep(sorted(range(n), key=lambda i: (-(bk_[i] + c[i]), i)), False)
            end2 = value(at2, bound)
            if end2 < end:
                at, end = at2, end2
        if end < cur[0] + CFG["HEAT"] * rnd() * (1 - it / runs[run]):
            cur, pairs = (end, at), None
            if end < best[0]:
                best = cur
    ORDER["end"], ORDER["at"] = max(best[1][i] + c[i] + lat[i] for i in range(n)), best[1]
    return sorted(ops, key=lambda o: (best[1][o["i"]], o["i"]))


def emit(g, T, ops, order):
    q = {"V": g.vector, "S": g.scalar, "P": g.tensor, "G": g, "Y": g.sync}
    pos, bank, seen, need = {}, {}, {}, set()
    for n, o in enumerate(order):
        pos[o["i"]] = n
    for o in order:
        if o["e"] == "X":
            continue
        d = set()
        for i in o["d"]:
            d.update(ops[i]["d"] if "join" in ops[i] else (i,))
        for b in o["b"]:
            for e, i in bank.get(b, {}).items():
                if e != o["e"]:
                    d.add(i)
            bank.setdefault(b, {})[o["e"]] = o["i"]
        best, ws = {}, []
        for i in d:
            p = ops[i]
            if "sem" in p:
                if (o["e"], p["sem"]) not in seen:
                    seen[(o["e"], p["sem"])] = 1
                    ws.append(i)
            elif "send" in p or (p["e"] == o["e"] == "P"):
                continue
            elif pos[i] > best.get(p["e"], -1):
                best[p["e"]] = pos[i]
        for e, n in best.items():
            if n > seen.get((o["e"], e), -1):
                seen[(o["e"], e)] = n
                ws.append(order[n]["i"])
                need.add(order[n]["i"])
        o["ws"] = ws
    cnt, sent = {}, 0
    for o in order:
        e = o["e"]
        if e == "X":
            continue
        for i in o["ws"]:
            p = ops[i]
            if "sem" in p:
                q[e].wait_ge(T.sem[p["sem"]], p.get("val", 16))
            else:
                q[e].wait_ge(T.sem["s" + p["e"]], p["n"])
        ins = o["f"]()
        if "sem" in o:
            ins.then_inc(T.sem[o["sem"]], 16)
        elif "send" in o:
            sent += o["send"]
        elif o["i"] in need:
            cnt[e] = cnt.get(e, 0) + 1
            o["n"] = cnt[e]
            ins.then_inc(T.sem["s" + e], 1)
    g.wait_ge(T.sem.sent, sent)
    for o in ops:
        if "sem" in o and o["e"] != "X" and o["w"][0].startswith("y"):
            g.wait_ge(T.sem[o["sem"]], 16)


def rank_program(g, core, T, topo):
    rank = T.rank_of(core)
    if rank is None:
        return
    ops = build(g, core, T, topo, rank, CFG["COSTS"][0])
    if "o" not in ORDER:
        other = [[o["c"] for o in build(g, core, T, topo, rank, m)] for m in CFG["COSTS"][1:]]
        ORDER["o"] = [(o["i"], o["d"]) for o in plan(ops, other)]
    for i, d in ORDER["o"]:
        ops[i]["d"] = d
    emit(g, T, ops, [ops[i] for i, d in ORDER["o"]])
